import numpy as np
import ml_dtypes


def mxq(x, axis, fmt="e4m3"):
    dtype, down = {"e4m3": (ml_dtypes.float8_e4m3fn, 7), "e5m2": (ml_dtypes.float8_e5m2, 14)}[fmt]
    v = np.moveaxis(np.asarray(x, np.float32).astype(ml_dtypes.bfloat16).astype(np.float64), axis, -1)
    blocks = v.reshape(v.shape[:-1] + (-1, 32))
    amax = np.abs(blocks).max(-1, keepdims=True)
    byte = np.maximum(np.where(amax > 0, np.frexp(amax)[1] - 1 + 127, 0) - down, 1)
    scale = np.exp2(byte - 127.0)
    codes = (blocks / scale).astype(np.float32).astype(dtype).astype(np.float64)
    return np.moveaxis((codes * scale).reshape(v.shape), -1, axis)


WIDE = False


def mx_kscale(k):
    if not WIDE:
        return np.ones(k)
    levels = np.array([24, -24, 12, -12, 0])
    if k % 512:
        return np.exp2(np.random.permutation(np.resize(levels, k // 32))).repeat(32)
    a = np.empty((k // 512, 16))
    for p in range(k // 512):
        a[p, :8] = np.random.permutation(np.resize(levels, 8))
        for g in range(8):
            far = levels[np.abs(levels - a[p, g]) >= 10]
            a[p, g + 8] = far[np.random.randint(len(far))]
    return np.exp2(a.ravel()).repeat(32)


def f64(x):
    return np.asarray(x).astype(np.float64)


def striped(idx):
    return np.tile(idx.reshape(-1, 16).T, (8, 1)).astype(np.uint16)


def unstriped(offs):
    return offs[:16].T.reshape(-1).astype(np.int64)


E2M1 = np.array([0.0, 0.5, 1.0, 1.5, 2.0, 3.0, 4.0, 6.0, -0.0, -0.5, -1.0, -1.5, -2.0, -3.0, -4.0, -6.0])


def pack_weight(w, fmt):
    k, n = w.shape
    w = f64(np.asarray(w, np.float32).astype(ml_dtypes.bfloat16)).reshape(k // 32, 32, n)
    amax = np.abs(w).max(1)
    if fmt == "e4m3":
        byte = np.frexp(amax)[1] - 1 + 127 - 7
    else:
        mant, ex = np.frexp(amax / 6.0)
        byte = np.where(mant > 0.5, ex, ex - 1) + 127
    byte = np.clip(np.where(amax > 0, byte, 1), 1, 254)
    scaled = (w * np.exp2(127.0 - byte)[:, None, :]).reshape(k, n).astype(np.float32)
    by_word = np.ascontiguousarray(scaled.reshape(k // 512, 128, 4, n).transpose(0, 1, 3, 2))
    if fmt == "e4m3":
        words = by_word.astype(ml_dtypes.float8_e4m3fn).view(np.uint8)
    else:
        c = by_word.astype(ml_dtypes.float4_e2m1fn).view(np.uint8) & 0xF
        words = (c[..., 0::2] | (c[..., 1::2] << 4)).reshape(k // 512, 128, 2 * n)
    return np.ascontiguousarray(words), np.ascontiguousarray(byte.astype(np.uint8).reshape(k // 512, 16, n))


def unpack_weight(words, scales, fmt):
    g, _, n = scales.shape
    words = np.ascontiguousarray(words).reshape(g, 128, n, -1)
    if fmt == "e4m3":
        vals = words.view(ml_dtypes.float8_e4m3fn).astype(np.float64)
    else:
        nib = np.empty((g, 128, n, 4), np.uint8)
        nib[..., 0::2] = words & 0xF
        nib[..., 1::2] = words >> 4
        vals = E2M1[nib]
    vals = vals * np.repeat(np.exp2(scales.astype(np.float64) - 127.0), 8, axis=1)[..., None]
    return vals.transpose(0, 1, 3, 2).reshape(g * 512, n)


def pack_table4(v):
    words, scales = pack_weight(v, "e2m1")
    g, t = words.shape[0] // 2, v.shape[1]
    return np.ascontiguousarray(words.reshape(g, 2, 128, t, 2).transpose(0, 2, 3, 1, 4).reshape(g, 128, t, 4)), scales


def unpack_table4(words, scales):
    g, _, t, _ = words.shape
    return unpack_weight(words.reshape(g, 128, t, 2, 2).transpose(0, 3, 1, 2, 4).reshape(2 * g, 128, 2 * t), scales, "e2m1")


K, F, N, T, J = 1024, 512, 256, 4096, 1024


def setup_inputs():
    n = np.random.standard_normal
    s = mx_kscale(K)[:, None]
    u = mx_kscale(F)[:, None]
    p_tab = pack_table4(n((K, T)) * s)
    p_fb = pack_weight(np.abs(n((F, N))) / F / u, "e2m1")
    return {
        "tab_words": p_tab[0],
        "tab_scales": p_tab[1],
        "co": (n((K, F)) / np.sqrt(K) / s).astype(np.float32),
        "si": (n((K, F)) / np.sqrt(K) / s).astype(np.float32),
        "gn": (np.random.uniform(0.5, 2.0, F) * u[:, 0]).astype(np.float32),
        "fb_words": p_fb[0],
        "fb_scales": p_fb[1],
        "mu": (np.random.uniform(0.5, 1.5, N)).astype(np.float32),
        "isd": (np.random.uniform(0.5, 2.0, N)).astype(np.float32),
        "offs": striped(np.random.permutation(T)[:J]),
    }


def reference(tab_words, tab_scales, co, si, gn, fb_words, fb_scales, mu, isd, offs):
    idx = unstriped(offs)
    tab_ = unpack_table4(tab_words, tab_scales)[:, idx]
    co_ = mxq(f64(co), 0, "e4m3")
    si_ = mxq(f64(si), 0, "e4m3")
    re = co_.T @ tab_
    im = si_.T @ tab_
    h = f64(gn)[:, None] * ((re) ** 2 + (im) ** 2)
    h_ = mxq(h, 0, "e4m3")
    fb_ = unpack_weight(fb_words, fb_scales, "e2m1")
    y = fb_.T @ h_
    return (y - f64(mu)[:, None]) * f64(isd)[:, None]

@@ -1,0 +1,253 @@
+from contextlib import ExitStack
+
+import concourse.mybir as mybir
+
+K, F, N, T, J = 1024, 512, 256, 4096, 1024
+FLOPS = 2 * (2 * K * F * J + F * N * J)
+
+F32 = mybir.dt.float32
+BF16 = mybir.dt.bfloat16
+I32 = mybir.dt.int32
+U32 = mybir.dt.uint32
+U16 = mybir.dt.uint16
+U8 = mybir.dt.uint8
+FP8X4 = mybir.dt.float8_e4m3fn_x4
+FP4X4 = mybir.dt.float4_e2m1fn_x4
+ALU = mybir.AluOpType
+ACT = mybir.ActivationFunctionType
+
+P = 128
+PACK = 4
+HALF = 512
+CHUNK = 256
+TAB_HEAD = 1024
+SHIFT = 16
+
+
+def tile_list_meltab_norm_kernel(
+    tc, tab_words, tab_scales, co, si, gn, fb_words, fb_scales, mu, isd, offs, out
+):
+    nc = tc.nc
+    with ExitStack() as ctx:
+        keep = ctx.enter_context(tc.tile_pool(name="keep", bufs=1))
+        psum = ctx.enter_context(tc.psum_pool(name="psum", bufs=1))
+
+        def sb(name, shape, dtype):
+            return keep.tile(shape, dtype, name=name, align_bytes=64)
+
+        def bank(b, name):
+            return psum.tile([P, HALF], F32, name=name, tag="bank%d" % b)
+
+        offsets = keep.tile([P, J // 16], U16, name="offsets")
+        nc.sync.dma_start(offsets[:], offs)
+
+        tab = sb("tab", [P, T], I32)
+        tab_hbm = tab_words[0].rearrange("p t b -> p (t b)").bitcast(I32)
+        nc.sync.dma_start(tab[:, :TAB_HEAD], tab_hbm[:, :TAB_HEAD])
+
+        tsc = sb("tsc", [P, T // 4], I32)
+        nc.vector.memset(tsc[:], 0)
+        tsc_hbm = tab_scales.bitcast(I32).rearrange("a (q r) w -> r q a w", r=4)
+        for r in range(4):
+            nc.sync.dma_start(tsc[r:P:SHIFT, :], tsc_hbm[r])
+        nc.sync.dma_start(tab[:, TAB_HEAD:], tab_hbm[:, TAB_HEAD:])
+
+        raw = {}
+        for name, w in (("co", co), ("si", si)):
+            for a in range(2):
+                raw[name, a] = sb("raw_%s%d" % (name, a), [P, PACK, F], F32)
+                src = w[512 * a : 512 * (a + 1), :].rearrange("(p i) f -> p i f", i=PACK)
+                if (name, a) == ("si", 1):
+                    for u in range(2):
+                        cols = slice(u * F // 2, (u + 1) * F // 2)
+                        nc.sync.dma_start(raw[name, a][:, :, cols], src[:, :, cols])
+                else:
+                    nc.sync.dma_start(raw[name, a][:], src)
+
+        gain = sb("gain", [P, PACK], F32)
+        nc.scalar.dma_start(gain[:], gn.rearrange("(p t) -> p t", t=PACK))
+        fbw = sb("fbw", [P, 2 * N // 4], I32)
+        nc.sync.dma_start(fbw[:], fb_words[0].bitcast(I32))
+        fbs = sb("fbs", [P, N // 4], I32)
+        nc.vector.memset(fbs[:], 0)
+        fbs_hbm = fb_scales[0].bitcast(I32).rearrange("(q r) w -> r q w", r=4)
+        for r in range(4):
+            nc.sync.dma_start(fbs[r:P:32, :], fbs_hbm[r])
+        mean = sb("mean", [P, 2], F32)
+        rdev = sb("rdev", [P, 2], F32)
+        with nc.allow_non_contiguous_dma(reason="one value a partition"):
+            nc.sync.dma_start(mean[:], mu.rearrange("(c p) -> p c", p=P))
+            nc.sync.dma_start(rdev[:], isd.rearrange("(c p) -> p c", p=P))
+
+        ps1 = sb("ps1", [P, J // 4], I32)
+        nc.vector.memset(ps1[:], 0)
+
+        ps0 = sb("ps0", [P, J // 4], I32)
+        nc.vector.tensor_copy(ps0[:].bitcast(U8), tsc[:].bitcast(U8).indirect(offsets[:]))
+        nc.scalar.dma_start(ps1[0 : P - SHIFT, :], ps0[SHIFT:P, :])
+        planes = (ps0, ps1)
+
+        parted = []
+        for h in range(2):
+            picked = sb("picked%d" % h, [P, HALF], U32)
+            cols = slice(h * HALF // 16, (h + 1) * HALF // 16)
+            nc.vector.tensor_copy(picked[:], tab[:].bitcast(U32).indirect(offsets[:, cols]))
+            words = sb("words%d" % h, [P, 2, HALF], U16)
+            nc.vector.tensor_copy(words[:], picked[:].bitcast(U16).rearrange("p (j d) -> p d j", d=2))
+            parted.append(words)
+
+        mag = sb("mag", [P, PACK], F32)
+        guess = sb("guess", [P, PACK], F32)
+        sgn = sb("sgn", [P, PACK], BF16)
+        nc.scalar.activation(mag[:], gain[:], ACT.Abs)
+        nc.scalar.activation(guess[:], mag[:], ACT.Sqrt)
+        nc.scalar.activation(sgn[:], gain[:], ACT.Sign)
+        twice = sb("twice", [P, PACK], F32)
+        nc.vector.tensor_scalar(twice[:], guess[:], 1e-30, 2.0, ALU.max, ALU.mult)
+        rcp = sb("rcp", [P, PACK], F32)
+        nc.vector.reciprocal(rcp[:], twice[:])
+        quot = sb("quot", [P, PACK], F32)
+        nc.vector.tensor_tensor(quot[:], mag[:], rcp[:], ALU.mult)
+        root = sb("root", [P, PACK], F32)
+        nc.vector.scalar_tensor_tensor(root[:], guess[:], 0.5, quot[:], ALU.mult, ALU.add)
+        signs = sgn[:].unsqueeze(1).to_broadcast([P, CHUNK, PACK])
+
+        grouped, codes, scales = {}, {}, {}
+        for key in raw:
+            tag = "%s%d" % key
+            grouped[key] = sb("grouped_" + tag, [P, PACK, P, PACK], BF16)
+            codes[key] = sb("codes_" + tag, [P, F], U32)
+            scales[key] = sb("scales_" + tag, [P, F], U8)
+
+        def cast(key, copy, m0, m1):
+            dst = grouped[key][:, :, m0:m1, :].rearrange("p t m i -> p m i t")
+            src = raw[key][:, :, PACK * m0 : PACK * m1].rearrange("p i (m t) -> p m i t", t=PACK)
+            copy(dst, src)
+
+        def quantise(key, t0, t1):
+            cols = slice(P * t0, P * t1)
+            nc.vector.quantize_mx(
+                out=codes[key][:, cols].bitcast(FP8X4),
+                scales=scales[key][:, cols],
+                in_=grouped[key][:, t0:t1, :, :].rearrange("p t m i -> p (t m i)"),
+            )
+
+        def stage1(acc, key, t, h):
+            a = key[1]
+            cols = slice(P * t, P * (t + 1))
+            nc.tensor.matmul_mx(
+                acc[:],
+                lhsT=codes[key][:, cols].bitcast(FP8X4),
+                lhsT_scale=scales[key][:, cols],
+                rhs=parted[h][:, a, :].bitcast(FP4X4),
+                rhs_scale=planes[a][:].bitcast(U8)[:, h * HALF : (h + 1) * HALF],
+                start=(a == 0),
+                stop=(a == 1),
+            )
+
+        sq_re = sb("sq_re", [P, PACK, J], F32)
+        sq_im = sb("sq_im", [P, PACK, J], F32)
+
+        def square(dst, acc, t, h, c0, c1):
+            nc.scalar.activation(
+                dst[:, t, h * HALF + c0 : h * HALF + c1], acc[:, c0:c1], ACT.Square, scale=root[:, t : t + 1]
+            )
+
+        cast(("co", 0), nc.scalar.copy, 0, 64)
+        cast(("co", 0), nc.vector.tensor_copy, 64, 128)
+        quantise(("co", 0), 0, 4)
+        re = {(h, t): bank(4 * h + t, "re%d%d" % (h, t)) for h in range(2) for t in range(PACK)}
+        for h in range(2):
+            for t in range(PACK):
+                stage1(re[h, t], ("co", 0), t, h)
+        cast(("co", 1), nc.scalar.copy, 0, 44)
+        cast(("co", 1), nc.vector.tensor_copy, 44, 128)
+        for t in range(PACK):
+            quantise(("co", 1), t, t + 1)
+        for h in range(2):
+            for t in range(PACK):
+                stage1(re[h, t], ("co", 1), t, h)
+        for t in range(PACK):
+            square(sq_re, re[0, t], t, 0, 0, HALF)
+        cast(("si", 0), nc.vector.tensor_copy, 0, 128)
+        quantise(("si", 0), 0, 4)
+        im = {(0, t): bank(t, "im0%d" % t) for t in range(PACK)}
+        for t in range(PACK):
+            stage1(im[0, t], ("si", 0), t, 0)
+        cast(("si", 1), nc.vector.tensor_copy, 0, 64)
+        cast(("si", 1), nc.vector.tensor_copy, 64, 128)
+        for t in range(PACK):
+            quantise(("si", 1), t, t + 1)
+            stage1(im[0, t], ("si", 1), t, 0)
+        shift = sb("shift", [P, 2], F32)
+        nc.vector.scalar_tensor_tensor(shift[:], mean[:], -1.0, rdev[:], ALU.mult, ALU.mult)
+
+        for t in range(2):
+            square(sq_re, re[1, t], t, 1, 0, HALF)
+        for c in range(2):
+            for t in range(PACK):
+                square(sq_im, im[0, t], t, 0, c * CHUNK, (c + 1) * CHUNK)
+        for t in range(2, PACK):
+            square(sq_re, re[1, t], t, 1, 0, HALF)
+        for t in range(PACK):
+            im[1, t] = bank(4 + t, "im1%d" % t)
+            for a in range(2):
+                stage1(im[1, t], ("si", a), t, 1)
+        for c in range(2):
+            for t in range(PACK):
+                square(sq_im, im[1, t], t, 1, c * CHUNK, (c + 1) * CHUNK)
+
+        chunks = J // CHUNK
+        power = [sb("power%d" % c, [P, CHUNK, PACK], BF16) for c in range(chunks)]
+        signed = [sb("signed%d" % c, [P, CHUNK, PACK], BF16) for c in range(chunks)]
+        h_codes = [sb("h_codes%d" % c, [P, CHUNK], U32) for c in range(chunks)]
+        h_scales = [sb("h_scales%d" % c, [P, CHUNK], U8) for c in range(chunks)]
+        result = [sb("result%d" % c, [P, 2, CHUNK], F32) for c in range(chunks)]
+        out_v = out.rearrange("(u p) j -> p u j", p=P)
+
+        def add(c):
+            cols = slice(c * CHUNK, (c + 1) * CHUNK)
+            nc.vector.tensor_tensor(
+                power[c][:].rearrange("p (n i) t -> p n t i", i=4),
+                sq_re[:, :, cols].rearrange("p t (n i) -> p n t i", i=4),
+                sq_im[:, :, cols].rearrange("p t (n i) -> p n t i", i=4),
+                ALU.add,
+            )
+
+        def sign(c):
+            nc.vector.tensor_tensor(signed[c][:], power[c][:], signs, ALU.mult)
+
+        def finish(c):
+            nc.vector.quantize_mx(
+                out=h_codes[c][:].bitcast(FP8X4),
+                scales=h_scales[c][:],
+                in_=signed[c][:].rearrange("p n t -> p (n t)"),
+            )
+            y = bank(c, "y%d" % c)
+            for u in range(2):
+                nc.tensor.matmul_mx(
+                    y[:, u * CHUNK : (u + 1) * CHUNK],
+                    lhsT=fbw[:].bitcast(U8)[:, 2 * P * u : 2 * P * (u + 1)].bitcast(FP4X4),
+                    lhsT_scale=fbs[:].bitcast(U8)[:, P * u : P * (u + 1)],
+                    rhs=h_codes[c][:].bitcast(FP8X4),
+                    rhs_scale=h_scales[c][:],
+                    start=True,
+                    stop=True,
+                )
+            for u in range(2):
+                nc.scalar.activation(
+                    result[c][:, u, :],
+                    y[:, u * CHUNK : (u + 1) * CHUNK],
+                    ACT.Identity,
+                    bias=shift[:, u : u + 1],
+                    scale=rdev[:, u : u + 1],
+                )
+            nc.sync.dma_start(out_v[:, :, c * CHUNK : (c + 1) * CHUNK], result[c][:])
+
+        for step in range(chunks + 2):
+            if step < chunks:
+                add(step)
+            if 0 <= step - 2 < chunks:
+                finish(step - 2)
+            if 0 <= step - 1 < chunks:
+                sign(step - 1)

@@ -19,9 +19,9 @@ ACT = mybir.ActivationFunctionType
 P = 128
 PACK = 4
 HALF = 512
-CHUNK = 256
-TAB_HEAD = 1024
+WIDTHS = (256, 256, 256, 128, 128)
 SHIFT = 16
+SI0_ON_SCALAR = 64
 
 
 def tile_list_meltab_norm_kernel(
@@ -38,34 +38,31 @@ def tile_list_meltab_norm_kernel(
         def bank(b, name):
             return psum.tile([P, HALF], F32, name=name, tag="bank%d" % b)
 
-        offsets = keep.tile([P, J // 16], U16, name="offsets")
-        nc.sync.dma_start(offsets[:], offs)
+        raw = {}
 
-        tab = sb("tab", [P, T], I32)
-        tab_hbm = tab_words[0].rearrange("p t b -> p (t b)").bitcast(I32)
-        nc.sync.dma_start(tab[:, :TAB_HEAD], tab_hbm[:, :TAB_HEAD])
+        def load(name, w, a, pieces):
+            raw[name, a] = sb("raw_%s%d" % (name, a), [P, PACK, F], F32)
+            src = w[512 * a : 512 * (a + 1), :].rearrange("(p i) f -> p i f", i=PACK)
+            for u in range(pieces):
+                cols = slice(u * F // pieces, (u + 1) * F // pieces)
+                nc.sync.dma_start(raw[name, a][:, :, cols], src[:, :, cols])
 
         tsc = sb("tsc", [P, T // 4], I32)
         nc.vector.memset(tsc[:], 0)
+        load("co", co, 0, 1)
+        offsets = keep.tile([P, J // 16], U16, name="offsets")
+        nc.sync.dma_start(offsets[:], offs)
+        gain = sb("gain", [P, PACK], F32)
+        nc.gpsimd.dma_start(gain[:], gn.rearrange("(p t) -> p t", t=PACK))
         tsc_hbm = tab_scales.bitcast(I32).rearrange("a (q r) w -> r q a w", r=4)
         for r in range(4):
             nc.sync.dma_start(tsc[r:P:SHIFT, :], tsc_hbm[r])
-        nc.sync.dma_start(tab[:, TAB_HEAD:], tab_hbm[:, TAB_HEAD:])
+        tab = sb("tab", [P, T], I32)
+        nc.sync.dma_start(tab[:], tab_words[0].rearrange("p t b -> p (t b)").bitcast(I32))
+        load("co", co, 1, 1)
+        load("si", si, 0, 1)
+        load("si", si, 1, 2)
 
-        raw = {}
-        for name, w in (("co", co), ("si", si)):
-            for a in range(2):
-                raw[name, a] = sb("raw_%s%d" % (name, a), [P, PACK, F], F32)
-                src = w[512 * a : 512 * (a + 1), :].rearrange("(p i) f -> p i f", i=PACK)
-                if (name, a) == ("si", 1):
-                    for u in range(2):
-                        cols = slice(u * F // 2, (u + 1) * F // 2)
-                        nc.sync.dma_start(raw[name, a][:, :, cols], src[:, :, cols])
-                else:
-                    nc.sync.dma_start(raw[name, a][:], src)
-
-        gain = sb("gain", [P, PACK], F32)
-        nc.scalar.dma_start(gain[:], gn.rearrange("(p t) -> p t", t=PACK))
         fbw = sb("fbw", [P, 2 * N // 4], I32)
         nc.sync.dma_start(fbw[:], fb_words[0].bitcast(I32))
         fbs = sb("fbs", [P, N // 4], I32)
@@ -81,36 +78,10 @@ def tile_list_meltab_norm_kernel(
 
         ps1 = sb("ps1", [P, J // 4], I32)
         nc.vector.memset(ps1[:], 0)
-
         ps0 = sb("ps0", [P, J // 4], I32)
         nc.vector.tensor_copy(ps0[:].bitcast(U8), tsc[:].bitcast(U8).indirect(offsets[:]))
-        nc.scalar.dma_start(ps1[0 : P - SHIFT, :], ps0[SHIFT:P, :])
+        nc.gpsimd.dma_start(ps1[0 : P - SHIFT, :], ps0[SHIFT:P, :])
         planes = (ps0, ps1)
-
-        parted = []
-        for h in range(2):
-            picked = sb("picked%d" % h, [P, HALF], U32)
-            cols = slice(h * HALF // 16, (h + 1) * HALF // 16)
-            nc.vector.tensor_copy(picked[:], tab[:].bitcast(U32).indirect(offsets[:, cols]))
-            words = sb("words%d" % h, [P, 2, HALF], U16)
-            nc.vector.tensor_copy(words[:], picked[:].bitcast(U16).rearrange("p (j d) -> p d j", d=2))
-            parted.append(words)
-
-        mag = sb("mag", [P, PACK], F32)
-        guess = sb("guess", [P, PACK], F32)
-        sgn = sb("sgn", [P, PACK], BF16)
-        nc.scalar.activation(mag[:], gain[:], ACT.Abs)
-        nc.scalar.activation(guess[:], mag[:], ACT.Sqrt)
-        nc.scalar.activation(sgn[:], gain[:], ACT.Sign)
-        twice = sb("twice", [P, PACK], F32)
-        nc.vector.tensor_scalar(twice[:], guess[:], 1e-30, 2.0, ALU.max, ALU.mult)
-        rcp = sb("rcp", [P, PACK], F32)
-        nc.vector.reciprocal(rcp[:], twice[:])
-        quot = sb("quot", [P, PACK], F32)
-        nc.vector.tensor_tensor(quot[:], mag[:], rcp[:], ALU.mult)
-        root = sb("root", [P, PACK], F32)
-        nc.vector.scalar_tensor_tensor(root[:], guess[:], 0.5, quot[:], ALU.mult, ALU.add)
-        signs = sgn[:].unsqueeze(1).to_broadcast([P, CHUNK, PACK])
 
         grouped, codes, scales = {}, {}, {}
         for key in raw:
@@ -132,6 +103,17 @@ def tile_list_meltab_norm_kernel(
                 in_=grouped[key][:, t0:t1, :, :].rearrange("p t m i -> p (t m i)"),
             )
 
+        picked = {}
+        parted = [sb("parted%d" % h, [P, 2, HALF], U16) for h in range(2)]
+
+        def gather(h):
+            cols = slice(h * HALF // 16, (h + 1) * HALF // 16)
+            picked[h] = sb("picked", [P, HALF], U32)
+            nc.vector.tensor_copy(picked[h][:], tab[:].bitcast(U32).indirect(offsets[:, cols]))
+
+        def part(h):
+            nc.vector.tensor_copy(parted[h][:], picked[h][:].bitcast(U16).rearrange("p (j d) -> p d j", d=2))
+
         def stage1(acc, key, t, h):
             a = key[1]
             cols = slice(P * t, P * (t + 1))
@@ -148,65 +130,80 @@ def tile_list_meltab_norm_kernel(
         sq_re = sb("sq_re", [P, PACK, J], F32)
         sq_im = sb("sq_im", [P, PACK, J], F32)
 
+        step = sb("step", [P, PACK], F32)
+        sgn = sb("sgn", [P, PACK], BF16)
+        mag = sb("mag", [P, PACK], F32)
+        half = sb("half", [P, PACK], F32)
+        root = sb("root", [P, PACK], F32)
+        nc.gpsimd.memset(half[:], 0.5)
+        nc.gpsimd.tensor_scalar(step[:], gain[:], 0.0, 2.0, ALU.is_ge, ALU.mult)
+        nc.gpsimd.tensor_scalar(sgn[:], step[:], -1.0, None, ALU.add)
+        nc.gpsimd.tensor_tensor(mag[:], gain[:], sgn[:], ALU.mult)
+        nc.gpsimd.tensor_tensor(root[:], mag[:], half[:], ALU.pow)
+        cast(("co", 0), nc.scalar.copy, 0, P)
+
         def square(dst, acc, t, h, c0, c1):
             nc.scalar.activation(
-                dst[:, t, h * HALF + c0 : h * HALF + c1], acc[:, c0:c1], ACT.Square, scale=root[:, t : t + 1]
+                dst[:, t, c0:c1], acc[:, c0 - h * HALF : c1 - h * HALF], ACT.Square, scale=root[:, t : t + 1]
             )
 
-        cast(("co", 0), nc.scalar.copy, 0, 64)
-        cast(("co", 0), nc.vector.tensor_copy, 64, 128)
         quantise(("co", 0), 0, 4)
+        gather(0)
+        part(0)
         re = {(h, t): bank(4 * h + t, "re%d%d" % (h, t)) for h in range(2) for t in range(PACK)}
-        for h in range(2):
-            for t in range(PACK):
-                stage1(re[h, t], ("co", 0), t, h)
-        cast(("co", 1), nc.scalar.copy, 0, 44)
-        cast(("co", 1), nc.vector.tensor_copy, 44, 128)
+        for t in range(PACK):
+            stage1(re[0, t], ("co", 0), t, 0)
+        gather(1)
+        cast(("co", 1), nc.scalar.copy, 0, P)
         for t in range(PACK):
             quantise(("co", 1), t, t + 1)
-        for h in range(2):
-            for t in range(PACK):
-                stage1(re[h, t], ("co", 1), t, h)
+            stage1(re[0, t], ("co", 1), t, 0)
+        part(1)
+        cast(("si", 0), nc.scalar.copy, 0, SI0_ON_SCALAR)
+        cast(("si", 0), nc.vector.tensor_copy, SI0_ON_SCALAR, P)
         for t in range(PACK):
             square(sq_re, re[0, t], t, 0, 0, HALF)
-        cast(("si", 0), nc.vector.tensor_copy, 0, 128)
         quantise(("si", 0), 0, 4)
         im = {(0, t): bank(t, "im0%d" % t) for t in range(PACK)}
         for t in range(PACK):
             stage1(im[0, t], ("si", 0), t, 0)
-        cast(("si", 1), nc.vector.tensor_copy, 0, 64)
-        cast(("si", 1), nc.vector.tensor_copy, 64, 128)
+        for u in range(2):
+            cast(("si", 1), nc.vector.tensor_copy, u * P // 2, (u + 1) * P // 2)
         for t in range(PACK):
             quantise(("si", 1), t, t + 1)
             stage1(im[0, t], ("si", 1), t, 0)
         shift = sb("shift", [P, 2], F32)
         nc.vector.scalar_tensor_tensor(shift[:], mean[:], -1.0, rdev[:], ALU.mult, ALU.mult)
 
-        for t in range(2):
-            square(sq_re, re[1, t], t, 1, 0, HALF)
-        for c in range(2):
-            for t in range(PACK):
-                square(sq_im, im[0, t], t, 0, c * CHUNK, (c + 1) * CHUNK)
-        for t in range(2, PACK):
-            square(sq_re, re[1, t], t, 1, 0, HALF)
         for t in range(PACK):
-            im[1, t] = bank(4 + t, "im1%d" % t)
+            for a in range(2):
+                stage1(re[1, t], ("co", a), t, 1)
+
+        chunks = len(WIDTHS)
+        spans = [(sum(WIDTHS[:c]), sum(WIDTHS[: c + 1])) for c in range(chunks)]
+        for c0, c1 in spans:
+            if c1 <= HALF:
+                for t in range(PACK):
+                    square(sq_im, im[0, t], t, 0, c0, c1)
+        for t in range(PACK):
+            square(sq_re, re[1, t], t, 1, HALF, J)
+            im[1, t] = bank(t, "im1%d" % t)
             for a in range(2):
                 stage1(im[1, t], ("si", a), t, 1)
-        for c in range(2):
-            for t in range(PACK):
-                square(sq_im, im[1, t], t, 1, c * CHUNK, (c + 1) * CHUNK)
+        for c0, c1 in spans:
+            if c1 > HALF:
+                for t in range(PACK):
+                    square(sq_im, im[1, t], t, 1, c0, c1)
 
-        chunks = J // CHUNK
-        power = [sb("power%d" % c, [P, CHUNK, PACK], BF16) for c in range(chunks)]
-        signed = [sb("signed%d" % c, [P, CHUNK, PACK], BF16) for c in range(chunks)]
-        h_codes = [sb("h_codes%d" % c, [P, CHUNK], U32) for c in range(chunks)]
-        h_scales = [sb("h_scales%d" % c, [P, CHUNK], U8) for c in range(chunks)]
-        result = [sb("result%d" % c, [P, 2, CHUNK], F32) for c in range(chunks)]
+        power = [sb("power%d" % c, [P, WIDTHS[c], PACK], BF16) for c in range(chunks)]
+        signed = [sb("signed%d" % c, [P, WIDTHS[c], PACK], BF16) for c in range(chunks)]
+        h_codes = [sb("h_codes%d" % c, [P, WIDTHS[c]], U32) for c in range(chunks)]
+        h_scales = [sb("h_scales%d" % c, [P, WIDTHS[c]], U8) for c in range(chunks)]
+        result = [sb("result%d" % c, [P, 2, WIDTHS[c]], F32) for c in range(chunks)]
         out_v = out.rearrange("(u p) j -> p u j", p=P)
 
         def add(c):
-            cols = slice(c * CHUNK, (c + 1) * CHUNK)
+            cols = slice(spans[c][0], spans[c][1])
             nc.vector.tensor_tensor(
                 power[c][:].rearrange("p (n i) t -> p n t i", i=4),
                 sq_re[:, :, cols].rearrange("p t (n i) -> p n t i", i=4),
@@ -215,18 +212,22 @@ def tile_list_meltab_norm_kernel(
             )
 
         def sign(c):
+            signs = sgn[:].unsqueeze(1).to_broadcast([P, WIDTHS[c], PACK])
             nc.vector.tensor_tensor(signed[c][:], power[c][:], signs, ALU.mult)
 
         def finish(c):
+            width = WIDTHS[c]
             nc.vector.quantize_mx(
                 out=h_codes[c][:].bitcast(FP8X4),
                 scales=h_scales[c][:],
                 in_=signed[c][:].rearrange("p n t -> p (n t)"),
             )
-            y = bank(c, "y%d" % c)
+            last = c == chunks - 1
+            y = [bank(4 + c % 4, "y%d" % c)]
+            y.append(bank(4 + (c + 1) % 4, "y_last") if last else y[0])
             for u in range(2):
                 nc.tensor.matmul_mx(
-                    y[:, u * CHUNK : (u + 1) * CHUNK],
+                    y[u][:, u * width : (u + 1) * width],
                     lhsT=fbw[:].bitcast(U8)[:, 2 * P * u : 2 * P * (u + 1)].bitcast(FP4X4),
                     lhsT_scale=fbs[:].bitcast(U8)[:, P * u : P * (u + 1)],
                     rhs=h_codes[c][:].bitcast(FP8X4),
@@ -235,19 +236,23 @@ def tile_list_meltab_norm_kernel(
                     stop=True,
                 )
             for u in range(2):
-                nc.scalar.activation(
-                    result[c][:, u, :],
-                    y[:, u * CHUNK : (u + 1) * CHUNK],
-                    ACT.Identity,
-                    bias=shift[:, u : u + 1],
-                    scale=rdev[:, u : u + 1],
-                )
-            nc.sync.dma_start(out_v[:, :, c * CHUNK : (c + 1) * CHUNK], result[c][:])
+                acc = y[u][:, u * width : (u + 1) * width]
+                if last and u == 1:
+                    nc.vector.tensor_scalar(
+                        result[c][:, u, :], acc, rdev[:, u : u + 1], shift[:, u : u + 1], ALU.mult, ALU.add
+                    )
+                else:
+                    nc.scalar.activation(
+                        result[c][:, u, :], acc, ACT.Identity, bias=shift[:, u : u + 1], scale=rdev[:, u : u + 1]
+                    )
+            nc.sync.dma_start(out_v[:, :, spans[c][0] : spans[c][1]], result[c][:])
 
-        for step in range(chunks + 2):
-            if step < chunks:
-                add(step)
-            if 0 <= step - 2 < chunks:
-                finish(step - 2)
-            if 0 <= step - 1 < chunks:
-                sign(step - 1)
+        add(0)
+        for c in range(1, chunks):
+            add(c)
+            if c >= 2:
+                finish(c - 2)
+            sign(c - 1)
+        sign(chunks - 1)
+        finish(chunks - 2)
+        finish(chunks - 1)

@@ -80,7 +80,7 @@ def tile_list_meltab_norm_kernel(
         nc.vector.memset(ps1[:], 0)
         ps0 = sb("ps0", [P, J // 4], I32)
         nc.vector.tensor_copy(ps0[:].bitcast(U8), tsc[:].bitcast(U8).indirect(offsets[:]))
-        nc.gpsimd.dma_start(ps1[0 : P - SHIFT, :], ps0[SHIFT:P, :])
+        nc.scalar.dma_start(ps1[0 : P - SHIFT, :], ps0[SHIFT:P, :])
         planes = (ps0, ps1)
 
         grouped, codes, scales = {}, {}, {}
@@ -147,10 +147,13 @@ def tile_list_meltab_norm_kernel(
                 dst[:, t, c0:c1], acc[:, c0 - h * HALF : c1 - h * HALF], ACT.Square, scale=root[:, t : t + 1]
             )
 
+        chunks = len(WIDTHS)
+        spans = [(sum(WIDTHS[:c]), sum(WIDTHS[: c + 1])) for c in range(chunks)]
+
         quantise(("co", 0), 0, 4)
         gather(0)
         part(0)
-        re = {(h, t): bank(4 * h + t, "re%d%d" % (h, t)) for h in range(2) for t in range(PACK)}
+        re = {(0, t): bank(t, "re0%d" % t) for t in range(PACK)}
         for t in range(PACK):
             stage1(re[0, t], ("co", 0), t, 0)
         gather(1)
@@ -158,13 +161,10 @@ def tile_list_meltab_norm_kernel(
         for t in range(PACK):
             quantise(("co", 1), t, t + 1)
             stage1(re[0, t], ("co", 1), t, 0)
-        part(1)
         cast(("si", 0), nc.scalar.copy, 0, SI0_ON_SCALAR)
         cast(("si", 0), nc.vector.tensor_copy, SI0_ON_SCALAR, P)
-        for t in range(PACK):
-            square(sq_re, re[0, t], t, 0, 0, HALF)
         quantise(("si", 0), 0, 4)
-        im = {(0, t): bank(t, "im0%d" % t) for t in range(PACK)}
+        im = {(0, t): bank(4 + t, "im0%d" % t) for t in range(PACK)}
         for t in range(PACK):
             stage1(im[0, t], ("si", 0), t, 0)
         for u in range(2):
@@ -172,24 +172,25 @@ def tile_list_meltab_norm_kernel(
         for t in range(PACK):
             quantise(("si", 1), t, t + 1)
             stage1(im[0, t], ("si", 1), t, 0)
+        part(1)
         shift = sb("shift", [P, 2], F32)
         nc.vector.scalar_tensor_tensor(shift[:], mean[:], -1.0, rdev[:], ALU.mult, ALU.mult)
-
         for t in range(PACK):
-            for a in range(2):
-                stage1(re[1, t], ("co", a), t, 1)
-
-        chunks = len(WIDTHS)
-        spans = [(sum(WIDTHS[:c]), sum(WIDTHS[: c + 1])) for c in range(chunks)]
+            square(sq_re, re[0, t], t, 0, 0, HALF)
         for c0, c1 in spans:
             if c1 <= HALF:
                 for t in range(PACK):
                     square(sq_im, im[0, t], t, 0, c0, c1)
         for t in range(PACK):
-            square(sq_re, re[1, t], t, 1, HALF, J)
-            im[1, t] = bank(t, "im1%d" % t)
+            re[1, t] = bank(t, "re1%d" % t)
+            for a in range(2):
+                stage1(re[1, t], ("co", a), t, 1)
+        for t in range(PACK):
+            im[1, t] = bank(4 + t, "im1%d" % t)
             for a in range(2):
                 stage1(im[1, t], ("si", a), t, 1)
+        for t in range(PACK):
+            square(sq_re, re[1, t], t, 1, HALF, J)
         for c0, c1 in spans:
             if c1 > HALF:
                 for t in range(PACK):
@@ -223,8 +224,8 @@ def tile_list_meltab_norm_kernel(
                 in_=signed[c][:].rearrange("p n t -> p (n t)"),
             )
             last = c == chunks - 1
-            y = [bank(4 + c % 4, "y%d" % c)]
-            y.append(bank(4 + (c + 1) % 4, "y_last") if last else y[0])
+            y = [bank(c % 4, "y%d" % c)]
+            y.append(bank((c + 1) % 4, "y_last") if last else y[0])
             for u in range(2):
                 nc.tensor.matmul_mx(
                     y[u][:, u * width : (u + 1) * width],

@@ -20,7 +20,6 @@ P = 128
 PACK = 4
 HALF = 512
 WIDTHS = (256, 256, 256, 128, 128)
-SHIFT = 16
 SI0_ON_SCALAR = 64
 
 
@@ -54,9 +53,7 @@ def tile_list_meltab_norm_kernel(
         nc.sync.dma_start(offsets[:], offs)
         gain = sb("gain", [P, PACK], F32)
         nc.gpsimd.dma_start(gain[:], gn.rearrange("(p t) -> p t", t=PACK))
-        tsc_hbm = tab_scales.bitcast(I32).rearrange("a (q r) w -> r q a w", r=4)
-        for r in range(4):
-            nc.sync.dma_start(tsc[r:P:SHIFT, :], tsc_hbm[r])
+        nc.sync.dma_start(tsc[0:P:4, :], tab_scales.bitcast(I32).rearrange("a q w -> (a q) w"))
         tab = sb("tab", [P, T], I32)
         nc.sync.dma_start(tab[:], tab_words[0].rearrange("p t b -> p (t b)").bitcast(I32))
         load("co", co, 1, 1)
@@ -76,12 +73,14 @@ def tile_list_meltab_norm_kernel(
             nc.sync.dma_start(mean[:], mu.rearrange("(c p) -> p c", p=P))
             nc.sync.dma_start(rdev[:], isd.rearrange("(c p) -> p c", p=P))
 
-        ps1 = sb("ps1", [P, J // 4], I32)
-        nc.vector.memset(ps1[:], 0)
-        ps0 = sb("ps0", [P, J // 4], I32)
-        nc.vector.tensor_copy(ps0[:].bitcast(U8), tsc[:].bitcast(U8).indirect(offsets[:]))
-        nc.scalar.dma_start(ps1[0 : P - SHIFT, :], ps0[SHIFT:P, :])
-        planes = (ps0, ps1)
+        planes = [sb("plane%d" % a, [P, J // 4], I32) for a in range(2)]
+        for plane in planes:
+            nc.vector.memset(plane[:], 0)
+        spread = sb("spread", [P, J // 4], I32)
+        nc.vector.tensor_copy(spread[:].bitcast(U8), tsc[:].bitcast(U8).indirect(offsets[:]))
+        for a in range(2):
+            for r in range(4):
+                nc.scalar.dma_start(planes[a][r:P:32, :], spread[64 * a + 4 * r : 64 * (a + 1) : 16, :])
 
         grouped, codes, scales = {}, {}, {}
         for key in raw:
@@ -91,8 +90,8 @@ def tile_list_meltab_norm_kernel(
             scales[key] = sb("scales_" + tag, [P, F], U8)
 
         def cast(key, copy, m0, m1):
-            dst = grouped[key][:, :, m0:m1, :].rearrange("p t m i -> p m i t")
-            src = raw[key][:, :, PACK * m0 : PACK * m1].rearrange("p i (m t) -> p m i t", t=PACK)
+            dst = grouped[key][:, :, m0:m1, :].rearrange("p t m i -> p m t i")
+            src = raw[key][:, :, PACK * m0 : PACK * m1].rearrange("p i (m t) -> p m t i", t=PACK)
             copy(dst, src)
 
         def quantise(key, t0, t1):

@@ -18,9 +18,13 @@ ACT = mybir.ActivationFunctionType
 
 P = 128
 PACK = 4
+K_PASS = P * PACK
+PASSES = K // K_PASS
 HALF = 512
 WIDTHS = (256, 256, 256, 128, 128)
-SI0_ON_SCALAR = 64
+ON_SCALAR = {("co", 0): 4, ("co", 1): 4, ("si", 0): 2, ("si", 1): 0}
+PIECES = {("co", 0): 1, ("co", 1): 1, ("si", 0): 1, ("si", 1): 2}
+RE_BANK, IM_BANK = 0, 4
 
 
 def tile_list_meltab_norm_kernel(
@@ -39,71 +43,78 @@ def tile_list_meltab_norm_kernel(
 
         raw = {}
 
-        def load(name, w, a, pieces):
-            raw[name, a] = sb("raw_%s%d" % (name, a), [P, PACK, F], F32)
-            src = w[512 * a : 512 * (a + 1), :].rearrange("(p i) f -> p i f", i=PACK)
-            for u in range(pieces):
-                cols = slice(u * F // pieces, (u + 1) * F // pieces)
-                nc.sync.dma_start(raw[name, a][:, :, cols], src[:, :, cols])
+        def load_weight(key, w):
+            name, a = key
+            width = F // PIECES[key]
+            src = w[K_PASS * a : K_PASS * (a + 1), :].rearrange("(p i) f -> p i f", i=PACK)
+            for u in range(PIECES[key]):
+                raw[key, u] = sb("raw_%s%d%d" % (name, a, u), [P, PACK, width], F32)
+                nc.sync.dma_start(raw[key, u][:], src[:, :, u * width : (u + 1) * width])
 
-        tsc = sb("tsc", [P, T // 4], I32)
-        nc.vector.memset(tsc[:], 0)
-        load("co", co, 0, 1)
+        tab_rows = sb("tab_rows", [P, T // 4], I32)
+        nc.vector.memset(tab_rows[:], 0)
+        load_weight(("co", 0), co)
         offsets = keep.tile([P, J // 16], U16, name="offsets")
         nc.sync.dma_start(offsets[:], offs)
         gain = sb("gain", [P, PACK], F32)
         nc.gpsimd.dma_start(gain[:], gn.rearrange("(p t) -> p t", t=PACK))
-        nc.sync.dma_start(tsc[0:P:4, :], tab_scales.bitcast(I32).rearrange("a q w -> (a q) w"))
+        nc.sync.dma_start(tab_rows[0:P:4, :], tab_scales.bitcast(I32).rearrange("a q w -> (a q) w"))
         tab = sb("tab", [P, T], I32)
         nc.sync.dma_start(tab[:], tab_words[0].rearrange("p t b -> p (t b)").bitcast(I32))
-        load("co", co, 1, 1)
-        load("si", si, 0, 1)
-        load("si", si, 1, 2)
+        load_weight(("co", 1), co)
+        load_weight(("si", 0), si)
+        load_weight(("si", 1), si)
 
-        fbw = sb("fbw", [P, 2 * N // 4], I32)
-        nc.sync.dma_start(fbw[:], fb_words[0].bitcast(I32))
-        fbs = sb("fbs", [P, N // 4], I32)
-        nc.vector.memset(fbs[:], 0)
-        fbs_hbm = fb_scales[0].bitcast(I32).rearrange("(q r) w -> r q w", r=4)
+        fb_codes = sb("fb_codes", [P, 2 * N // 4], I32)
+        nc.sync.dma_start(fb_codes[:], fb_words[0].bitcast(I32))
+        fb_plane = sb("fb_plane", [P, N // 4], I32)
+        nc.vector.memset(fb_plane[:], 0)
+        fb_rows = fb_scales[0].bitcast(I32).rearrange("(q r) w -> r q w", r=4)
         for r in range(4):
-            nc.sync.dma_start(fbs[r:P:32, :], fbs_hbm[r])
+            nc.sync.dma_start(fb_plane[r:P:32, :], fb_rows[r])
         mean = sb("mean", [P, 2], F32)
         rdev = sb("rdev", [P, 2], F32)
         with nc.allow_non_contiguous_dma(reason="one value a partition"):
-            nc.sync.dma_start(mean[:], mu.rearrange("(c p) -> p c", p=P))
-            nc.sync.dma_start(rdev[:], isd.rearrange("(c p) -> p c", p=P))
+            nc.sync.dma_start(mean[:], mu.rearrange("(u p) -> p u", p=P))
+            nc.sync.dma_start(rdev[:], isd.rearrange("(u p) -> p u", p=P))
 
-        planes = [sb("plane%d" % a, [P, J // 4], I32) for a in range(2)]
+        planes = [sb("plane%d" % a, [P, J // 4], I32) for a in range(PASSES)]
         for plane in planes:
             nc.vector.memset(plane[:], 0)
-        spread = sb("spread", [P, J // 4], I32)
-        nc.vector.tensor_copy(spread[:].bitcast(U8), tsc[:].bitcast(U8).indirect(offsets[:]))
-        for a in range(2):
+        picked_rows = sb("picked_rows", [P, J // 4], I32)
+        nc.vector.tensor_copy(picked_rows[:].bitcast(U8), tab_rows[:].bitcast(U8).indirect(offsets[:]))
+        for a in range(PASSES):
             for r in range(4):
-                nc.scalar.dma_start(planes[a][r:P:32, :], spread[64 * a + 4 * r : 64 * (a + 1) : 16, :])
+                nc.scalar.dma_start(planes[a][r:P:32, :], picked_rows[64 * a + 4 * r : 64 * (a + 1) : 16, :])
 
         grouped, codes, scales = {}, {}, {}
-        for key in raw:
-            tag = "%s%d" % key
-            grouped[key] = sb("grouped_" + tag, [P, PACK, P, PACK], BF16)
-            codes[key] = sb("codes_" + tag, [P, F], U32)
-            scales[key] = sb("scales_" + tag, [P, F], U8)
+        for key in PIECES:
+            codes[key] = sb("codes_%s%d" % key, [P, F], U32)
+            scales[key] = sb("scales_%s%d" % key, [P, F], U8)
+            for u in range(PIECES[key]):
+                shape = [P, PACK, P // PIECES[key], PACK]
+                grouped[key, u] = sb("grouped_%s%d%d" % (key[0], key[1], u), shape, BF16)
 
-        def cast(key, copy, m0, m1):
-            dst = grouped[key][:, :, m0:m1, :].rearrange("p t m i -> p m t i")
-            src = raw[key][:, :, PACK * m0 : PACK * m1].rearrange("p i (m t) -> p m t i", t=PACK)
-            copy(dst, src)
+        def cast(key, u):
+            src = raw[key, u][:].rearrange("p i (m t) -> p m i t", t=PACK)
+            dst = grouped[key, u][:].rearrange("p t m i -> p m i t")
+            split = ON_SCALAR[key]
+            if split > 0:
+                nc.scalar.copy(dst[:, :, :, :split], src[:, :, :, :split])
+            if split < PACK:
+                nc.vector.tensor_copy(dst[:, :, :, split:], src[:, :, :, split:])
 
-        def quantise(key, t0, t1):
-            cols = slice(P * t0, P * t1)
+        def quantise(key, u, t0, t1):
+            width = P // PIECES[key]
+            cols = slice(P * t0 + width * u, P * (t1 - 1) + width * (u + 1))
             nc.vector.quantize_mx(
                 out=codes[key][:, cols].bitcast(FP8X4),
                 scales=scales[key][:, cols],
-                in_=grouped[key][:, t0:t1, :, :].rearrange("p t m i -> p (t m i)"),
+                in_=grouped[key, u][:, t0:t1, :, :].rearrange("p t m i -> p (t m i)"),
             )
 
         picked = {}
-        parted = [sb("parted%d" % h, [P, 2, HALF], U16) for h in range(2)]
+        parted = [sb("parted%d" % h, [P, PASSES, HALF], U16) for h in range(2)]
 
         def gather(h):
             cols = slice(h * HALF // 16, (h + 1) * HALF // 16)
@@ -111,9 +122,9 @@ def tile_list_meltab_norm_kernel(
             nc.vector.tensor_copy(picked[h][:], tab[:].bitcast(U32).indirect(offsets[:, cols]))
 
         def part(h):
-            nc.vector.tensor_copy(parted[h][:], picked[h][:].bitcast(U16).rearrange("p (j d) -> p d j", d=2))
+            nc.vector.tensor_copy(parted[h][:], picked[h][:].bitcast(U16).rearrange("p (j a) -> p a j", a=PASSES))
 
-        def stage1(acc, key, t, h):
+        def transform(acc, key, t, h):
             a = key[1]
             cols = slice(P * t, P * (t + 1))
             nc.tensor.matmul_mx(
@@ -123,91 +134,90 @@ def tile_list_meltab_norm_kernel(
                 rhs=parted[h][:, a, :].bitcast(FP4X4),
                 rhs_scale=planes[a][:].bitcast(U8)[:, h * HALF : (h + 1) * HALF],
                 start=(a == 0),
-                stop=(a == 1),
-            )
-
-        sq_re = sb("sq_re", [P, PACK, J], F32)
-        sq_im = sb("sq_im", [P, PACK, J], F32)
-
-        step = sb("step", [P, PACK], F32)
-        sgn = sb("sgn", [P, PACK], BF16)
-        mag = sb("mag", [P, PACK], F32)
-        half = sb("half", [P, PACK], F32)
-        root = sb("root", [P, PACK], F32)
-        nc.gpsimd.memset(half[:], 0.5)
-        nc.gpsimd.tensor_scalar(step[:], gain[:], 0.0, 2.0, ALU.is_ge, ALU.mult)
-        nc.gpsimd.tensor_scalar(sgn[:], step[:], -1.0, None, ALU.add)
-        nc.gpsimd.tensor_tensor(mag[:], gain[:], sgn[:], ALU.mult)
-        nc.gpsimd.tensor_tensor(root[:], mag[:], half[:], ALU.pow)
-        cast(("co", 0), nc.scalar.copy, 0, P)
-
-        def square(dst, acc, t, h, c0, c1):
-            nc.scalar.activation(
-                dst[:, t, c0:c1], acc[:, c0 - h * HALF : c1 - h * HALF], ACT.Square, scale=root[:, t : t + 1]
+                stop=(a == PASSES - 1),
             )
 
         chunks = len(WIDTHS)
         spans = [(sum(WIDTHS[:c]), sum(WIDTHS[: c + 1])) for c in range(chunks)]
+        half_of = [j0 // HALF for j0, j1 in spans]
+        sq_re = [sb("sq_re%d" % h, [P, PACK, HALF], F32) for h in range(2)]
+        sq_im = [sb("sq_im%d" % c, [P, PACK, WIDTHS[c]], F32) for c in range(chunks)]
 
-        quantise(("co", 0), 0, 4)
+        def in_half(c):
+            return slice(spans[c][0] % HALF, spans[c][0] % HALF + WIDTHS[c])
+
+        step = sb("step", [P, PACK], F32)
+        sgn = sb("sgn", [P, PACK], BF16)
+        mag = sb("mag", [P, PACK], F32)
+        exponent = sb("exponent", [P, PACK], F32)
+        root = sb("root", [P, PACK], F32)
+        nc.gpsimd.memset(exponent[:], 0.5)
+        nc.gpsimd.tensor_scalar(step[:], gain[:], 0.0, 2.0, ALU.is_ge, ALU.mult)
+        nc.gpsimd.tensor_scalar(sgn[:], step[:], -1.0, None, ALU.add)
+        nc.gpsimd.tensor_tensor(mag[:], gain[:], sgn[:], ALU.mult)
+        nc.gpsimd.tensor_tensor(root[:], mag[:], exponent[:], ALU.pow)
+        cast(("co", 0), 0)
+
+        def square(dst, acc, t):
+            nc.scalar.activation(dst, acc, ACT.Square, scale=root[:, t : t + 1])
+
+        def square_half(h):
+            for t in range(PACK):
+                square(sq_re[h][:, t, :], re[h, t][:], t)
+            for c in range(chunks):
+                if half_of[c] == h:
+                    for t in range(PACK):
+                        square(sq_im[c][:, t, :], im[h, t][:, in_half(c)], t)
+
+        quantise(("co", 0), 0, 0, PACK)
         gather(0)
         part(0)
-        re = {(0, t): bank(t, "re0%d" % t) for t in range(PACK)}
+        re = {(0, t): bank(RE_BANK + t, "re0%d" % t) for t in range(PACK)}
         for t in range(PACK):
-            stage1(re[0, t], ("co", 0), t, 0)
+            transform(re[0, t], ("co", 0), t, 0)
         gather(1)
-        cast(("co", 1), nc.scalar.copy, 0, P)
+        cast(("co", 1), 0)
         for t in range(PACK):
-            quantise(("co", 1), t, t + 1)
-            stage1(re[0, t], ("co", 1), t, 0)
-        cast(("si", 0), nc.scalar.copy, 0, SI0_ON_SCALAR)
-        cast(("si", 0), nc.vector.tensor_copy, SI0_ON_SCALAR, P)
-        quantise(("si", 0), 0, 4)
-        im = {(0, t): bank(4 + t, "im0%d" % t) for t in range(PACK)}
+            quantise(("co", 1), 0, t, t + 1)
+            transform(re[0, t], ("co", 1), t, 0)
+        cast(("si", 0), 0)
+        quantise(("si", 0), 0, 0, PACK)
+        im = {(0, t): bank(IM_BANK + t, "im0%d" % t) for t in range(PACK)}
         for t in range(PACK):
-            stage1(im[0, t], ("si", 0), t, 0)
-        for u in range(2):
-            cast(("si", 1), nc.vector.tensor_copy, u * P // 2, (u + 1) * P // 2)
+            transform(im[0, t], ("si", 0), t, 0)
+        cast(("si", 1), 0)
+        cast(("si", 1), 1)
         for t in range(PACK):
-            quantise(("si", 1), t, t + 1)
-            stage1(im[0, t], ("si", 1), t, 0)
+            quantise(("si", 1), 0, t, t + 1)
+            quantise(("si", 1), 1, t, t + 1)
+            transform(im[0, t], ("si", 1), t, 0)
         part(1)
         shift = sb("shift", [P, 2], F32)
         nc.vector.scalar_tensor_tensor(shift[:], mean[:], -1.0, rdev[:], ALU.mult, ALU.mult)
+        square_half(0)
+
         for t in range(PACK):
-            square(sq_re, re[0, t], t, 0, 0, HALF)
-        for c0, c1 in spans:
-            if c1 <= HALF:
-                for t in range(PACK):
-                    square(sq_im, im[0, t], t, 0, c0, c1)
+            re[1, t] = bank(RE_BANK + t, "re1%d" % t)
+            for a in range(PASSES):
+                transform(re[1, t], ("co", a), t, 1)
         for t in range(PACK):
-            re[1, t] = bank(t, "re1%d" % t)
-            for a in range(2):
-                stage1(re[1, t], ("co", a), t, 1)
-        for t in range(PACK):
-            im[1, t] = bank(4 + t, "im1%d" % t)
-            for a in range(2):
-                stage1(im[1, t], ("si", a), t, 1)
-        for t in range(PACK):
-            square(sq_re, re[1, t], t, 1, HALF, J)
-        for c0, c1 in spans:
-            if c1 > HALF:
-                for t in range(PACK):
-                    square(sq_im, im[1, t], t, 1, c0, c1)
+            im[1, t] = bank(IM_BANK + t, "im1%d" % t)
+            for a in range(PASSES):
+                transform(im[1, t], ("si", a), t, 1)
+        square_half(1)
 
         power = [sb("power%d" % c, [P, WIDTHS[c], PACK], BF16) for c in range(chunks)]
         signed = [sb("signed%d" % c, [P, WIDTHS[c], PACK], BF16) for c in range(chunks)]
         h_codes = [sb("h_codes%d" % c, [P, WIDTHS[c]], U32) for c in range(chunks)]
         h_scales = [sb("h_scales%d" % c, [P, WIDTHS[c]], U8) for c in range(chunks)]
         result = [sb("result%d" % c, [P, 2, WIDTHS[c]], F32) for c in range(chunks)]
-        out_v = out.rearrange("(u p) j -> p u j", p=P)
+        out_rows = out.rearrange("(u p) j -> p u j", p=P)
 
         def add(c):
-            cols = slice(spans[c][0], spans[c][1])
             nc.vector.tensor_tensor(
-                power[c][:].rearrange("p (n i) t -> p n t i", i=4),
-                sq_re[:, :, cols].rearrange("p t (n i) -> p n t i", i=4),
-                sq_im[:, :, cols].rearrange("p t (n i) -> p n t i", i=4),
+                power[c][:].rearrange("p (n e) t -> p n t e", e=2),
+                sq_re[half_of[c]][:, :, in_half(c)].rearrange("p t (n e) -> p n t e", e=2),
+                sq_im[c][:].rearrange("p t (n e) -> p n t e", e=2),
                 ALU.add,
             )
 
@@ -220,24 +230,22 @@ def tile_list_meltab_norm_kernel(
             nc.vector.quantize_mx(
                 out=h_codes[c][:].bitcast(FP8X4),
                 scales=h_scales[c][:],
-                in_=signed[c][:].rearrange("p n t -> p (n t)"),
+                in_=signed[c][:].rearrange("p j t -> p (j t)"),
             )
-            last = c == chunks - 1
-            y = [bank(c % 4, "y%d" % c)]
-            y.append(bank((c + 1) % 4, "y_last") if last else y[0])
+            y = [bank(RE_BANK + 2 * (c % 2) + u, "y%d%d" % (c, u)) for u in range(2)]
             for u in range(2):
                 nc.tensor.matmul_mx(
-                    y[u][:, u * width : (u + 1) * width],
-                    lhsT=fbw[:].bitcast(U8)[:, 2 * P * u : 2 * P * (u + 1)].bitcast(FP4X4),
-                    lhsT_scale=fbs[:].bitcast(U8)[:, P * u : P * (u + 1)],
+                    y[u][:, :width],
+                    lhsT=fb_codes[:].bitcast(U8)[:, 2 * P * u : 2 * P * (u + 1)].bitcast(FP4X4),
+                    lhsT_scale=fb_plane[:].bitcast(U8)[:, P * u : P * (u + 1)],
                     rhs=h_codes[c][:].bitcast(FP8X4),
                     rhs_scale=h_scales[c][:],
                     start=True,
                     stop=True,
                 )
             for u in range(2):
-                acc = y[u][:, u * width : (u + 1) * width]
-                if last and u == 1:
+                acc = y[u][:, :width]
+                if c == chunks - 1 and u == 1:
                     nc.vector.tensor_scalar(
                         result[c][:, u, :], acc, rdev[:, u : u + 1], shift[:, u : u + 1], ALU.mult, ALU.add
                     )
@@ -245,14 +253,17 @@ def tile_list_meltab_norm_kernel(
                     nc.scalar.activation(
                         result[c][:, u, :], acc, ACT.Identity, bias=shift[:, u : u + 1], scale=rdev[:, u : u + 1]
                     )
-            nc.sync.dma_start(out_v[:, :, spans[c][0] : spans[c][1]], result[c][:])
+            nc.sync.dma_start(out_rows[:, :, spans[c][0] : spans[c][1]], result[c][:])
 
-        add(0)
-        for c in range(1, chunks):
-            add(c)
-            if c >= 2:
-                finish(c - 2)
-            sign(c - 1)
-        sign(chunks - 1)
-        finish(chunks - 2)
-        finish(chunks - 1)
+        last = chunks - 1
+        for first in range(0, last, 2):
+            add(first)
+            add(first + 1)
+            sign(first)
+            sign(first + 1)
+            finish(first)
+            if first + 2 == last:
+                add(last)
+            finish(first + 1)
+        sign(last)
+        finish(last)

@@ -21,10 +21,10 @@ PACK = 4
 K_PASS = P * PACK
 PASSES = K // K_PASS
 HALF = 512
-WIDTHS = (256, 256, 256, 128, 128)
-ON_SCALAR = {("co", 0): 4, ("co", 1): 4, ("si", 0): 2, ("si", 1): 0}
-PIECES = {("co", 0): 1, ("co", 1): 1, ("si", 0): 1, ("si", 1): 2}
-RE_BANK, IM_BANK = 0, 4
+WIDTHS = (128, 128, 256, 256, 128, 128)
+PAIRS_ON_SCALAR = {("co", 0): (1,), ("co", 1): (0,), ("si", 0): (), ("si", 1): ()}
+Y_BANKS = (0, 1, 6, 7, 2, 3, 4)
+WEIGHTS = (("co", 0), ("co", 1), ("si", 0), ("si", 1))
 
 
 def tile_list_meltab_norm_kernel(
@@ -35,35 +35,32 @@ def tile_list_meltab_norm_kernel(
         keep = ctx.enter_context(tc.tile_pool(name="keep", bufs=1))
         psum = ctx.enter_context(tc.psum_pool(name="psum", bufs=1))
 
-        def sb(name, shape, dtype):
-            return keep.tile(shape, dtype, name=name, align_bytes=64)
+        def sb(name, shape, dtype, tag=None):
+            return keep.tile(shape, dtype, name=name, tag=tag or name, align_bytes=64)
 
         def bank(b, name):
             return psum.tile([P, HALF], F32, name=name, tag="bank%d" % b)
 
-        raw = {}
-
-        def load_weight(key, w):
-            name, a = key
-            width = F // PIECES[key]
-            src = w[K_PASS * a : K_PASS * (a + 1), :].rearrange("(p i) f -> p i f", i=PACK)
-            for u in range(PIECES[key]):
-                raw[key, u] = sb("raw_%s%d%d" % (name, a, u), [P, PACK, width], F32)
-                nc.sync.dma_start(raw[key, u][:], src[:, :, u * width : (u + 1) * width])
-
-        tab_rows = sb("tab_rows", [P, T // 4], I32)
-        nc.vector.memset(tab_rows[:], 0)
-        load_weight(("co", 0), co)
         offsets = keep.tile([P, J // 16], U16, name="offsets")
         nc.sync.dma_start(offsets[:], offs)
-        gain = sb("gain", [P, PACK], F32)
-        nc.gpsimd.dma_start(gain[:], gn.rearrange("(p t) -> p t", t=PACK))
-        nc.sync.dma_start(tab_rows[0:P:4, :], tab_scales.bitcast(I32).rearrange("a q w -> (a q) w"))
         tab = sb("tab", [P, T], I32)
         nc.sync.dma_start(tab[:], tab_words[0].rearrange("p t b -> p (t b)").bitcast(I32))
-        load_weight(("co", 1), co)
-        load_weight(("si", 0), si)
-        load_weight(("si", 1), si)
+        tab_rows = sb("tab_rows", [P, T // 4], I32)
+        nc.vector.memset(tab_rows[:], 0)
+        nc.scalar.dma_start(tab_rows[0:P:4, :], tab_scales.bitcast(I32).rearrange("a q w -> (a q) w"))
+        gain = sb("gain", [P, PACK], F32)
+        nc.gpsimd.dma_start(gain[:], gn.rearrange("(p t) -> p t", t=PACK))
+        mean = sb("mean", [P, 2], F32)
+        rdev = sb("rdev", [P, 2], F32)
+        with nc.allow_non_contiguous_dma(reason="one value a partition"):
+            nc.gpsimd.dma_start(mean[:], mu.rearrange("(u p) -> p u", p=P))
+            nc.gpsimd.dma_start(rdev[:], isd.rearrange("(u p) -> p u", p=P))
+        raw = {}
+        for key in WEIGHTS:
+            name, a = key
+            w = co if name == "co" else si
+            raw[key] = sb("raw_%s%d" % key, [P, PACK, F], F32)
+            nc.sync.dma_start(raw[key][:], w[K_PASS * a : K_PASS * (a + 1), :].rearrange("(p i) f -> p i f", i=PACK))
 
         fb_codes = sb("fb_codes", [P, 2 * N // 4], I32)
         nc.sync.dma_start(fb_codes[:], fb_words[0].bitcast(I32))
@@ -72,11 +69,6 @@ def tile_list_meltab_norm_kernel(
         fb_rows = fb_scales[0].bitcast(I32).rearrange("(q r) w -> r q w", r=4)
         for r in range(4):
             nc.sync.dma_start(fb_plane[r:P:32, :], fb_rows[r])
-        mean = sb("mean", [P, 2], F32)
-        rdev = sb("rdev", [P, 2], F32)
-        with nc.allow_non_contiguous_dma(reason="one value a partition"):
-            nc.sync.dma_start(mean[:], mu.rearrange("(u p) -> p u", p=P))
-            nc.sync.dma_start(rdev[:], isd.rearrange("(u p) -> p u", p=P))
 
         planes = [sb("plane%d" % a, [P, J // 4], I32) for a in range(PASSES)]
         for plane in planes:
@@ -88,53 +80,50 @@ def tile_list_meltab_norm_kernel(
                 nc.scalar.dma_start(planes[a][r:P:32, :], picked_rows[64 * a + 4 * r : 64 * (a + 1) : 16, :])
 
         grouped, codes, scales = {}, {}, {}
-        for key in PIECES:
-            codes[key] = sb("codes_%s%d" % key, [P, F], U32)
-            scales[key] = sb("scales_%s%d" % key, [P, F], U8)
-            for u in range(PIECES[key]):
-                shape = [P, PACK, P // PIECES[key], PACK]
-                grouped[key, u] = sb("grouped_%s%d%d" % (key[0], key[1], u), shape, BF16)
+        for key in WEIGHTS:
+            for g in range(2):
+                names = (key[0], key[1], g)
+                grouped[key, g] = sb("grouped_%s%d%d" % names, [P, 2, P, PACK], BF16)
+                codes[key, g] = sb("codes_%s%d%d" % names, [P, 2 * P], U32)
+                scales[key, g] = sb("scales_%s%d%d" % names, [P, 2 * P], U8)
 
-        def cast(key, u):
-            src = raw[key, u][:].rearrange("p i (m t) -> p m i t", t=PACK)
-            dst = grouped[key, u][:].rearrange("p t m i -> p m i t")
-            split = ON_SCALAR[key]
-            if split > 0:
-                nc.scalar.copy(dst[:, :, :, :split], src[:, :, :, :split])
-            if split < PACK:
-                nc.vector.tensor_copy(dst[:, :, :, split:], src[:, :, :, split:])
+        def cast(key, g):
+            src = raw[key][:].rearrange("p i (m t) -> p m i t", t=PACK)[:, :, :, 2 * g : 2 * g + 2]
+            dst = grouped[key, g][:].rearrange("p t m i -> p m i t")
+            if g in PAIRS_ON_SCALAR[key]:
+                nc.scalar.copy(dst, src)
+            else:
+                nc.vector.tensor_copy(dst, src)
 
-        def quantise(key, u, t0, t1):
-            width = P // PIECES[key]
-            cols = slice(P * t0 + width * u, P * (t1 - 1) + width * (u + 1))
+        def quantise(key, g):
             nc.vector.quantize_mx(
-                out=codes[key][:, cols].bitcast(FP8X4),
-                scales=scales[key][:, cols],
-                in_=grouped[key, u][:, t0:t1, :, :].rearrange("p t m i -> p (t m i)"),
+                out=codes[key, g][:].bitcast(FP8X4),
+                scales=scales[key, g][:],
+                in_=grouped[key, g][:].rearrange("p t m i -> p (t m i)"),
             )
 
-        picked = {}
-        parted = [sb("parted%d" % h, [P, PASSES, HALF], U16) for h in range(2)]
+        picked, parted = {}, {}
 
         def gather(h):
+            picked[h] = sb("picked%d" % h, [P, HALF], U32, "grouped_co00" if h else None)
             cols = slice(h * HALF // 16, (h + 1) * HALF // 16)
-            picked[h] = sb("picked", [P, HALF], U32)
             nc.vector.tensor_copy(picked[h][:], tab[:].bitcast(U32).indirect(offsets[:, cols]))
 
         def part(h):
+            parted[h] = sb("parted%d" % h, [P, PASSES, HALF], U16, "grouped_co11" if h else None)
             nc.vector.tensor_copy(parted[h][:], picked[h][:].bitcast(U16).rearrange("p (j a) -> p a j", a=PASSES))
 
-        def transform(acc, key, t, h):
+        def transform(acc, key, t, h, first):
             a = key[1]
-            cols = slice(P * t, P * (t + 1))
+            cols = slice(P * (t % 2), P * (t % 2 + 1))
             nc.tensor.matmul_mx(
                 acc[:],
-                lhsT=codes[key][:, cols].bitcast(FP8X4),
-                lhsT_scale=scales[key][:, cols],
+                lhsT=codes[key, t // 2][:, cols].bitcast(FP8X4),
+                lhsT_scale=scales[key, t // 2][:, cols],
                 rhs=parted[h][:, a, :].bitcast(FP4X4),
                 rhs_scale=planes[a][:].bitcast(U8)[:, h * HALF : (h + 1) * HALF],
-                start=(a == 0),
-                stop=(a == PASSES - 1),
+                start=first,
+                stop=not first,
             )
 
         chunks = len(WIDTHS)
@@ -146,65 +135,92 @@ def tile_list_meltab_norm_kernel(
         def in_half(c):
             return slice(spans[c][0] % HALF, spans[c][0] % HALF + WIDTHS[c])
 
-        step = sb("step", [P, PACK], F32)
         sgn = sb("sgn", [P, PACK], BF16)
         mag = sb("mag", [P, PACK], F32)
         exponent = sb("exponent", [P, PACK], F32)
         root = sb("root", [P, PACK], F32)
         nc.gpsimd.memset(exponent[:], 0.5)
-        nc.gpsimd.tensor_scalar(step[:], gain[:], 0.0, 2.0, ALU.is_ge, ALU.mult)
-        nc.gpsimd.tensor_scalar(sgn[:], step[:], -1.0, None, ALU.add)
-        nc.gpsimd.tensor_tensor(mag[:], gain[:], sgn[:], ALU.mult)
+        nc.scalar.activation(mag[:], gain[:], ACT.Abs)
+        nc.scalar.activation(sgn[:], gain[:], ACT.Sign)
         nc.gpsimd.tensor_tensor(root[:], mag[:], exponent[:], ALU.pow)
-        cast(("co", 0), 0)
+        centre = sb("centre", [P, 2], F32)
+        shift = sb("shift", [P, 2], F32)
+        nc.gpsimd.tensor_tensor(centre[:], mean[:], rdev[:], ALU.mult)
+        nc.gpsimd.tensor_scalar(shift[:], centre[:], -1.0, 0.0, ALU.mult, ALU.add)
 
         def square(dst, acc, t):
             nc.scalar.activation(dst, acc, ACT.Square, scale=root[:, t : t + 1])
 
-        def square_half(h):
-            for t in range(PACK):
-                square(sq_re[h][:, t, :], re[h, t][:], t)
-            for c in range(chunks):
-                if half_of[c] == h:
-                    for t in range(PACK):
-                        square(sq_im[c][:, t, :], im[h, t][:, in_half(c)], t)
+        acc = {}
 
-        quantise(("co", 0), 0, 0, PACK)
+        def prepare(key):
+            for g in range(2):
+                cast(key, g)
+
+        def open_sum(name, h, t, b, a):
+            acc[name, h, t] = bank(b, "%s%d%d" % (name, h, t))
+            transform(acc[name, h, t], (name, a), t, h, True)
+
+        def close_sum(name, h, t, a):
+            transform(acc[name, h, t], (name, a), t, h, False)
+
+        def square_re(h, t):
+            square(sq_re[h][:, t, :], acc["co", h, t][:], t)
+
+        def square_im(c):
+            for t in range(PACK):
+                square(sq_im[c][:, t, :], acc["si", half_of[c], t][:, in_half(c)], t)
+
         gather(0)
         part(0)
-        re = {(0, t): bank(RE_BANK + t, "re0%d" % t) for t in range(PACK)}
-        for t in range(PACK):
-            transform(re[0, t], ("co", 0), t, 0)
+        prepare(("co", 0))
+        for g in range(2):
+            quantise(("co", 0), g)
+            for t in (2 * g, 2 * g + 1):
+                open_sum("co", 0, t, t, 0)
         gather(1)
-        cast(("co", 1), 0)
-        for t in range(PACK):
-            quantise(("co", 1), 0, t, t + 1)
-            transform(re[0, t], ("co", 1), t, 0)
-        cast(("si", 0), 0)
-        quantise(("si", 0), 0, 0, PACK)
-        im = {(0, t): bank(IM_BANK + t, "im0%d" % t) for t in range(PACK)}
-        for t in range(PACK):
-            transform(im[0, t], ("si", 0), t, 0)
-        cast(("si", 1), 0)
-        cast(("si", 1), 1)
-        for t in range(PACK):
-            quantise(("si", 1), 0, t, t + 1)
-            quantise(("si", 1), 1, t, t + 1)
-            transform(im[0, t], ("si", 1), t, 0)
+        prepare(("co", 1))
+        for g in range(2):
+            quantise(("co", 1), g)
+            for t in (2 * g, 2 * g + 1):
+                close_sum("co", 0, t, 1)
         part(1)
-        shift = sb("shift", [P, 2], F32)
-        nc.vector.scalar_tensor_tensor(shift[:], mean[:], -1.0, rdev[:], ALU.mult, ALU.mult)
-        square_half(0)
-
+        for t in range(2):
+            open_sum("co", 1, t, 4 + t, 0)
+            close_sum("co", 1, t, 1)
         for t in range(PACK):
-            re[1, t] = bank(RE_BANK + t, "re1%d" % t)
-            for a in range(PASSES):
-                transform(re[1, t], ("co", a), t, 1)
-        for t in range(PACK):
-            im[1, t] = bank(IM_BANK + t, "im1%d" % t)
-            for a in range(PASSES):
-                transform(im[1, t], ("si", a), t, 1)
-        square_half(1)
+            square_re(0, t)
+        for t in range(2):
+            square_re(1, t)
+        prepare(("si", 0))
+        for g in range(2):
+            quantise(("si", 0), g)
+            for t in (2 * g, 2 * g + 1):
+                open_sum("si", 0, t, (6 + t) % 8, 0)
+        for t in range(2):
+            open_sum("si", 1, t, 2 + t, 0)
+        prepare(("si", 1))
+        for g in range(2):
+            quantise(("si", 1), g)
+            for t in (2 * g, 2 * g + 1):
+                close_sum("si", 0, t, 1)
+        for t in range(2):
+            close_sum("si", 1, t, 1)
+        for t in range(2, PACK):
+            open_sum("si", 1, t, 2 + t, 1)
+            close_sum("si", 1, t, 0)
+        first_half = [c for c in range(chunks) if half_of[c] == 0]
+        second_half = [c for c in range(chunks) if half_of[c] == 1]
+        for c in first_half:
+            square_im(c)
+        for t in range(2, PACK):
+            open_sum("co", 1, t, 4 + t, 0)
+            close_sum("co", 1, t, 1)
+        square_im(second_half[0])
+        for t in range(2, PACK):
+            square_re(1, t)
+        for c in second_half[1:]:
+            square_im(c)
 
         power = [sb("power%d" % c, [P, WIDTHS[c], PACK], BF16) for c in range(chunks)]
         signed = [sb("signed%d" % c, [P, WIDTHS[c], PACK], BF16) for c in range(chunks)]
@@ -225,17 +241,21 @@ def tile_list_meltab_norm_kernel(
             signs = sgn[:].unsqueeze(1).to_broadcast([P, WIDTHS[c], PACK])
             nc.vector.tensor_tensor(signed[c][:], power[c][:], signs, ALU.mult)
 
-        def finish(c):
-            width = WIDTHS[c]
+        def quantise_h(c):
             nc.vector.quantize_mx(
                 out=h_codes[c][:].bitcast(FP8X4),
                 scales=h_scales[c][:],
                 in_=signed[c][:].rearrange("p j t -> p (j t)"),
             )
-            y = [bank(RE_BANK + 2 * (c % 2) + u, "y%d%d" % (c, u)) for u in range(2)]
+
+        def finish(c):
+            width = WIDTHS[c]
+            first = bank(Y_BANKS[c], "y%d" % c)
+            second = bank(Y_BANKS[c + 1], "y_last") if c == chunks - 1 else first
+            y = [first[:, :width], second[:, width : 2 * width]]
             for u in range(2):
                 nc.tensor.matmul_mx(
-                    y[u][:, :width],
+                    y[u],
                     lhsT=fb_codes[:].bitcast(U8)[:, 2 * P * u : 2 * P * (u + 1)].bitcast(FP4X4),
                     lhsT_scale=fb_plane[:].bitcast(U8)[:, P * u : P * (u + 1)],
                     rhs=h_codes[c][:].bitcast(FP8X4),
@@ -244,7 +264,7 @@ def tile_list_meltab_norm_kernel(
                     stop=True,
                 )
             for u in range(2):
-                acc = y[u][:, :width]
+                acc = y[u]
                 if c == chunks - 1 and u == 1:
                     nc.vector.tensor_scalar(
                         result[c][:, u, :], acc, rdev[:, u : u + 1], shift[:, u : u + 1], ALU.mult, ALU.add
@@ -255,15 +275,11 @@ def tile_list_meltab_norm_kernel(
                     )
             nc.sync.dma_start(out_rows[:, :, spans[c][0] : spans[c][1]], result[c][:])
 
-        last = chunks - 1
-        for first in range(0, last, 2):
-            add(first)
-            add(first + 1)
-            sign(first)
-            sign(first + 1)
-            finish(first)
-            if first + 2 == last:
-                add(last)
-            finish(first + 1)
-        sign(last)
-        finish(last)
+        for step in range(chunks + 2):
+            if step < chunks:
+                add(step)
+            if 1 <= step <= chunks:
+                sign(step - 1)
+            if step >= 2:
+                quantise_h(step - 2)
+                finish(step - 2)

@@ -44,23 +44,35 @@ def tile_list_meltab_norm_kernel(
         offsets = keep.tile([P, J // 16], U16, name="offsets")
         nc.sync.dma_start(offsets[:], offs)
         tab = sb("tab", [P, T], I32)
-        nc.sync.dma_start(tab[:], tab_words[0].rearrange("p t b -> p (t b)").bitcast(I32))
-        tab_rows = sb("tab_rows", [P, T // 4], I32)
-        nc.vector.memset(tab_rows[:], 0)
-        nc.scalar.dma_start(tab_rows[0:P:4, :], tab_scales.bitcast(I32).rearrange("a q w -> (a q) w"))
+        tab_src = tab_words[0].rearrange("p t b -> p (t b)").bitcast(I32)
+        nc.sync.dma_start(tab[:, : T // 4], tab_src[:, : T // 4])
         gain = sb("gain", [P, PACK], F32)
-        nc.gpsimd.dma_start(gain[:], gn.rearrange("(p t) -> p t", t=PACK))
-        mean = sb("mean", [P, 2], F32)
-        rdev = sb("rdev", [P, 2], F32)
-        with nc.allow_non_contiguous_dma(reason="one value a partition"):
-            nc.gpsimd.dma_start(mean[:], mu.rearrange("(u p) -> p u", p=P))
-            nc.gpsimd.dma_start(rdev[:], isd.rearrange("(u p) -> p u", p=P))
+        nc.sync.dma_start(gain[:], gn.rearrange("(p t) -> p t", t=PACK))
+        tab_rows = sb("tab_rows", [P, T // 4], I32)
+        nc.vector.memset(tab_rows[:, : T // 8], 0)
+        nc.gpsimd.memset(tab_rows[:, T // 8 :], 0)
+        nc.sync.dma_start(tab_rows[0:P:4, :], tab_scales.bitcast(I32).rearrange("a q w -> (a q) w"))
+        nc.sync.dma_start(tab[:, T // 4 :], tab_src[:, T // 4 :])
+
         raw = {}
-        for key in WEIGHTS:
+
+        def load_weight(key):
             name, a = key
             w = co if name == "co" else si
             raw[key] = sb("raw_%s%d" % key, [P, PACK, F], F32)
             nc.sync.dma_start(raw[key][:], w[K_PASS * a : K_PASS * (a + 1), :].rearrange("(p i) f -> p i f", i=PACK))
+
+        planes = [sb("plane%d" % a, [P, J // 4], I32) for a in range(PASSES)]
+        for plane in planes:
+            nc.vector.memset(plane[:], 0)
+        picked_rows = sb("picked_rows", [P, J // 4], I32)
+        nc.vector.tensor_copy(picked_rows[:].bitcast(U8), tab_rows[:].bitcast(U8).indirect(offsets[:]))
+        for a in range(PASSES):
+            load_weight(("co", a))
+            for r in range(4):
+                nc.sync.dma_start(planes[a][r:P:32, :], picked_rows[64 * a + 4 * r : 64 * (a + 1) : 16, :])
+        for a in range(PASSES):
+            load_weight(("si", a))
 
         fb_codes = sb("fb_codes", [P, 2 * N // 4], I32)
         nc.sync.dma_start(fb_codes[:], fb_words[0].bitcast(I32))
@@ -69,15 +81,11 @@ def tile_list_meltab_norm_kernel(
         fb_rows = fb_scales[0].bitcast(I32).rearrange("(q r) w -> r q w", r=4)
         for r in range(4):
             nc.sync.dma_start(fb_plane[r:P:32, :], fb_rows[r])
-
-        planes = [sb("plane%d" % a, [P, J // 4], I32) for a in range(PASSES)]
-        for plane in planes:
-            nc.vector.memset(plane[:], 0)
-        picked_rows = sb("picked_rows", [P, J // 4], I32)
-        nc.vector.tensor_copy(picked_rows[:].bitcast(U8), tab_rows[:].bitcast(U8).indirect(offsets[:]))
-        for a in range(PASSES):
-            for r in range(4):
-                nc.scalar.dma_start(planes[a][r:P:32, :], picked_rows[64 * a + 4 * r : 64 * (a + 1) : 16, :])
+        mean = sb("mean", [P, 2], F32)
+        rdev = sb("rdev", [P, 2], F32)
+        with nc.allow_non_contiguous_dma(reason="one value a partition"):
+            nc.sync.dma_start(mean[:], mu.rearrange("(u p) -> p u", p=P))
+            nc.sync.dma_start(rdev[:], isd.rearrange("(u p) -> p u", p=P))
 
         grouped, codes, scales = {}, {}, {}
         for key in WEIGHTS:

@@ -24,6 +24,7 @@ HALF = 512
 WIDTHS = (128, 128, 256, 256, 128, 128)
 PAIRS_ON_SCALAR = {("co", 0): (1,), ("co", 1): (0,), ("si", 0): (), ("si", 1): ()}
 Y_BANKS = (0, 1, 6, 7, 2, 3, 4)
+HEAD = 768
 WEIGHTS = (("co", 0), ("co", 1), ("si", 0), ("si", 1))
 
 
@@ -45,14 +46,14 @@ def tile_list_meltab_norm_kernel(
         nc.sync.dma_start(offsets[:], offs)
         tab = sb("tab", [P, T], I32)
         tab_src = tab_words[0].rearrange("p t b -> p (t b)").bitcast(I32)
-        nc.sync.dma_start(tab[:, : T // 4], tab_src[:, : T // 4])
+        nc.sync.dma_start(tab[:, :HEAD], tab_src[:, :HEAD])
         gain = sb("gain", [P, PACK], F32)
         nc.sync.dma_start(gain[:], gn.rearrange("(p t) -> p t", t=PACK))
         tab_rows = sb("tab_rows", [P, T // 4], I32)
         nc.vector.memset(tab_rows[:, : T // 8], 0)
         nc.gpsimd.memset(tab_rows[:, T // 8 :], 0)
         nc.sync.dma_start(tab_rows[0:P:4, :], tab_scales.bitcast(I32).rearrange("a q w -> (a q) w"))
-        nc.sync.dma_start(tab[:, T // 4 :], tab_src[:, T // 4 :])
+        nc.sync.dma_start(tab[:, HEAD:], tab_src[:, HEAD:])
 
         raw = {}
 
@@ -146,15 +147,13 @@ def tile_list_meltab_norm_kernel(
         sgn = sb("sgn", [P, PACK], BF16)
         mag = sb("mag", [P, PACK], F32)
         exponent = sb("exponent", [P, PACK], F32)
-        root = sb("root", [P, PACK], F32)
+        root = sb("root", [P, PACK], F32, "tab_rows")
         nc.gpsimd.memset(exponent[:], 0.5)
         nc.scalar.activation(mag[:], gain[:], ACT.Abs)
         nc.scalar.activation(sgn[:], gain[:], ACT.Sign)
         nc.gpsimd.tensor_tensor(root[:], mag[:], exponent[:], ALU.pow)
-        centre = sb("centre", [P, 2], F32)
         shift = sb("shift", [P, 2], F32)
-        nc.gpsimd.tensor_tensor(centre[:], mean[:], rdev[:], ALU.mult)
-        nc.gpsimd.tensor_scalar(shift[:], centre[:], -1.0, 0.0, ALU.mult, ALU.add)
+        nc.vector.scalar_tensor_tensor(shift[:], mean[:], -1.0, rdev[:], ALU.mult, ALU.mult)
 
         def square(dst, acc, t):
             nc.scalar.activation(dst, acc, ACT.Square, scale=root[:, t : t + 1])

@@ -22,7 +22,7 @@ K_PASS = P * PACK
 PASSES = K // K_PASS
 HALF = 512
 WIDTHS = (128, 128, 256, 256, 128, 128)
-PAIRS_ON_SCALAR = {("co", 0): (1,), ("co", 1): (0,), ("si", 0): (), ("si", 1): ()}
+ON_SCALAR = {("co", 0): 128, ("co", 1): 44, ("si", 0): 44, ("si", 1): 0}
 Y_BANKS = (0, 1, 6, 7, 2, 3, 4)
 HEAD = 768
 WEIGHTS = (("co", 0), ("co", 1), ("si", 0), ("si", 1))
@@ -34,6 +34,7 @@ def tile_list_meltab_norm_kernel(
     nc = tc.nc
     with ExitStack() as ctx:
         keep = ctx.enter_context(tc.tile_pool(name="keep", bufs=1))
+        laid = ctx.enter_context(tc.tile_pool(name="laid", bufs=1))
         psum = ctx.enter_context(tc.psum_pool(name="psum", bufs=1))
 
         def sb(name, shape, dtype, tag=None):
@@ -60,8 +61,11 @@ def tile_list_meltab_norm_kernel(
         def load_weight(key):
             name, a = key
             w = co if name == "co" else si
-            raw[key] = sb("raw_%s%d" % key, [P, PACK, F], F32)
-            nc.sync.dma_start(raw[key][:], w[K_PASS * a : K_PASS * (a + 1), :].rearrange("(p i) f -> p i f", i=PACK))
+            if key == ("si", 0):
+                raw[key] = laid.tile([P, PACK, F], F32, name="raw_si0", offset=2 * PACK * HALF)[:]
+            else:
+                raw[key] = sb("raw_%s%d" % key, [P, PACK, F], F32)[:]
+            nc.sync.dma_start(raw[key], w[K_PASS * a : K_PASS * (a + 1), :].rearrange("(p i) f -> p i f", i=PACK))
 
         planes = [sb("plane%d" % a, [P, J // 4], I32) for a in range(PASSES)]
         for plane in planes:
@@ -90,36 +94,40 @@ def tile_list_meltab_norm_kernel(
 
         grouped, codes, scales = {}, {}, {}
         for key in WEIGHTS:
+            grouped[key] = sb("grouped_%s%d" % key, [P, PACK, P, PACK], BF16)
             for g in range(2):
-                names = (key[0], key[1], g)
-                grouped[key, g] = sb("grouped_%s%d%d" % names, [P, 2, P, PACK], BF16)
-                codes[key, g] = sb("codes_%s%d%d" % names, [P, 2 * P], U32)
-                scales[key, g] = sb("scales_%s%d%d" % names, [P, 2 * P], U8)
+                codes[key, g] = sb("codes_%s%d%d" % (key[0], key[1], g), [P, 2 * P], U32)
+                scales[key, g] = sb("scales_%s%d%d" % (key[0], key[1], g), [P, 2 * P], U8)
 
-        def cast(key, g):
-            src = raw[key][:].rearrange("p i (m t) -> p m i t", t=PACK)[:, :, :, 2 * g : 2 * g + 2]
-            dst = grouped[key, g][:].rearrange("p t m i -> p m i t")
-            if g in PAIRS_ON_SCALAR[key]:
-                nc.scalar.copy(dst, src)
-            else:
-                nc.vector.tensor_copy(dst, src)
+        def cast(key):
+            src = raw[key].rearrange("p i (m t) -> p m t i", t=PACK)
+            dst = grouped[key][:].rearrange("p t m i -> p m t i")
+            split = ON_SCALAR[key]
+            if split == P:
+                for t in (0, 2):
+                    nc.scalar.copy(dst[:, :, t : t + 2], src[:, :, t : t + 2])
+                return
+            if split > 0:
+                nc.scalar.copy(dst[:, :split], src[:, :split])
+            nc.vector.tensor_copy(dst[:, split:], src[:, split:])
 
-        def quantise(key, g):
+        def quantise(key, t0, t1):
+            cols = slice(P * (t0 % 2), P * (t0 % 2 + t1 - t0))
             nc.vector.quantize_mx(
-                out=codes[key, g][:].bitcast(FP8X4),
-                scales=scales[key, g][:],
-                in_=grouped[key, g][:].rearrange("p t m i -> p (t m i)"),
+                out=codes[key, t0 // 2][:, cols].bitcast(FP8X4),
+                scales=scales[key, t0 // 2][:, cols],
+                in_=grouped[key][:, t0:t1].rearrange("p t m i -> p (t m i)"),
             )
 
         picked, parted = {}, {}
 
         def gather(h):
-            picked[h] = sb("picked%d" % h, [P, HALF], U32, "grouped_co00" if h else None)
+            picked[h] = sb("picked%d" % h, [P, HALF], U32, None)
             cols = slice(h * HALF // 16, (h + 1) * HALF // 16)
             nc.vector.tensor_copy(picked[h][:], tab[:].bitcast(U32).indirect(offsets[:, cols]))
 
         def part(h):
-            parted[h] = sb("parted%d" % h, [P, PASSES, HALF], U16, "grouped_co11" if h else None)
+            parted[h] = sb("parted%d" % h, [P, PASSES, HALF], U16, None)
             nc.vector.tensor_copy(parted[h][:], picked[h][:].bitcast(U16).rearrange("p (j a) -> p a j", a=PASSES))
 
         def transform(acc, key, t, h, first):
@@ -138,7 +146,7 @@ def tile_list_meltab_norm_kernel(
         chunks = len(WIDTHS)
         spans = [(sum(WIDTHS[:c]), sum(WIDTHS[: c + 1])) for c in range(chunks)]
         half_of = [j0 // HALF for j0, j1 in spans]
-        sq_re = [sb("sq_re%d" % h, [P, PACK, HALF], F32) for h in range(2)]
+        sq_re = [laid.tile([P, PACK, HALF], F32, name="sq_re%d" % h, offset=4 * PACK * HALF * h) for h in range(2)]
         sq_im = [sb("sq_im%d" % c, [P, PACK, WIDTHS[c]], F32) for c in range(chunks)]
 
         def in_half(c):
@@ -160,10 +168,6 @@ def tile_list_meltab_norm_kernel(
 
         acc = {}
 
-        def prepare(key):
-            for g in range(2):
-                cast(key, g)
-
         def open_sum(name, h, t, b, a):
             acc[name, h, t] = bank(b, "%s%d%d" % (name, h, t))
             transform(acc[name, h, t], (name, a), t, h, True)
@@ -178,39 +182,38 @@ def tile_list_meltab_norm_kernel(
             for t in range(PACK):
                 square(sq_im[c][:, t, :], acc["si", half_of[c], t][:, in_half(c)], t)
 
-        gather(0)
-        part(0)
-        prepare(("co", 0))
+        for h in range(2):
+            gather(h)
+        for h in range(2):
+            part(h)
+        cast(("co", 0))
         for g in range(2):
-            quantise(("co", 0), g)
+            quantise(("co", 0), 2 * g, 2 * g + 2)
             for t in (2 * g, 2 * g + 1):
                 open_sum("co", 0, t, t, 0)
-        gather(1)
-        prepare(("co", 1))
+        cast(("co", 1))
         for g in range(2):
-            quantise(("co", 1), g)
+            quantise(("co", 1), 2 * g, 2 * g + 2)
             for t in (2 * g, 2 * g + 1):
                 close_sum("co", 0, t, 1)
-        part(1)
         for t in range(2):
             open_sum("co", 1, t, 4 + t, 0)
             close_sum("co", 1, t, 1)
+        cast(("si", 0))
         for t in range(PACK):
             square_re(0, t)
         for t in range(2):
             square_re(1, t)
-        prepare(("si", 0))
         for g in range(2):
-            quantise(("si", 0), g)
+            quantise(("si", 0), 2 * g, 2 * g + 2)
             for t in (2 * g, 2 * g + 1):
                 open_sum("si", 0, t, (6 + t) % 8, 0)
         for t in range(2):
             open_sum("si", 1, t, 2 + t, 0)
-        prepare(("si", 1))
-        for g in range(2):
-            quantise(("si", 1), g)
-            for t in (2 * g, 2 * g + 1):
-                close_sum("si", 0, t, 1)
+        cast(("si", 1))
+        for t in range(PACK):
+            quantise(("si", 1), t, t + 1)
+            close_sum("si", 0, t, 1)
         for t in range(2):
             close_sum("si", 1, t, 1)
         for t in range(2, PACK):

@@ -22,10 +22,12 @@ K_PASS = P * PACK
 PASSES = K // K_PASS
 HALF = 512
 WIDTHS = (128, 128, 256, 256, 128, 128)
-ON_SCALAR = {("co", 0): 128, ("co", 1): 44, ("si", 0): 44, ("si", 1): 0}
-Y_BANKS = (0, 1, 6, 7, 2, 3, 4)
+ON_SCALAR = {("co", 0): 76, ("co", 1): 64, ("si", 0): 56, ("si", 1): 0}
+WEIGHTS = tuple(ON_SCALAR)
 HEAD = 768
-WEIGHTS = (("co", 0), ("co", 1), ("si", 0), ("si", 1))
+BANKS = {("co", 0): (0, 1, 2, 3), ("co", 1): (4, 5, 6, 7), ("si", 0): (6, 7, 0, 1), ("si", 1): (2, 3, 4, 5)}
+EARLY = 2
+Y_BANKS = (0, 1, 6, 7, 2, 3, 4)
 
 
 def tile_list_meltab_norm_kernel(
@@ -100,16 +102,13 @@ def tile_list_meltab_norm_kernel(
                 scales[key, g] = sb("scales_%s%d%d" % (key[0], key[1], g), [P, 2 * P], U8)
 
         def cast(key):
-            src = raw[key].rearrange("p i (m t) -> p m t i", t=PACK)
-            dst = grouped[key][:].rearrange("p t m i -> p m t i")
+            src = raw[key].rearrange("p i (m t) -> p m i t", t=PACK)
+            dst = grouped[key][:].rearrange("p t m i -> p m i t")
             split = ON_SCALAR[key]
-            if split == P:
-                for t in (0, 2):
-                    nc.scalar.copy(dst[:, :, t : t + 2], src[:, :, t : t + 2])
-                return
             if split > 0:
                 nc.scalar.copy(dst[:, :split], src[:, :split])
-            nc.vector.tensor_copy(dst[:, split:], src[:, split:])
+            for t in (0, 2):
+                nc.vector.tensor_copy(dst[:, split:, :, t : t + 2], src[:, split:, :, t : t + 2])
 
         def quantise(key, t0, t1):
             cols = slice(P * (t0 % 2), P * (t0 % 2 + t1 - t0))
@@ -122,19 +121,19 @@ def tile_list_meltab_norm_kernel(
         picked, parted = {}, {}
 
         def gather(h):
-            picked[h] = sb("picked%d" % h, [P, HALF], U32, None)
+            picked[h] = sb("picked%d" % h, [P, HALF], U32)
             cols = slice(h * HALF // 16, (h + 1) * HALF // 16)
             nc.vector.tensor_copy(picked[h][:], tab[:].bitcast(U32).indirect(offsets[:, cols]))
 
         def part(h):
-            parted[h] = sb("parted%d" % h, [P, PASSES, HALF], U16, None)
+            parted[h] = sb("parted%d" % h, [P, PASSES, HALF], U16, "grouped_co0" if h else None)
             nc.vector.tensor_copy(parted[h][:], picked[h][:].bitcast(U16).rearrange("p (j a) -> p a j", a=PASSES))
 
-        def transform(acc, key, t, h, first):
+        def transform(dst, key, t, h, first):
             a = key[1]
             cols = slice(P * (t % 2), P * (t % 2 + 1))
             nc.tensor.matmul_mx(
-                acc[:],
+                dst[:],
                 lhsT=codes[key, t // 2][:, cols].bitcast(FP8X4),
                 lhsT_scale=scales[key, t // 2][:, cols],
                 rhs=parted[h][:, a, :].bitcast(FP4X4),
@@ -163,13 +162,13 @@ def tile_list_meltab_norm_kernel(
         shift = sb("shift", [P, 2], F32)
         nc.vector.scalar_tensor_tensor(shift[:], mean[:], -1.0, rdev[:], ALU.mult, ALU.mult)
 
-        def square(dst, acc, t):
-            nc.scalar.activation(dst, acc, ACT.Square, scale=root[:, t : t + 1])
+        def square(dst, src, t):
+            nc.scalar.activation(dst, src, ACT.Square, scale=root[:, t : t + 1])
 
         acc = {}
 
-        def open_sum(name, h, t, b, a):
-            acc[name, h, t] = bank(b, "%s%d%d" % (name, h, t))
+        def open_sum(name, h, t, a):
+            acc[name, h, t] = bank(BANKS[name, h][t], "%s%d%d" % (name, h, t))
             transform(acc[name, h, t], (name, a), t, h, True)
 
         def close_sum(name, h, t, a):
@@ -184,50 +183,51 @@ def tile_list_meltab_norm_kernel(
 
         for h in range(2):
             gather(h)
-        for h in range(2):
-            part(h)
+        part(0)
         cast(("co", 0))
         for g in range(2):
             quantise(("co", 0), 2 * g, 2 * g + 2)
             for t in (2 * g, 2 * g + 1):
-                open_sum("co", 0, t, t, 0)
+                open_sum("co", 0, t, 0)
+        part(1)
         cast(("co", 1))
         for g in range(2):
             quantise(("co", 1), 2 * g, 2 * g + 2)
             for t in (2 * g, 2 * g + 1):
                 close_sum("co", 0, t, 1)
-        for t in range(2):
-            open_sum("co", 1, t, 4 + t, 0)
+        for t in range(EARLY):
+            open_sum("co", 1, t, 0)
             close_sum("co", 1, t, 1)
+
         cast(("si", 0))
         for t in range(PACK):
             square_re(0, t)
-        for t in range(2):
+        for t in range(EARLY):
             square_re(1, t)
         for g in range(2):
             quantise(("si", 0), 2 * g, 2 * g + 2)
             for t in (2 * g, 2 * g + 1):
-                open_sum("si", 0, t, (6 + t) % 8, 0)
-        for t in range(2):
-            open_sum("si", 1, t, 2 + t, 0)
+                open_sum("si", 0, t, 0)
+        for t in range(EARLY):
+            open_sum("si", 1, t, 0)
         cast(("si", 1))
         for t in range(PACK):
             quantise(("si", 1), t, t + 1)
             close_sum("si", 0, t, 1)
-        for t in range(2):
+        for t in range(EARLY):
             close_sum("si", 1, t, 1)
-        for t in range(2, PACK):
-            open_sum("si", 1, t, 2 + t, 1)
+        for t in range(EARLY, PACK):
+            open_sum("si", 1, t, 1)
             close_sum("si", 1, t, 0)
         first_half = [c for c in range(chunks) if half_of[c] == 0]
         second_half = [c for c in range(chunks) if half_of[c] == 1]
         for c in first_half:
             square_im(c)
-        for t in range(2, PACK):
-            open_sum("co", 1, t, 4 + t, 0)
+        for t in range(EARLY, PACK):
+            open_sum("co", 1, t, 0)
             close_sum("co", 1, t, 1)
         square_im(second_half[0])
-        for t in range(2, PACK):
+        for t in range(EARLY, PACK):
             square_re(1, t)
         for c in second_half[1:]:
             square_im(c)
@@ -274,14 +274,13 @@ def tile_list_meltab_norm_kernel(
                     stop=True,
                 )
             for u in range(2):
-                acc = y[u]
                 if c == chunks - 1 and u == 1:
                     nc.vector.tensor_scalar(
-                        result[c][:, u, :], acc, rdev[:, u : u + 1], shift[:, u : u + 1], ALU.mult, ALU.add
+                        result[c][:, u, :], y[u], rdev[:, u : u + 1], shift[:, u : u + 1], ALU.mult, ALU.add
                     )
                 else:
                     nc.scalar.activation(
-                        result[c][:, u, :], acc, ACT.Identity, bias=shift[:, u : u + 1], scale=rdev[:, u : u + 1]
+                        result[c][:, u, :], y[u], ACT.Identity, bias=shift[:, u : u + 1], scale=rdev[:, u : u + 1]
                     )
             nc.sync.dma_start(out_rows[:, :, spans[c][0] : spans[c][1]], result[c][:])
 

@@ -22,7 +22,8 @@ K_PASS = P * PACK
 PASSES = K // K_PASS
 HALF = 512
 WIDTHS = (128, 128, 256, 256, 128, 128)
-ON_SCALAR = {("co", 0): 76, ("co", 1): 64, ("si", 0): 56, ("si", 1): 0}
+QUARTER = 256
+ON_SCALAR = {("co", 0): 76, ("co", 1): 44, ("si", 0): 0, ("si", 1): 44}
 WEIGHTS = tuple(ON_SCALAR)
 HEAD = 768
 BANKS = {("co", 0): (0, 1, 2, 3), ("co", 1): (4, 5, 6, 7), ("si", 0): (6, 7, 0, 1), ("si", 1): (2, 3, 4, 5)}
@@ -55,7 +56,7 @@ def tile_list_meltab_norm_kernel(
         tab_rows = sb("tab_rows", [P, T // 4], I32)
         nc.vector.memset(tab_rows[:, : T // 8], 0)
         nc.gpsimd.memset(tab_rows[:, T // 8 :], 0)
-        nc.sync.dma_start(tab_rows[0:P:4, :], tab_scales.bitcast(I32).rearrange("a q w -> (a q) w"))
+        nc.sync.dma_start(tab_rows[0:P:4, :], tab_scales.bitcast(I32).rearrange("a q w -> q a w"))
         nc.sync.dma_start(tab[:, HEAD:], tab_src[:, HEAD:])
 
         raw = {}
@@ -63,23 +64,21 @@ def tile_list_meltab_norm_kernel(
         def load_weight(key):
             name, a = key
             w = co if name == "co" else si
-            if key == ("si", 0):
-                raw[key] = laid.tile([P, PACK, F], F32, name="raw_si0", offset=2 * PACK * HALF)[:]
+            if key == ("si", 1):
+                raw[key] = laid.tile([P, PACK, F], F32, name="raw_si1", offset=4 * PACK * HALF)[:]
             else:
                 raw[key] = sb("raw_%s%d" % key, [P, PACK, F], F32)[:]
             nc.sync.dma_start(raw[key], w[K_PASS * a : K_PASS * (a + 1), :].rearrange("(p i) f -> p i f", i=PACK))
 
-        planes = [sb("plane%d" % a, [P, J // 4], I32) for a in range(PASSES)]
-        for plane in planes:
-            nc.vector.memset(plane[:], 0)
+        planes = sb("planes", [P, PASSES * J // 4], I32)
+        nc.vector.memset(planes[:], 0)
         picked_rows = sb("picked_rows", [P, J // 4], I32)
         nc.vector.tensor_copy(picked_rows[:].bitcast(U8), tab_rows[:].bitcast(U8).indirect(offsets[:]))
-        for a in range(PASSES):
-            load_weight(("co", a))
-            for r in range(4):
-                nc.sync.dma_start(planes[a][r:P:32, :], picked_rows[64 * a + 4 * r : 64 * (a + 1) : 16, :])
-        for a in range(PASSES):
-            load_weight(("si", a))
+        load_weight(("co", 0))
+        for q in range(4):
+            nc.sync.dma_start(planes[32 * q : 32 * q + 4, :], picked_rows[32 * q : 32 * (q + 1) : 4, :])
+        for key in WEIGHTS[1:]:
+            load_weight(key)
 
         fb_codes = sb("fb_codes", [P, 2 * N // 4], I32)
         nc.sync.dma_start(fb_codes[:], fb_words[0].bitcast(I32))
@@ -126,30 +125,35 @@ def tile_list_meltab_norm_kernel(
             nc.vector.tensor_copy(picked[h][:], tab[:].bitcast(U32).indirect(offsets[:, cols]))
 
         def part(h):
-            parted[h] = sb("parted%d" % h, [P, PASSES, HALF], U16, "grouped_co0" if h else None)
+            parted[h] = sb("parted%d" % h, [P, PASSES, HALF], U16, "grouped_co1" if h else None)
             nc.vector.tensor_copy(parted[h][:], picked[h][:].bitcast(U16).rearrange("p (j a) -> p a j", a=PASSES))
 
-        def transform(dst, key, t, h, first):
+        def transform(dst, key, t, h, first, j0=0, j1=HALF):
             a = key[1]
             cols = slice(P * (t % 2), P * (t % 2 + 1))
             nc.tensor.matmul_mx(
-                dst[:],
+                dst,
                 lhsT=codes[key, t // 2][:, cols].bitcast(FP8X4),
                 lhsT_scale=scales[key, t // 2][:, cols],
-                rhs=parted[h][:, a, :].bitcast(FP4X4),
-                rhs_scale=planes[a][:].bitcast(U8)[:, h * HALF : (h + 1) * HALF],
+                rhs=parted[h][:, a, j0:j1].bitcast(FP4X4),
+                rhs_scale=planes[:].bitcast(U8)[:, a * J + h * HALF + j0 : a * J + h * HALF + j1],
                 start=first,
                 stop=not first,
             )
 
         chunks = len(WIDTHS)
         spans = [(sum(WIDTHS[:c]), sum(WIDTHS[: c + 1])) for c in range(chunks)]
-        half_of = [j0 // HALF for j0, j1 in spans]
-        sq_re = [laid.tile([P, PACK, HALF], F32, name="sq_re%d" % h, offset=4 * PACK * HALF * h) for h in range(2)]
-        sq_im = [sb("sq_im%d" % c, [P, PACK, WIDTHS[c]], F32) for c in range(chunks)]
+        re_ranges = ((0, 512), (512, 768), (768, 1024))
+        im_ranges = ((0, 128), (128, 256), (256, 512), (512, 768), (768, 1024))
+        sq_re = [
+            laid.tile([P, PACK, j1 - j0], F32, name="sq_re%d" % j0, offset=4 * PACK * j0) for j0, j1 in re_ranges
+        ]
+        sq_im = [sb("sq_im%d" % j0, [P, PACK, j1 - j0], F32) for j0, j1 in im_ranges]
 
-        def in_half(c):
-            return slice(spans[c][0] % HALF, spans[c][0] % HALF + WIDTHS[c])
+        def squares_of(tiles, ranges, c):
+            j0, j1 = spans[c]
+            r = max(i for i in range(len(ranges)) if ranges[i][0] <= j0)
+            return tiles[r][:, :, j0 - ranges[r][0] : j1 - ranges[r][0]]
 
         sgn = sb("sgn", [P, PACK], BF16)
         mag = sb("mag", [P, PACK], F32)
@@ -169,17 +173,31 @@ def tile_list_meltab_norm_kernel(
 
         def open_sum(name, h, t, a):
             acc[name, h, t] = bank(BANKS[name, h][t], "%s%d%d" % (name, h, t))
-            transform(acc[name, h, t], (name, a), t, h, True)
+            transform(acc[name, h, t][:], (name, a), t, h, True)
 
         def close_sum(name, h, t, a):
-            transform(acc[name, h, t], (name, a), t, h, False)
+            transform(acc[name, h, t][:], (name, a), t, h, False)
 
-        def square_re(h, t):
-            square(sq_re[h][:, t, :], acc["co", h, t][:], t)
+        def re_quarter(q):
+            for g in range(2):
+                acc["co", q, g] = bank(BANKS["co", 1][2 * (q - 2) + g], "co%d%d" % (q, g))
+                for t in (2 * g, 2 * g + 1):
+                    dst = acc["co", q, g][:, QUARTER * (t % 2) : QUARTER * (t % 2 + 1)]
+                    for a in range(PASSES):
+                        transform(dst, ("co", a), t, 1, a == 0, QUARTER * (q - 2), QUARTER * (q - 1))
 
-        def square_im(c):
+        def square_re(t):
+            square(sq_re[0][:, t, :], acc["co", 0, t][:], t)
+
+        def square_re_quarter(q):
             for t in range(PACK):
-                square(sq_im[c][:, t, :], acc["si", half_of[c], t][:, in_half(c)], t)
+                square(sq_re[q - 1][:, t, :], acc["co", q, t // 2][:, QUARTER * (t % 2) : QUARTER * (t % 2 + 1)], t)
+
+        def square_im(r):
+            j0, j1 = im_ranges[r]
+            h = j0 // HALF
+            for t in range(PACK):
+                square(sq_im[r][:, t, :], acc["si", h, t][:, j0 - h * HALF : j1 - h * HALF], t)
 
         for h in range(2):
             gather(h)
@@ -189,21 +207,17 @@ def tile_list_meltab_norm_kernel(
             quantise(("co", 0), 2 * g, 2 * g + 2)
             for t in (2 * g, 2 * g + 1):
                 open_sum("co", 0, t, 0)
-        part(1)
         cast(("co", 1))
         for g in range(2):
             quantise(("co", 1), 2 * g, 2 * g + 2)
             for t in (2 * g, 2 * g + 1):
                 close_sum("co", 0, t, 1)
-        for t in range(EARLY):
-            open_sum("co", 1, t, 0)
-            close_sum("co", 1, t, 1)
+        part(1)
+        re_quarter(2)
 
         cast(("si", 0))
         for t in range(PACK):
-            square_re(0, t)
-        for t in range(EARLY):
-            square_re(1, t)
+            square_re(t)
         for g in range(2):
             quantise(("si", 0), 2 * g, 2 * g + 2)
             for t in (2 * g, 2 * g + 1):
@@ -216,21 +230,17 @@ def tile_list_meltab_norm_kernel(
             close_sum("si", 0, t, 1)
         for t in range(EARLY):
             close_sum("si", 1, t, 1)
+        square_im(0)
+        square_re_quarter(2)
         for t in range(EARLY, PACK):
             open_sum("si", 1, t, 1)
             close_sum("si", 1, t, 0)
-        first_half = [c for c in range(chunks) if half_of[c] == 0]
-        second_half = [c for c in range(chunks) if half_of[c] == 1]
-        for c in first_half:
-            square_im(c)
-        for t in range(EARLY, PACK):
-            open_sum("co", 1, t, 0)
-            close_sum("co", 1, t, 1)
-        square_im(second_half[0])
-        for t in range(EARLY, PACK):
-            square_re(1, t)
-        for c in second_half[1:]:
-            square_im(c)
+        square_im(1)
+        square_im(2)
+        re_quarter(3)
+        square_im(3)
+        square_re_quarter(3)
+        square_im(4)
 
         power = [sb("power%d" % c, [P, WIDTHS[c], PACK], BF16) for c in range(chunks)]
         signed = [sb("signed%d" % c, [P, WIDTHS[c], PACK], BF16) for c in range(chunks)]
@@ -242,8 +252,8 @@ def tile_list_meltab_norm_kernel(
         def add(c):
             nc.vector.tensor_tensor(
                 power[c][:].rearrange("p (n e) t -> p n t e", e=2),
-                sq_re[half_of[c]][:, :, in_half(c)].rearrange("p t (n e) -> p n t e", e=2),
-                sq_im[c][:].rearrange("p t (n e) -> p n t e", e=2),
+                squares_of(sq_re, re_ranges, c).rearrange("p t (n e) -> p n t e", e=2),
+                squares_of(sq_im, im_ranges, c).rearrange("p t (n e) -> p n t e", e=2),
                 ALU.add,
             )
 

@@ -23,11 +23,12 @@ PASSES = K // K_PASS
 HALF = 512
 WIDTHS = (128, 128, 256, 256, 128, 128)
 QUARTER = 256
-ON_SCALAR = {("co", 0): 76, ("co", 1): 44, ("si", 0): 0, ("si", 1): 44}
+ON_SCALAR = {("co", 0): 76, ("co", 1): 44, ("si", 0): 0, ("si", 1): 36}
 WEIGHTS = tuple(ON_SCALAR)
 HEAD = 768
 BANKS = {("co", 0): (0, 1, 2, 3), ("co", 1): (4, 5, 6, 7), ("si", 0): (6, 7, 0, 1), ("si", 1): (2, 3, 4, 5)}
 EARLY = 2
+SHARED = 4
 Y_BANKS = (0, 1, 6, 7, 2, 3, 4)
 
 
@@ -47,10 +48,10 @@ def tile_list_meltab_norm_kernel(
             return psum.tile([P, HALF], F32, name=name, tag="bank%d" % b)
 
         offsets = keep.tile([P, J // 16], U16, name="offsets")
-        nc.sync.dma_start(offsets[:], offs)
         tab = sb("tab", [P, T], I32)
         tab_src = tab_words[0].rearrange("p t b -> p (t b)").bitcast(I32)
         nc.sync.dma_start(tab[:, :HEAD], tab_src[:, :HEAD])
+        nc.sync.dma_start(offsets[:], offs)
         gain = sb("gain", [P, PACK], F32)
         nc.sync.dma_start(gain[:], gn.rearrange("(p t) -> p t", t=PACK))
         tab_rows = sb("tab_rows", [P, T // 4], I32)
@@ -76,10 +77,15 @@ def tile_list_meltab_norm_kernel(
         nc.vector.tensor_copy(picked_rows[:].bitcast(U8), tab_rows[:].bitcast(U8).indirect(offsets[:]))
         load_weight(("co", 0))
         for q in range(4):
-            nc.sync.dma_start(planes[32 * q : 32 * q + 4, :], picked_rows[32 * q : 32 * (q + 1) : 4, :])
+            (nc.sync if q < 2 else nc.scalar).dma_start(planes[32 * q : 32 * q + 4, :], picked_rows[32 * q : 32 * (q + 1) : 4, :])
         for key in WEIGHTS[1:]:
             load_weight(key)
 
+        mean = sb("mean", [P, 2], F32)
+        rdev = sb("rdev", [P, 2], F32)
+        with nc.allow_non_contiguous_dma(reason="one value a partition"):
+            nc.sync.dma_start(mean[:], mu.rearrange("(u p) -> p u", p=P))
+            nc.sync.dma_start(rdev[:], isd.rearrange("(u p) -> p u", p=P))
         fb_codes = sb("fb_codes", [P, 2 * N // 4], I32)
         nc.sync.dma_start(fb_codes[:], fb_words[0].bitcast(I32))
         fb_plane = sb("fb_plane", [P, N // 4], I32)
@@ -87,11 +93,6 @@ def tile_list_meltab_norm_kernel(
         fb_rows = fb_scales[0].bitcast(I32).rearrange("(q r) w -> r q w", r=4)
         for r in range(4):
             nc.sync.dma_start(fb_plane[r:P:32, :], fb_rows[r])
-        mean = sb("mean", [P, 2], F32)
-        rdev = sb("rdev", [P, 2], F32)
-        with nc.allow_non_contiguous_dma(reason="one value a partition"):
-            nc.sync.dma_start(mean[:], mu.rearrange("(u p) -> p u", p=P))
-            nc.sync.dma_start(rdev[:], isd.rearrange("(u p) -> p u", p=P))
 
         grouped, codes, scales = {}, {}, {}
         for key in WEIGHTS:
@@ -222,31 +223,21 @@ def tile_list_meltab_norm_kernel(
             quantise(("si", 0), 2 * g, 2 * g + 2)
             for t in (2 * g, 2 * g + 1):
                 open_sum("si", 0, t, 0)
-        for t in range(EARLY):
-            open_sum("si", 1, t, 0)
         cast(("si", 1))
-        for t in range(PACK):
-            quantise(("si", 1), t, t + 1)
-            close_sum("si", 0, t, 1)
+        for t0, t1 in ((0, 2), (2, 3), (3, 4)):
+            quantise(("si", 1), t0, t1)
+            for t in range(t0, t1):
+                close_sum("si", 0, t, 1)
         for t in range(EARLY):
-            close_sum("si", 1, t, 1)
-        square_im(0)
-        square_re_quarter(2)
-        for t in range(EARLY, PACK):
             open_sum("si", 1, t, 1)
             close_sum("si", 1, t, 0)
-        square_im(1)
-        square_im(2)
-        re_quarter(3)
-        square_im(3)
-        square_re_quarter(3)
-        square_im(4)
-
         power = [sb("power%d" % c, [P, WIDTHS[c], PACK], BF16) for c in range(chunks)]
         signed = [sb("signed%d" % c, [P, WIDTHS[c], PACK], BF16) for c in range(chunks)]
         h_codes = [sb("h_codes%d" % c, [P, WIDTHS[c]], U32) for c in range(chunks)]
         h_scales = [sb("h_scales%d" % c, [P, WIDTHS[c]], U8) for c in range(chunks)]
-        result = [sb("result%d" % c, [P, 2, WIDTHS[c]], F32) for c in range(chunks)]
+        out_ranges = ((0, 256), (256, 512), (512, 768), (768, 896), (896, 1024))
+        store_of = [max(r for r in range(len(out_ranges)) if out_ranges[r][0] <= j0) for j0, j1 in spans]
+        result = [sb("result%d" % j0, [P, 2, j1 - j0], F32) for j0, j1 in out_ranges]
         out_rows = out.rearrange("(u p) j -> p u j", p=P)
 
         def add(c):
@@ -268,14 +259,17 @@ def tile_list_meltab_norm_kernel(
                 in_=signed[c][:].rearrange("p j t -> p (j t)"),
             )
 
-        def finish(c):
-            width = WIDTHS[c]
-            first = bank(Y_BANKS[c], "y%d" % c)
-            second = bank(Y_BANKS[c + 1], "y_last") if c == chunks - 1 else first
-            y = [first[:, :width], second[:, width : 2 * width]]
+        y_bank = {}
+
+        def filters(c):
+            r = store_of[c]
+            j0, j1 = out_ranges[r]
             for u in range(2):
+                if (r, u) not in y_bank:
+                    y_bank[r, u] = y_bank[r, 0] if u and r < SHARED else bank(Y_BANKS[r + u], "y%d%d" % (r, u))
+                first = (j1 - j0) * u + spans[c][0] - j0
                 nc.tensor.matmul_mx(
-                    y[u],
+                    y_bank[r, u][:, first : first + WIDTHS[c]],
                     lhsT=fb_codes[:].bitcast(U8)[:, 2 * P * u : 2 * P * (u + 1)].bitcast(FP4X4),
                     lhsT_scale=fb_plane[:].bitcast(U8)[:, P * u : P * (u + 1)],
                     rhs=h_codes[c][:].bitcast(FP8X4),
@@ -283,22 +277,55 @@ def tile_list_meltab_norm_kernel(
                     start=True,
                     stop=True,
                 )
+
+        def finish(r):
+            j0, j1 = out_ranges[r]
             for u in range(2):
-                if c == chunks - 1 and u == 1:
+                y = y_bank[r, u][:, (j1 - j0) * u : (j1 - j0) * (u + 1)]
+                if r >= SHARED and u == 1:
                     nc.vector.tensor_scalar(
-                        result[c][:, u, :], y[u], rdev[:, u : u + 1], shift[:, u : u + 1], ALU.mult, ALU.add
+                        result[r][:, u, :], y, rdev[:, u : u + 1], shift[:, u : u + 1], ALU.mult, ALU.add
                     )
                 else:
                     nc.scalar.activation(
-                        result[c][:, u, :], y[u], ACT.Identity, bias=shift[:, u : u + 1], scale=rdev[:, u : u + 1]
+                        result[r][:, u, :], y, ACT.Identity, bias=shift[:, u : u + 1], scale=rdev[:, u : u + 1]
                     )
-            nc.sync.dma_start(out_rows[:, :, spans[c][0] : spans[c][1]], result[c][:])
+            nc.sync.dma_start(out_rows[:, :, j0:j1], result[r][:])
 
-        for step in range(chunks + 2):
-            if step < chunks:
-                add(step)
-            if 1 <= step <= chunks:
-                sign(step - 1)
-            if step >= 2:
-                quantise_h(step - 2)
-                finish(step - 2)
+        def close(c):
+            quantise_h(c)
+            filters(c)
+
+        square_im(0)
+        square_re_quarter(2)
+        for t in range(EARLY, PACK):
+            open_sum("si", 1, t, 1)
+            close_sum("si", 1, t, 0)
+        square_im(1)
+        square_im(2)
+        re_quarter(3)
+        square_im(3)
+        add(0)
+        add(1)
+        sign(0)
+        sign(1)
+        close(0)
+        add(2)
+        close(1)
+        finish(0)
+        sign(2)
+        add(3)
+        close(2)
+        square_re_quarter(3)
+        square_im(4)
+        finish(1)
+        sign(3)
+        add(4)
+        close(3)
+        add(5)
+        sign(4)
+        sign(5)
+        close(4)
+        close(5)
+        for r in range(2, len(out_ranges)):
+            finish(r)

@@ -29,7 +29,8 @@ HEAD = 768
 BANKS = {("co", 0): (0, 1, 2, 3), ("co", 1): (4, 5, 6, 7), ("si", 0): (6, 7, 0, 1), ("si", 1): (2, 3, 4, 5)}
 EARLY = 2
 SHARED = 4
-Y_BANKS = (0, 1, 6, 7, 2, 3, 4)
+QUARTER_BANKS = {("co", 2): 4, ("co", 3): 6, ("si", 0): 6, ("si", 1): 0, ("si", 2): 2, ("si", 3): 4}
+Y_BANKS = (0, 1, 2, 3, 6, 7)
 
 
 def tile_list_meltab_norm_kernel(
@@ -129,7 +130,7 @@ def tile_list_meltab_norm_kernel(
             parted[h] = sb("parted%d" % h, [P, PASSES, HALF], U16, "grouped_co1" if h else None)
             nc.vector.tensor_copy(parted[h][:], picked[h][:].bitcast(U16).rearrange("p (j a) -> p a j", a=PASSES))
 
-        def transform(dst, key, t, h, first, j0=0, j1=HALF):
+        def transform(dst, key, t, h, start, stop, j0=0, j1=HALF):
             a = key[1]
             cols = slice(P * (t % 2), P * (t % 2 + 1))
             nc.tensor.matmul_mx(
@@ -138,8 +139,8 @@ def tile_list_meltab_norm_kernel(
                 lhsT_scale=scales[key, t // 2][:, cols],
                 rhs=parted[h][:, a, j0:j1].bitcast(FP4X4),
                 rhs_scale=planes[:].bitcast(U8)[:, a * J + h * HALF + j0 : a * J + h * HALF + j1],
-                start=first,
-                stop=not first,
+                start=start,
+                stop=stop,
             )
 
         chunks = len(WIDTHS)
@@ -174,31 +175,37 @@ def tile_list_meltab_norm_kernel(
 
         def open_sum(name, h, t, a):
             acc[name, h, t] = bank(BANKS[name, h][t], "%s%d%d" % (name, h, t))
-            transform(acc[name, h, t][:], (name, a), t, h, True)
+            transform(acc[name, h, t][:], (name, a), t, h, True, False)
 
         def close_sum(name, h, t, a):
-            transform(acc[name, h, t][:], (name, a), t, h, False)
+            transform(acc[name, h, t][:], (name, a), t, h, False, True)
 
-        def re_quarter(q):
-            for g in range(2):
-                acc["co", q, g] = bank(BANKS["co", 1][2 * (q - 2) + g], "co%d%d" % (q, g))
-                for t in (2 * g, 2 * g + 1):
-                    dst = acc["co", q, g][:, QUARTER * (t % 2) : QUARTER * (t % 2 + 1)]
-                    for a in range(PASSES):
-                        transform(dst, ("co", a), t, 1, a == 0, QUARTER * (q - 2), QUARTER * (q - 1))
+        def quarter_pass(name, q, t, a, start, stop):
+            if (name, "q", q, t // 2) not in acc:
+                acc[name, "q", q, t // 2] = bank(QUARTER_BANKS[name, q] + t // 2, "%sq%d%d" % (name, q, t // 2))
+            dst = acc[name, "q", q, t // 2][:, QUARTER * (t % 2) : QUARTER * (t % 2 + 1)]
+            transform(dst, (name, a), t, q // 2, start, stop, QUARTER * (q % 2), QUARTER * (q % 2 + 1))
+
+        def whole_quarter(name, q):
+            for t in range(PACK):
+                quarter_pass(name, q, t, 1, True, False)
+                quarter_pass(name, q, t, 0, False, True)
+
+        def quarter_sums(name, q, t):
+            return acc[name, "q", q, t // 2][:, QUARTER * (t % 2) : QUARTER * (t % 2 + 1)]
 
         def square_re(t):
             square(sq_re[0][:, t, :], acc["co", 0, t][:], t)
 
         def square_re_quarter(q):
             for t in range(PACK):
-                square(sq_re[q - 1][:, t, :], acc["co", q, t // 2][:, QUARTER * (t % 2) : QUARTER * (t % 2 + 1)], t)
+                square(sq_re[q - 1][:, t, :], quarter_sums("co", q, t), t)
 
         def square_im(r):
             j0, j1 = im_ranges[r]
-            h = j0 // HALF
+            q = j0 // QUARTER
             for t in range(PACK):
-                square(sq_im[r][:, t, :], acc["si", h, t][:, j0 - h * HALF : j1 - h * HALF], t)
+                square(sq_im[r][:, t, :], quarter_sums("si", q, t)[:, j0 - q * QUARTER : j1 - q * QUARTER], t)
 
         for h in range(2):
             gather(h)
@@ -214,23 +221,24 @@ def tile_list_meltab_norm_kernel(
             for t in (2 * g, 2 * g + 1):
                 close_sum("co", 0, t, 1)
         part(1)
-        re_quarter(2)
+        whole_quarter("co", 2)
 
         cast(("si", 0))
         for t in range(PACK):
             square_re(t)
         for g in range(2):
             quantise(("si", 0), 2 * g, 2 * g + 2)
-            for t in (2 * g, 2 * g + 1):
-                open_sum("si", 0, t, 0)
+            for q in range(2):
+                for t in (2 * g, 2 * g + 1):
+                    quarter_pass("si", q, t, 0, t % 2 == 0, False)
         cast(("si", 1))
         for t0, t1 in ((0, 2), (2, 3), (3, 4)):
             quantise(("si", 1), t0, t1)
             for t in range(t0, t1):
-                close_sum("si", 0, t, 1)
-        for t in range(EARLY):
-            open_sum("si", 1, t, 1)
-            close_sum("si", 1, t, 0)
+                quarter_pass("si", 0, t, 1, False, t % 2 == 1)
+        for t in range(PACK):
+            quarter_pass("si", 1, t, 1, False, t % 2 == 1)
+        whole_quarter("si", 2)
         power = [sb("power%d" % c, [P, WIDTHS[c], PACK], BF16) for c in range(chunks)]
         signed = [sb("signed%d" % c, [P, WIDTHS[c], PACK], BF16) for c in range(chunks)]
         h_codes = [sb("h_codes%d" % c, [P, WIDTHS[c]], U32) for c in range(chunks)]
@@ -297,13 +305,11 @@ def tile_list_meltab_norm_kernel(
             filters(c)
 
         square_im(0)
-        square_re_quarter(2)
-        for t in range(EARLY, PACK):
-            open_sum("si", 1, t, 1)
-            close_sum("si", 1, t, 0)
         square_im(1)
+        whole_quarter("co", 3)
         square_im(2)
-        re_quarter(3)
+        square_re_quarter(2)
+        whole_quarter("si", 3)
         square_im(3)
         add(0)
         add(1)

@@ -23,14 +23,14 @@ PASSES = K // K_PASS
 HALF = 512
 WIDTHS = (128, 128, 256, 256, 128, 128)
 QUARTER = 256
-ON_SCALAR = {("co", 0): 76, ("co", 1): 44, ("si", 0): 0, ("si", 1): 36}
+ON_SCALAR = {("co", 0): 76, ("co", 1): 44, ("si", 0): 0, ("si", 1): 28}
 WEIGHTS = tuple(ON_SCALAR)
 HEAD = 768
 BANKS = {("co", 0): (0, 1, 2, 3), ("co", 1): (4, 5, 6, 7), ("si", 0): (6, 7, 0, 1), ("si", 1): (2, 3, 4, 5)}
 EARLY = 2
-SHARED = 4
-QUARTER_BANKS = {("co", 2): 4, ("co", 3): 6, ("si", 0): 6, ("si", 1): 0, ("si", 2): 2, ("si", 3): 4}
-Y_BANKS = (0, 1, 2, 3, 6, 7)
+SHARED = 3
+QUARTER_BANKS = {("co", 2): (4, 4), ("co", 3): (6, 7), ("si", 0): (6, 7), ("si", 1): (0, 1), ("si", 2): (2, 3), ("si", 3): (5, 4)}
+Y_BANKS = (0, 1, 2, 3, 6, 7, 4)
 
 
 def tile_list_meltab_norm_kernel(
@@ -105,6 +105,10 @@ def tile_list_meltab_norm_kernel(
         def cast(key):
             src = raw[key].rearrange("p i (m t) -> p m i t", t=PACK)
             dst = grouped[key][:].rearrange("p t m i -> p m i t")
+            if key == ("co", 1):
+                nc.vector.tensor_copy(dst[:, :, :, :2], src[:, :, :, :2])
+                nc.scalar.copy(dst[:, :, :, 2:], src[:, :, :, 2:])
+                return
             split = ON_SCALAR[key]
             if split > 0:
                 nc.scalar.copy(dst[:, :split], src[:, :split])
@@ -159,12 +163,10 @@ def tile_list_meltab_norm_kernel(
 
         sgn = sb("sgn", [P, PACK], BF16)
         mag = sb("mag", [P, PACK], F32)
-        exponent = sb("exponent", [P, PACK], F32)
-        root = sb("root", [P, PACK], F32, "tab_rows")
-        nc.gpsimd.memset(exponent[:], 0.5)
+        root = sb("root", [P, PACK], F32)
         nc.scalar.activation(mag[:], gain[:], ACT.Abs)
         nc.scalar.activation(sgn[:], gain[:], ACT.Sign)
-        nc.gpsimd.tensor_tensor(root[:], mag[:], exponent[:], ALU.pow)
+        nc.scalar.activation(root[:], mag[:], ACT.Sqrt)
         shift = sb("shift", [P, 2], F32)
         nc.vector.scalar_tensor_tensor(shift[:], mean[:], -1.0, rdev[:], ALU.mult, ALU.mult)
 
@@ -180,25 +182,26 @@ def tile_list_meltab_norm_kernel(
         def close_sum(name, h, t, a):
             transform(acc[name, h, t][:], (name, a), t, h, False, True)
 
-        def quarter_pass(name, q, t, a, start, stop):
-            if (name, "q", q, t // 2) not in acc:
-                acc[name, "q", q, t // 2] = bank(QUARTER_BANKS[name, q] + t // 2, "%sq%d%d" % (name, q, t // 2))
-            dst = acc[name, "q", q, t // 2][:, QUARTER * (t % 2) : QUARTER * (t % 2 + 1)]
-            transform(dst, (name, a), t, q // 2, start, stop, QUARTER * (q % 2), QUARTER * (q % 2 + 1))
+        def quarter_sums(name, q, t):
+            g, side = (t // 2, t % 2) if name == "co" or q == 0 else (min(t, 3 - t), t // 2)
+            if (name, "q", q, g) not in acc:
+                acc[name, "q", q, g] = bank(QUARTER_BANKS[name, q][g], "%sq%d%d" % (name, q, g))
+            return acc[name, "q", q, g][:, QUARTER * side : QUARTER * (side + 1)]
 
-        def whole_quarter(name, q):
-            for t in range(PACK):
+        def quarter_pass(name, q, t, a, start, stop):
+            j0 = QUARTER * (q % 2)
+            transform(quarter_sums(name, q, t), (name, a), t, q // 2, start, stop, j0, j0 + QUARTER)
+
+        def whole_quarter(name, q, classes=range(PACK)):
+            for t in classes:
                 quarter_pass(name, q, t, 1, True, False)
                 quarter_pass(name, q, t, 0, False, True)
-
-        def quarter_sums(name, q, t):
-            return acc[name, "q", q, t // 2][:, QUARTER * (t % 2) : QUARTER * (t % 2 + 1)]
 
         def square_re(t):
             square(sq_re[0][:, t, :], acc["co", 0, t][:], t)
 
-        def square_re_quarter(q):
-            for t in range(PACK):
+        def square_re_quarter(q, classes=range(PACK)):
+            for t in classes:
                 square(sq_re[q - 1][:, t, :], quarter_sums("co", q, t), t)
 
         def square_im(r):
@@ -213,15 +216,18 @@ def tile_list_meltab_norm_kernel(
         cast(("co", 0))
         for g in range(2):
             quantise(("co", 0), 2 * g, 2 * g + 2)
-            for t in (2 * g, 2 * g + 1):
-                open_sum("co", 0, t, 0)
+        for t in range(2):
+            open_sum("co", 0, t, 0)
         cast(("co", 1))
-        for g in range(2):
-            quantise(("co", 1), 2 * g, 2 * g + 2)
-            for t in (2 * g, 2 * g + 1):
-                close_sum("co", 0, t, 1)
+        for t in range(2):
+            quantise(("co", 1), t, t + 1)
+            close_sum("co", 0, t, 1)
+        quantise(("co", 1), 2, 4)
+        for t in range(2, PACK):
+            open_sum("co", 0, t, 1)
+            close_sum("co", 0, t, 0)
         part(1)
-        whole_quarter("co", 2)
+        whole_quarter("co", 2, (0, 1))
 
         cast(("si", 0))
         for t in range(PACK):
@@ -230,15 +236,15 @@ def tile_list_meltab_norm_kernel(
             quantise(("si", 0), 2 * g, 2 * g + 2)
             for q in range(2):
                 for t in (2 * g, 2 * g + 1):
-                    quarter_pass("si", q, t, 0, t % 2 == 0, False)
+                    quarter_pass("si", q, t, 0, t % 2 == 0 if q == 0 else t < 2, False)
         cast(("si", 1))
         for t0, t1 in ((0, 2), (2, 3), (3, 4)):
             quantise(("si", 1), t0, t1)
             for t in range(t0, t1):
                 quarter_pass("si", 0, t, 1, False, t % 2 == 1)
-        for t in range(PACK):
-            quarter_pass("si", 1, t, 1, False, t % 2 == 1)
-        whole_quarter("si", 2)
+        for t in (2, 1, 3, 0):
+            quarter_pass("si", 1, t, 1, False, t < 2)
+        whole_quarter("si", 2, (2, 1, 3, 0))
         power = [sb("power%d" % c, [P, WIDTHS[c], PACK], BF16) for c in range(chunks)]
         signed = [sb("signed%d" % c, [P, WIDTHS[c], PACK], BF16) for c in range(chunks)]
         h_codes = [sb("h_codes%d" % c, [P, WIDTHS[c]], U32) for c in range(chunks)]
@@ -274,7 +280,7 @@ def tile_list_meltab_norm_kernel(
             j0, j1 = out_ranges[r]
             for u in range(2):
                 if (r, u) not in y_bank:
-                    y_bank[r, u] = y_bank[r, 0] if u and r < SHARED else bank(Y_BANKS[r + u], "y%d%d" % (r, u))
+                    y_bank[r, u] = y_bank[r, 0] if u and r < SHARED else bank(Y_BANKS[r if r < SHARED else 2 * r - SHARED + u], "y%d%d" % (r, u))
                 first = (j1 - j0) * u + spans[c][0] - j0
                 nc.tensor.matmul_mx(
                     y_bank[r, u][:, first : first + WIDTHS[c]],
@@ -304,11 +310,13 @@ def tile_list_meltab_norm_kernel(
             quantise_h(c)
             filters(c)
 
+        square_re_quarter(2, (0, 1))
+        whole_quarter("co", 2, (2, 3))
         square_im(0)
         square_im(1)
         whole_quarter("co", 3)
         square_im(2)
-        square_re_quarter(2)
+        square_re_quarter(2, (2, 3))
         whole_quarter("si", 3)
         square_im(3)
         add(0)

@@ -25,11 +25,11 @@ WIDTHS = (128, 128, 256, 256, 128, 128)
 QUARTER = 256
 ON_SCALAR = {("co", 0): 76, ("co", 1): 44, ("si", 0): 0, ("si", 1): 28}
 WEIGHTS = tuple(ON_SCALAR)
-HEAD = 768
+HEAD = 1024
 BANKS = {("co", 0): (0, 1, 2, 3), ("co", 1): (4, 5, 6, 7), ("si", 0): (6, 7, 0, 1), ("si", 1): (2, 3, 4, 5)}
 EARLY = 2
 SHARED = 3
-QUARTER_BANKS = {("co", 2): (4, 4), ("co", 3): (6, 7), ("si", 0): (6, 7), ("si", 1): (0, 1), ("si", 2): (2, 3), ("si", 3): (5, 4)}
+QUARTER_BANKS = {("co", 2): (4, 5), ("co", 3): (6, 7), ("si", 0): (6, 7), ("si", 1): (0, 1), ("si", 2): (2, 3), ("si", 3): (4, 5)}
 Y_BANKS = (0, 1, 2, 3, 6, 7, 4)
 
 
@@ -150,7 +150,7 @@ def tile_list_meltab_norm_kernel(
         chunks = len(WIDTHS)
         spans = [(sum(WIDTHS[:c]), sum(WIDTHS[: c + 1])) for c in range(chunks)]
         re_ranges = ((0, 512), (512, 768), (768, 1024))
-        im_ranges = ((0, 128), (128, 256), (256, 512), (512, 768), (768, 1024))
+        im_ranges = ((0, 128), (128, 256), (256, 512), (512, 768), (768, 896), (896, 1024))
         sq_re = [
             laid.tile([P, PACK, j1 - j0], F32, name="sq_re%d" % j0, offset=4 * PACK * j0) for j0, j1 in re_ranges
         ]
@@ -227,7 +227,7 @@ def tile_list_meltab_norm_kernel(
             open_sum("co", 0, t, 1)
             close_sum("co", 0, t, 0)
         part(1)
-        whole_quarter("co", 2, (0, 1))
+        whole_quarter("co", 2, range(3))
 
         cast(("si", 0))
         for t in range(PACK):
@@ -310,13 +310,13 @@ def tile_list_meltab_norm_kernel(
             quantise_h(c)
             filters(c)
 
-        square_re_quarter(2, (0, 1))
-        whole_quarter("co", 2, (2, 3))
+        square_re_quarter(2, range(3))
+        whole_quarter("co", 2, (3,))
         square_im(0)
         square_im(1)
         whole_quarter("co", 3)
         square_im(2)
-        square_re_quarter(2, (2, 3))
+        square_re_quarter(2, (3,))
         whole_quarter("si", 3)
         square_im(3)
         add(0)
@@ -332,6 +332,7 @@ def tile_list_meltab_norm_kernel(
         close(2)
         square_re_quarter(3)
         square_im(4)
+        square_im(5)
         finish(1)
         sign(3)
         add(4)

@@ -21,16 +21,21 @@ PACK = 4
 K_PASS = P * PACK
 PASSES = K // K_PASS
 HALF = 512
-WIDTHS = (128, 128, 256, 256, 128, 128)
 QUARTER = 256
-ON_SCALAR = {("co", 0): 76, ("co", 1): 44, ("si", 0): 0, ("si", 1): 28}
-WEIGHTS = tuple(ON_SCALAR)
-HEAD = 1024
-BANKS = {("co", 0): (0, 1, 2, 3), ("co", 1): (4, 5, 6, 7), ("si", 0): (6, 7, 0, 1), ("si", 1): (2, 3, 4, 5)}
-EARLY = 2
-SHARED = 3
-QUARTER_BANKS = {("co", 2): (4, 5), ("co", 3): (6, 7), ("si", 0): (6, 7), ("si", 1): (0, 1), ("si", 2): (2, 3), ("si", 3): (4, 5)}
-Y_BANKS = (0, 1, 2, 3, 6, 7, 4)
+HEAD = 1280
+CO0_ON_SCALAR = 76
+CHUNKS = ((0, 128), (128, 256), (256, 512), (512, 768), (768, 896), (896, 1024))
+STORES = ((0, 256),) + CHUNKS[2:]
+TWO_ENGINES = 3
+QUARTER_BANKS = {
+    ("co", 2): (4, 5),
+    ("co", 3): (6, 2),
+    ("si", 0): (0, 1, 2, 3),
+    ("si", 1): (4, 5),
+    ("si", 2): (7, 6),
+    ("si", 3): (0, 1),
+}
+Y_BANKS = ((3, 3), (4, 4), (5, 5), (6, 7), (0, 1))
 
 
 def tile_list_meltab_norm_kernel(
@@ -39,7 +44,6 @@ def tile_list_meltab_norm_kernel(
     nc = tc.nc
     with ExitStack() as ctx:
         keep = ctx.enter_context(tc.tile_pool(name="keep", bufs=1))
-        laid = ctx.enter_context(tc.tile_pool(name="laid", bufs=1))
         psum = ctx.enter_context(tc.psum_pool(name="psum", bufs=1))
 
         def sb(name, shape, dtype, tag=None):
@@ -63,24 +67,23 @@ def tile_list_meltab_norm_kernel(
 
         raw = {}
 
-        def load_weight(key):
-            name, a = key
+        def load_weight(name, a):
             w = co if name == "co" else si
-            if key == ("si", 1):
-                raw[key] = laid.tile([P, PACK, F], F32, name="raw_si1", offset=4 * PACK * HALF)[:]
-            else:
-                raw[key] = sb("raw_%s%d" % key, [P, PACK, F], F32)[:]
-            nc.sync.dma_start(raw[key], w[K_PASS * a : K_PASS * (a + 1), :].rearrange("(p i) f -> p i f", i=PACK))
+            raw[name, a] = sb("raw_%s%d" % (name, a), [P, PACK, F], F32)
+            rows = w[K_PASS * a : K_PASS * (a + 1), :].rearrange("(p i) f -> p i f", i=PACK)
+            nc.sync.dma_start(raw[name, a][:], rows)
 
         planes = sb("planes", [P, PASSES * J // 4], I32)
         nc.vector.memset(planes[:], 0)
         picked_rows = sb("picked_rows", [P, J // 4], I32)
         nc.vector.tensor_copy(picked_rows[:].bitcast(U8), tab_rows[:].bitcast(U8).indirect(offsets[:]))
-        load_weight(("co", 0))
-        for q in range(4):
-            (nc.sync if q < 2 else nc.scalar).dma_start(planes[32 * q : 32 * q + 4, :], picked_rows[32 * q : 32 * (q + 1) : 4, :])
-        for key in WEIGHTS[1:]:
-            load_weight(key)
+        load_weight("co", 0)
+        for p0 in range(0, P, 32):
+            queue = nc.sync if p0 < P // 2 else nc.scalar
+            queue.dma_start(planes[p0 : p0 + 4, :], picked_rows[p0 : p0 + 32 : 4, :])
+        load_weight("co", 1)
+        for a in range(PASSES):
+            load_weight("si", a)
 
         mean = sb("mean", [P, 2], F32)
         rdev = sb("rdev", [P, 2], F32)
@@ -96,31 +99,27 @@ def tile_list_meltab_norm_kernel(
             nc.sync.dma_start(fb_plane[r:P:32, :], fb_rows[r])
 
         grouped, codes, scales = {}, {}, {}
-        for key in WEIGHTS:
-            grouped[key] = sb("grouped_%s%d" % key, [P, PACK, P, PACK], BF16)
+        for name, a in raw:
+            grouped[name, a] = sb("grouped_%s%d" % (name, a), [P, PACK, P, PACK], BF16)
             for g in range(2):
-                codes[key, g] = sb("codes_%s%d%d" % (key[0], key[1], g), [P, 2 * P], U32)
-                scales[key, g] = sb("scales_%s%d%d" % (key[0], key[1], g), [P, 2 * P], U8)
+                codes[name, a, g] = sb("codes_%s%d%d" % (name, a, g), [P, 2 * P], U32)
+                scales[name, a, g] = sb("scales_%s%d%d" % (name, a, g), [P, 2 * P], U8)
 
-        def cast(key):
-            src = raw[key].rearrange("p i (m t) -> p m i t", t=PACK)
-            dst = grouped[key][:].rearrange("p t m i -> p m i t")
-            if key == ("co", 1):
-                nc.vector.tensor_copy(dst[:, :, :, :2], src[:, :, :, :2])
-                nc.scalar.copy(dst[:, :, :, 2:], src[:, :, :, 2:])
-                return
-            split = ON_SCALAR[key]
-            if split > 0:
-                nc.scalar.copy(dst[:, :split], src[:, :split])
-            for t in (0, 2):
-                nc.vector.tensor_copy(dst[:, split:, :, t : t + 2], src[:, split:, :, t : t + 2])
+        def cast(copy, name, a, groups, classes):
+            src = raw[name, a][:].rearrange("p i (m t) -> p m i t", t=PACK)
+            dst = grouped[name, a][:].rearrange("p t m i -> p m i t")
+            copy(dst[:, groups, :, classes], src[:, groups, :, classes])
 
-        def quantise(key, t0, t1):
+        def cast_on_vector(name, a, groups):
+            for g in range(2):
+                cast(nc.vector.tensor_copy, name, a, groups, slice(2 * g, 2 * g + 2))
+
+        def quantise(name, a, t0, t1):
             cols = slice(P * (t0 % 2), P * (t0 % 2 + t1 - t0))
             nc.vector.quantize_mx(
-                out=codes[key, t0 // 2][:, cols].bitcast(FP8X4),
-                scales=scales[key, t0 // 2][:, cols],
-                in_=grouped[key][:, t0:t1].rearrange("p t m i -> p (t m i)"),
+                out=codes[name, a, t0 // 2][:, cols].bitcast(FP8X4),
+                scales=scales[name, a, t0 // 2][:, cols],
+                in_=grouped[name, a][:, t0:t1].rearrange("p t m i -> p (t m i)"),
             )
 
         picked, parted = {}, {}
@@ -134,32 +133,44 @@ def tile_list_meltab_norm_kernel(
             parted[h] = sb("parted%d" % h, [P, PASSES, HALF], U16, "grouped_co1" if h else None)
             nc.vector.tensor_copy(parted[h][:], picked[h][:].bitcast(U16).rearrange("p (j a) -> p a j", a=PASSES))
 
-        def transform(dst, key, t, h, start, stop, j0=0, j1=HALF):
-            a = key[1]
+        def transform(dst, name, a, t, j0, j1, first):
+            h = j0 // HALF
             cols = slice(P * (t % 2), P * (t % 2 + 1))
             nc.tensor.matmul_mx(
                 dst,
-                lhsT=codes[key, t // 2][:, cols].bitcast(FP8X4),
-                lhsT_scale=scales[key, t // 2][:, cols],
-                rhs=parted[h][:, a, j0:j1].bitcast(FP4X4),
-                rhs_scale=planes[:].bitcast(U8)[:, a * J + h * HALF + j0 : a * J + h * HALF + j1],
-                start=start,
-                stop=stop,
+                lhsT=codes[name, a, t // 2][:, cols].bitcast(FP8X4),
+                lhsT_scale=scales[name, a, t // 2][:, cols],
+                rhs=parted[h][:, a, j0 - h * HALF : j1 - h * HALF].bitcast(FP4X4),
+                rhs_scale=planes[:].bitcast(U8)[:, a * J + j0 : a * J + j1],
+                start=first,
+                stop=not first,
             )
 
-        chunks = len(WIDTHS)
-        spans = [(sum(WIDTHS[:c]), sum(WIDTHS[: c + 1])) for c in range(chunks)]
-        re_ranges = ((0, 512), (512, 768), (768, 1024))
-        im_ranges = ((0, 128), (128, 256), (256, 512), (512, 768), (768, 896), (896, 1024))
-        sq_re = [
-            laid.tile([P, PACK, j1 - j0], F32, name="sq_re%d" % j0, offset=4 * PACK * j0) for j0, j1 in re_ranges
-        ]
-        sq_im = [sb("sq_im%d" % j0, [P, PACK, j1 - j0], F32) for j0, j1 in im_ranges]
+        acc = {}
 
-        def squares_of(tiles, ranges, c):
-            j0, j1 = spans[c]
-            r = max(i for i in range(len(ranges)) if ranges[i][0] <= j0)
-            return tiles[r][:, :, j0 - ranges[r][0] : j1 - ranges[r][0]]
+        def half_pass(t, a, first):
+            if first:
+                acc["half", t] = bank(t, "re_half%d" % t)
+            transform(acc["half", t][:], "co", a, t, 0, HALF, first)
+
+        def quarter_sums(name, q, t):
+            if name == "co":
+                g, side = t // 2, t % 2
+            elif q == 0:
+                g, side = t, 0
+            else:
+                g, side = min(t, 3 - t), t // 2
+            if (name, q, g) not in acc:
+                acc[name, q, g] = bank(QUARTER_BANKS[name, q][g], "%s%d%d" % (name, q, g))
+            return acc[name, q, g][:, QUARTER * side : QUARTER * (side + 1)]
+
+        def quarter_pass(name, a, q, t, first):
+            transform(quarter_sums(name, q, t), name, a, t, QUARTER * q, QUARTER * (q + 1), first)
+
+        def whole_sums(name, q, classes):
+            for t in classes:
+                quarter_pass(name, 1, q, t, True)
+                quarter_pass(name, 0, q, t, False)
 
         sgn = sb("sgn", [P, PACK], BF16)
         mag = sb("mag", [P, PACK], F32)
@@ -170,120 +181,101 @@ def tile_list_meltab_norm_kernel(
         shift = sb("shift", [P, 2], F32)
         nc.vector.scalar_tensor_tensor(shift[:], mean[:], -1.0, rdev[:], ALU.mult, ALU.mult)
 
+        re_ranges = ((0, HALF), (HALF, HALF + QUARTER), (HALF + QUARTER, J))
+        sq_re = [sb("sq_re%d" % j0, [P, PACK, j1 - j0], F32) for j0, j1 in re_ranges]
+        sq_im = [sb("sq_im%d" % j0, [P, PACK, j1 - j0], F32) for j0, j1 in CHUNKS]
+
         def square(dst, src, t):
             nc.scalar.activation(dst, src, ACT.Square, scale=root[:, t : t + 1])
 
-        acc = {}
-
-        def open_sum(name, h, t, a):
-            acc[name, h, t] = bank(BANKS[name, h][t], "%s%d%d" % (name, h, t))
-            transform(acc[name, h, t][:], (name, a), t, h, True, False)
-
-        def close_sum(name, h, t, a):
-            transform(acc[name, h, t][:], (name, a), t, h, False, True)
-
-        def quarter_sums(name, q, t):
-            g, side = (t // 2, t % 2) if name == "co" or q == 0 else (min(t, 3 - t), t // 2)
-            if (name, "q", q, g) not in acc:
-                acc[name, "q", q, g] = bank(QUARTER_BANKS[name, q][g], "%sq%d%d" % (name, q, g))
-            return acc[name, "q", q, g][:, QUARTER * side : QUARTER * (side + 1)]
-
-        def quarter_pass(name, q, t, a, start, stop):
-            j0 = QUARTER * (q % 2)
-            transform(quarter_sums(name, q, t), (name, a), t, q // 2, start, stop, j0, j0 + QUARTER)
-
-        def whole_quarter(name, q, classes=range(PACK)):
-            for t in classes:
-                quarter_pass(name, q, t, 1, True, False)
-                quarter_pass(name, q, t, 0, False, True)
-
-        def square_re(t):
-            square(sq_re[0][:, t, :], acc["co", 0, t][:], t)
-
-        def square_re_quarter(q, classes=range(PACK)):
+        def square_re(q, classes):
             for t in classes:
                 square(sq_re[q - 1][:, t, :], quarter_sums("co", q, t), t)
 
-        def square_im(r):
-            j0, j1 = im_ranges[r]
+        def square_im(c):
+            j0, j1 = CHUNKS[c]
             q = j0 // QUARTER
             for t in range(PACK):
-                square(sq_im[r][:, t, :], quarter_sums("si", q, t)[:, j0 - q * QUARTER : j1 - q * QUARTER], t)
+                square(sq_im[c][:, t, :], quarter_sums("si", q, t)[:, j0 - q * QUARTER : j1 - q * QUARTER], t)
 
         for h in range(2):
             gather(h)
         part(0)
-        cast(("co", 0))
+        cast(nc.scalar.copy, "co", 0, slice(0, CO0_ON_SCALAR), slice(0, PACK))
+        cast_on_vector("co", 0, slice(CO0_ON_SCALAR, P))
         for g in range(2):
-            quantise(("co", 0), 2 * g, 2 * g + 2)
+            quantise("co", 0, 2 * g, 2 * g + 2)
         for t in range(2):
-            open_sum("co", 0, t, 0)
-        cast(("co", 1))
+            half_pass(t, 0, True)
+        cast(nc.vector.tensor_copy, "co", 1, slice(0, P), slice(0, 2))
+        cast(nc.scalar.copy, "co", 1, slice(0, P), slice(2, PACK))
         for t in range(2):
-            quantise(("co", 1), t, t + 1)
-            close_sum("co", 0, t, 1)
-        quantise(("co", 1), 2, 4)
+            quantise("co", 1, t, t + 1)
+            half_pass(t, 1, False)
+        quantise("co", 1, 2, PACK)
         for t in range(2, PACK):
-            open_sum("co", 0, t, 1)
-            close_sum("co", 0, t, 0)
+            half_pass(t, 1, True)
+            half_pass(t, 0, False)
         part(1)
-        whole_quarter("co", 2, range(3))
+        whole_sums("co", 2, range(PACK))
+        whole_sums("co", 3, (0, 1))
 
-        cast(("si", 0))
+        cast_on_vector("si", 0, slice(0, P))
         for t in range(PACK):
-            square_re(t)
+            square(sq_re[0][:, t, :], acc["half", t][:], t)
+        square_re(2, range(PACK))
+        square_re(3, (0, 1))
         for g in range(2):
-            quantise(("si", 0), 2 * g, 2 * g + 2)
-            for q in range(2):
-                for t in (2 * g, 2 * g + 1):
-                    quarter_pass("si", q, t, 0, t % 2 == 0 if q == 0 else t < 2, False)
-        cast(("si", 1))
-        for t0, t1 in ((0, 2), (2, 3), (3, 4)):
-            quantise(("si", 1), t0, t1)
-            for t in range(t0, t1):
-                quarter_pass("si", 0, t, 1, False, t % 2 == 1)
-        for t in (2, 1, 3, 0):
-            quarter_pass("si", 1, t, 1, False, t < 2)
-        whole_quarter("si", 2, (2, 1, 3, 0))
-        power = [sb("power%d" % c, [P, WIDTHS[c], PACK], BF16) for c in range(chunks)]
-        signed = [sb("signed%d" % c, [P, WIDTHS[c], PACK], BF16) for c in range(chunks)]
-        h_codes = [sb("h_codes%d" % c, [P, WIDTHS[c]], U32) for c in range(chunks)]
-        h_scales = [sb("h_scales%d" % c, [P, WIDTHS[c]], U8) for c in range(chunks)]
-        out_ranges = ((0, 256), (256, 512), (512, 768), (768, 896), (896, 1024))
-        store_of = [max(r for r in range(len(out_ranges)) if out_ranges[r][0] <= j0) for j0, j1 in spans]
-        result = [sb("result%d" % j0, [P, 2, j1 - j0], F32) for j0, j1 in out_ranges]
+            quantise("si", 0, 2 * g, 2 * g + 2)
+            for t in (2 * g, 2 * g + 1):
+                quarter_pass("si", 0, 0, t, True)
+        cast_on_vector("si", 1, slice(0, P))
+        for t in range(PACK):
+            quantise("si", 1, t, t + 1)
+            quarter_pass("si", 1, 0, t, False)
+        for q in (1, 2):
+            whole_sums("si", q, (2, 1, 3, 0))
+
+        widths = [j1 - j0 for j0, j1 in CHUNKS]
+        power = [sb("power%d" % c, [P, w, PACK], BF16) for c, w in enumerate(widths)]
+        signed = [sb("signed%d" % c, [P, w, PACK], BF16) for c, w in enumerate(widths)]
+        h_codes = [sb("h_codes%d" % c, [P, w], U32) for c, w in enumerate(widths)]
+        h_scales = [sb("h_scales%d" % c, [P, w], U8) for c, w in enumerate(widths)]
+        result = [sb("result%d" % j0, [P, 2, j1 - j0], F32) for j0, j1 in STORES]
         out_rows = out.rearrange("(u p) j -> p u j", p=P)
 
         def add(c):
+            j0, j1 = CHUNKS[c]
+            r = max(0, j0 // QUARTER - 1)
             nc.vector.tensor_tensor(
                 power[c][:].rearrange("p (n e) t -> p n t e", e=2),
-                squares_of(sq_re, re_ranges, c).rearrange("p t (n e) -> p n t e", e=2),
-                squares_of(sq_im, im_ranges, c).rearrange("p t (n e) -> p n t e", e=2),
+                sq_re[r][:, :, j0 - re_ranges[r][0] : j1 - re_ranges[r][0]].rearrange("p t (n e) -> p n t e", e=2),
+                sq_im[c][:].rearrange("p t (n e) -> p n t e", e=2),
                 ALU.add,
             )
 
         def sign(c):
-            signs = sgn[:].unsqueeze(1).to_broadcast([P, WIDTHS[c], PACK])
+            signs = sgn[:].unsqueeze(1).to_broadcast([P, widths[c], PACK])
             nc.vector.tensor_tensor(signed[c][:], power[c][:], signs, ALU.mult)
 
-        def quantise_h(c):
+        def y_sums(s, u):
+            b = Y_BANKS[s][u]
+            if ("y", s, b) not in acc:
+                acc["y", s, b] = bank(b, "y%d%d" % (s, u))
+            width = STORES[s][1] - STORES[s][0]
+            return acc["y", s, b][:, width * u : width * (u + 1)]
+
+        def quantise_and_filter(c):
             nc.vector.quantize_mx(
                 out=h_codes[c][:].bitcast(FP8X4),
                 scales=h_scales[c][:],
                 in_=signed[c][:].rearrange("p j t -> p (j t)"),
             )
-
-        y_bank = {}
-
-        def filters(c):
-            r = store_of[c]
-            j0, j1 = out_ranges[r]
+            s = max(0, c - 1)
+            j0, j1 = CHUNKS[c]
             for u in range(2):
-                if (r, u) not in y_bank:
-                    y_bank[r, u] = y_bank[r, 0] if u and r < SHARED else bank(Y_BANKS[r if r < SHARED else 2 * r - SHARED + u], "y%d%d" % (r, u))
-                first = (j1 - j0) * u + spans[c][0] - j0
                 nc.tensor.matmul_mx(
-                    y_bank[r, u][:, first : first + WIDTHS[c]],
+                    y_sums(s, u)[:, j0 - STORES[s][0] : j1 - STORES[s][0]],
                     lhsT=fb_codes[:].bitcast(U8)[:, 2 * P * u : 2 * P * (u + 1)].bitcast(FP4X4),
                     lhsT_scale=fb_plane[:].bitcast(U8)[:, P * u : P * (u + 1)],
                     rhs=h_codes[c][:].bitcast(FP8X4),
@@ -292,55 +284,32 @@ def tile_list_meltab_norm_kernel(
                     stop=True,
                 )
 
-        def finish(r):
-            j0, j1 = out_ranges[r]
+        def pair_of_chunks(c):
+            for stage in (add, sign, quantise_and_filter):
+                stage(c)
+                stage(c + 1)
+
+        def finish(s):
             for u in range(2):
-                y = y_bank[r, u][:, (j1 - j0) * u : (j1 - j0) * (u + 1)]
-                if r >= SHARED and u == 1:
-                    nc.vector.tensor_scalar(
-                        result[r][:, u, :], y, rdev[:, u : u + 1], shift[:, u : u + 1], ALU.mult, ALU.add
-                    )
+                scale, bias = rdev[:, u : u + 1], shift[:, u : u + 1]
+                if s >= TWO_ENGINES and u == 1:
+                    nc.vector.tensor_scalar(result[s][:, u, :], y_sums(s, u), scale, bias, ALU.mult, ALU.add)
                 else:
-                    nc.scalar.activation(
-                        result[r][:, u, :], y, ACT.Identity, bias=shift[:, u : u + 1], scale=rdev[:, u : u + 1]
-                    )
-            nc.sync.dma_start(out_rows[:, :, j0:j1], result[r][:])
+                    nc.scalar.activation(result[s][:, u, :], y_sums(s, u), ACT.Identity, bias=bias, scale=scale)
+            nc.sync.dma_start(out_rows[:, :, STORES[s][0] : STORES[s][1]], result[s][:])
 
-        def close(c):
-            quantise_h(c)
-            filters(c)
-
-        square_re_quarter(2, range(3))
-        whole_quarter("co", 2, (3,))
         square_im(0)
         square_im(1)
-        whole_quarter("co", 3)
+        whole_sums("co", 3, (2, 3))
+        whole_sums("si", 3, range(PACK))
         square_im(2)
-        square_re_quarter(2, (3,))
-        whole_quarter("si", 3)
         square_im(3)
-        add(0)
-        add(1)
-        sign(0)
-        sign(1)
-        close(0)
-        add(2)
-        close(1)
+        pair_of_chunks(0)
         finish(0)
-        sign(2)
-        add(3)
-        close(2)
-        square_re_quarter(3)
+        pair_of_chunks(2)
+        square_re(3, (2, 3))
         square_im(4)
         square_im(5)
-        finish(1)
-        sign(3)
-        add(4)
-        close(3)
-        add(5)
-        sign(4)
-        sign(5)
-        close(4)
-        close(5)
-        for r in range(2, len(out_ranges)):
-            finish(r)
+        pair_of_chunks(4)
+        for s in range(1, len(STORES)):
+            finish(s)

@@ -1,6 +1,7 @@
 from contextlib import ExitStack
 
 import concourse.mybir as mybir
+from concourse.masks import make_identity
 
 K, F, N, T, J = 1024, 512, 256, 4096, 1024
 FLOPS = 2 * (2 * K * F * J + F * N * J)
@@ -22,20 +23,19 @@ K_PASS = P * PACK
 PASSES = K // K_PASS
 HALF = 512
 QUARTER = 256
-HEAD = 1280
+HEAD = 1024
 CO0_ON_SCALAR = 76
 CHUNKS = ((0, 128), (128, 256), (256, 512), (512, 768), (768, 896), (896, 1024))
 STORES = ((0, 256),) + CHUNKS[2:]
 TWO_ENGINES = 3
 QUARTER_BANKS = {
     ("co", 2): (4, 5),
-    ("co", 3): (6, 2),
     ("si", 0): (0, 1, 2, 3),
     ("si", 1): (4, 5),
     ("si", 2): (7, 6),
-    ("si", 3): (0, 1),
 }
-Y_BANKS = ((3, 3), (4, 4), (5, 5), (6, 7), (0, 1))
+TURNED_BANKS = {"co": (6, 2), "si": (0, 1), "power": (3, 4)}
+Y_BANKS = ((5, 5), (6, 6), (7, 7), (2, 0), (1, 3))
 
 
 def tile_list_meltab_norm_kernel(
@@ -172,6 +172,41 @@ def tile_list_meltab_norm_kernel(
                 quarter_pass(name, 1, q, t, True)
                 quarter_pass(name, 0, q, t, False)
 
+        def turned_sums(name, b):
+            acc[name, "turned", b] = bank(TURNED_BANKS[name][b], "%s_turned%d" % (name, b))
+            j0 = 3 * QUARTER + P * b
+            for a in (1, 0):
+                for g in (1, 0):
+                    nc.tensor.matmul_mx(
+                        acc[name, "turned", b][:, QUARTER * g : QUARTER * (g + 1)],
+                        lhsT=parted[1][:, a, j0 - HALF : j0 - HALF + P].bitcast(FP4X4),
+                        lhsT_scale=planes[:].bitcast(U8)[:, a * J + j0 : a * J + j0 + P],
+                        rhs=codes[name, a, g][:].bitcast(FP8X4),
+                        rhs_scale=scales[name, a, g][:],
+                        start=a == 1 and g == 1,
+                        stop=a == 0 and g == 0,
+                    )
+
+        identity = sb("identity", [P, P], F32)
+        make_identity(nc, identity[:])
+        sq_turned = {(name, b): sb("sq_turned_%s%d" % (name, b), [P, HALF], F32) for name in ("co", "si") for b in range(2)}
+
+        def square_turned(name, b):
+            nc.scalar.activation(sq_turned[name, b][:], acc[name, "turned", b][:], ACT.Square)
+
+        def turn(name, b):
+            if name == "co":
+                acc["power", b] = bank(TURNED_BANKS["power"][b], "power_turned%d" % b)
+            for t in range(PACK):
+                nc.tensor.matmul(
+                    acc["power", b][:, P * t : P * (t + 1)],
+                    lhsT=sq_turned[name, b][:, P * t : P * (t + 1)],
+                    rhs=identity[:],
+                    is_transpose=True,
+                    start=name == "co" and t == 0,
+                    stop=name == "si" and t == PACK - 1,
+                )
+
         sgn = sb("sgn", [P, PACK], BF16)
         mag = sb("mag", [P, PACK], F32)
         root = sb("root", [P, PACK], F32)
@@ -181,9 +216,9 @@ def tile_list_meltab_norm_kernel(
         shift = sb("shift", [P, 2], F32)
         nc.vector.scalar_tensor_tensor(shift[:], mean[:], -1.0, rdev[:], ALU.mult, ALU.mult)
 
-        re_ranges = ((0, HALF), (HALF, HALF + QUARTER), (HALF + QUARTER, J))
+        re_ranges = ((0, HALF), (HALF, HALF + QUARTER))
         sq_re = [sb("sq_re%d" % j0, [P, PACK, j1 - j0], F32) for j0, j1 in re_ranges]
-        sq_im = [sb("sq_im%d" % j0, [P, PACK, j1 - j0], F32) for j0, j1 in CHUNKS]
+        sq_im = [sb("sq_im%d" % j0, [P, PACK, j1 - j0], F32) for j0, j1 in CHUNKS[:4]]
 
         def square(dst, src, t):
             nc.scalar.activation(dst, src, ACT.Square, scale=root[:, t : t + 1])
@@ -218,13 +253,13 @@ def tile_list_meltab_norm_kernel(
             half_pass(t, 0, False)
         part(1)
         whole_sums("co", 2, range(PACK))
-        whole_sums("co", 3, (0, 1))
+        turned_sums("co", 0)
 
         cast_on_vector("si", 0, slice(0, P))
         for t in range(PACK):
             square(sq_re[0][:, t, :], acc["half", t][:], t)
         square_re(2, range(PACK))
-        square_re(3, (0, 1))
+        square_turned("co", 0)
         for g in range(2):
             quantise("si", 0, 2 * g, 2 * g + 2)
             for t in (2 * g, 2 * g + 1):
@@ -237,7 +272,7 @@ def tile_list_meltab_norm_kernel(
             whole_sums("si", q, (2, 1, 3, 0))
 
         widths = [j1 - j0 for j0, j1 in CHUNKS]
-        power = [sb("power%d" % c, [P, w, PACK], BF16) for c, w in enumerate(widths)]
+        power = [sb("power%d" % c, [P, w, PACK], BF16) for c, w in enumerate(widths[:4])]
         signed = [sb("signed%d" % c, [P, w, PACK], BF16) for c, w in enumerate(widths)]
         h_codes = [sb("h_codes%d" % c, [P, w], U32) for c, w in enumerate(widths)]
         h_scales = [sb("h_scales%d" % c, [P, w], U8) for c, w in enumerate(widths)]
@@ -257,6 +292,14 @@ def tile_list_meltab_norm_kernel(
         def sign(c):
             signs = sgn[:].unsqueeze(1).to_broadcast([P, widths[c], PACK])
             nc.vector.tensor_tensor(signed[c][:], power[c][:], signs, ALU.mult)
+
+        def weigh(b):
+            nc.vector.tensor_tensor(
+                signed[4 + b][:],
+                acc["power", b][:].rearrange("p (t j) -> p j t", t=PACK),
+                gain[:].unsqueeze(1).to_broadcast([P, P, PACK]),
+                ALU.mult,
+            )
 
         def y_sums(s, u):
             b = Y_BANKS[s][u]
@@ -300,16 +343,22 @@ def tile_list_meltab_norm_kernel(
 
         square_im(0)
         square_im(1)
-        whole_sums("co", 3, (2, 3))
-        whole_sums("si", 3, range(PACK))
+        turned_sums("si", 0)
+        turned_sums("co", 1)
+        turned_sums("si", 1)
+        turn("co", 0)
         square_im(2)
         square_im(3)
+        square_turned("si", 0)
+        turn("si", 0)
+        for name in ("co", "si"):
+            square_turned(name, 1)
+            turn(name, 1)
         pair_of_chunks(0)
         finish(0)
         pair_of_chunks(2)
-        square_re(3, (2, 3))
-        square_im(4)
-        square_im(5)
-        pair_of_chunks(4)
+        for stage in (weigh, lambda b: quantise_and_filter(4 + b)):
+            stage(0)
+            stage(1)
         for s in range(1, len(STORES)):
             finish(s)

@@ -26,16 +26,13 @@ QUARTER = 256
 HEAD = 1024
 CO0_ON_SCALAR = 76
 CHUNKS = ((0, 128), (128, 256), (256, 512), (512, 768), (768, 896), (896, 1024))
+DIRECT = 4
 STORES = ((0, 256),) + CHUNKS[2:]
+BY_GROUP = (1, 2)
 TWO_ENGINES = 3
-QUARTER_BANKS = {
-    ("co", 2): (4, 5),
-    ("si", 0): (0, 1, 2, 3),
-    ("si", 1): (4, 5),
-    ("si", 2): (7, 6),
-}
+QUARTER_BANKS = {("co", 2): (4, 5), ("si", 0): (0, 1, 2, 3), ("si", 1): (4, 5), ("si", 2): (7, 6)}
 TURNED_BANKS = {"co": (6, 2), "si": (0, 1), "power": (3, 4)}
-Y_BANKS = ((5, 5), (6, 6), (7, 7), (2, 0), (1, 3))
+Y_BANKS = ((5, 5), (6, 0), (7, 1), (2, 5), (3, 4))
 
 
 def tile_list_meltab_norm_kernel(
@@ -174,7 +171,7 @@ def tile_list_meltab_norm_kernel(
 
         def turned_sums(name, b):
             acc[name, "turned", b] = bank(TURNED_BANKS[name][b], "%s_turned%d" % (name, b))
-            j0 = 3 * QUARTER + P * b
+            j0 = CHUNKS[DIRECT + b][0]
             for a in (1, 0):
                 for g in (1, 0):
                     nc.tensor.matmul_mx(
@@ -189,7 +186,10 @@ def tile_list_meltab_norm_kernel(
 
         identity = sb("identity", [P, P], F32)
         make_identity(nc, identity[:])
-        sq_turned = {(name, b): sb("sq_turned_%s%d" % (name, b), [P, HALF], F32) for name in ("co", "si") for b in range(2)}
+        sq_turned = {}
+        for name in ("co", "si"):
+            for b in range(2):
+                sq_turned[name, b] = sb("sq_turned_%s%d" % (name, b), [P, HALF], F32)
 
         def square_turned(name, b):
             nc.scalar.activation(sq_turned[name, b][:], acc[name, "turned", b][:], ACT.Square)
@@ -218,14 +218,10 @@ def tile_list_meltab_norm_kernel(
 
         re_ranges = ((0, HALF), (HALF, HALF + QUARTER))
         sq_re = [sb("sq_re%d" % j0, [P, PACK, j1 - j0], F32) for j0, j1 in re_ranges]
-        sq_im = [sb("sq_im%d" % j0, [P, PACK, j1 - j0], F32) for j0, j1 in CHUNKS[:4]]
+        sq_im = [sb("sq_im%d" % j0, [P, PACK, j1 - j0], F32) for j0, j1 in CHUNKS[:DIRECT]]
 
         def square(dst, src, t):
             nc.scalar.activation(dst, src, ACT.Square, scale=root[:, t : t + 1])
-
-        def square_re(q, classes):
-            for t in classes:
-                square(sq_re[q - 1][:, t, :], quarter_sums("co", q, t), t)
 
         def square_im(c):
             j0, j1 = CHUNKS[c]
@@ -258,7 +254,8 @@ def tile_list_meltab_norm_kernel(
         cast_on_vector("si", 0, slice(0, P))
         for t in range(PACK):
             square(sq_re[0][:, t, :], acc["half", t][:], t)
-        square_re(2, range(PACK))
+        for t in range(PACK):
+            square(sq_re[1][:, t, :], quarter_sums("co", 2, t), t)
         square_turned("co", 0)
         for g in range(2):
             quantise("si", 0, 2 * g, 2 * g + 2)
@@ -272,7 +269,7 @@ def tile_list_meltab_norm_kernel(
             whole_sums("si", q, (2, 1, 3, 0))
 
         widths = [j1 - j0 for j0, j1 in CHUNKS]
-        power = [sb("power%d" % c, [P, w, PACK], BF16) for c, w in enumerate(widths[:4])]
+        power = [sb("power%d" % c, [P, w, PACK], BF16) for c, w in enumerate(widths[:DIRECT])]
         signed = [sb("signed%d" % c, [P, w, PACK], BF16) for c, w in enumerate(widths)]
         h_codes = [sb("h_codes%d" % c, [P, w], U32) for c, w in enumerate(widths)]
         h_scales = [sb("h_scales%d" % c, [P, w], U8) for c, w in enumerate(widths)]
@@ -295,7 +292,7 @@ def tile_list_meltab_norm_kernel(
 
         def weigh(b):
             nc.vector.tensor_tensor(
-                signed[4 + b][:],
+                signed[DIRECT + b][:],
                 acc["power", b][:].rearrange("p (t j) -> p j t", t=PACK),
                 gain[:].unsqueeze(1).to_broadcast([P, P, PACK]),
                 ALU.mult,
@@ -339,7 +336,10 @@ def tile_list_meltab_norm_kernel(
                     nc.vector.tensor_scalar(result[s][:, u, :], y_sums(s, u), scale, bias, ALU.mult, ALU.add)
                 else:
                     nc.scalar.activation(result[s][:, u, :], y_sums(s, u), ACT.Identity, bias=bias, scale=scale)
-            nc.sync.dma_start(out_rows[:, :, STORES[s][0] : STORES[s][1]], result[s][:])
+                if s in BY_GROUP:
+                    nc.sync.dma_start(out_rows[:, u, STORES[s][0] : STORES[s][1]], result[s][:, u, :])
+            if s not in BY_GROUP:
+                nc.sync.dma_start(out_rows[:, :, STORES[s][0] : STORES[s][1]], result[s][:])
 
         square_im(0)
         square_im(1)
@@ -357,8 +357,9 @@ def tile_list_meltab_norm_kernel(
         pair_of_chunks(0)
         finish(0)
         pair_of_chunks(2)
-        for stage in (weigh, lambda b: quantise_and_filter(4 + b)):
-            stage(0)
-            stage(1)
+        for b in range(2):
+            weigh(b)
+        for b in range(2):
+            quantise_and_filter(DIRECT + b)
         for s in range(1, len(STORES)):
             finish(s)

@@ -24,7 +24,7 @@ PASSES = K // K_PASS
 HALF = 512
 QUARTER = 256
 HEAD = 1024
-CO0_ON_SCALAR = 76
+GROUPS = F // PACK // 2
 CHUNKS = ((0, 128), (128, 256), (256, 512), (512, 768), (768, 896), (896, 1024))
 DIRECT = 4
 STORES = ((0, 256),) + CHUNKS[2:]
@@ -66,9 +66,10 @@ def tile_list_meltab_norm_kernel(
 
         def load_weight(name, a):
             w = co if name == "co" else si
-            raw[name, a] = sb("raw_%s%d" % (name, a), [P, PACK, F], F32)
-            rows = w[K_PASS * a : K_PASS * (a + 1), :].rearrange("(p i) f -> p i f", i=PACK)
-            nc.sync.dma_start(raw[name, a][:], rows)
+            for h in range(2):
+                raw[name, a, h] = sb("raw_%s%d%d" % (name, a, h), [P, PACK, F // 2], F32)
+                rows = w[K_PASS * a : K_PASS * (a + 1), F // 2 * h : F // 2 * (h + 1)]
+                nc.sync.dma_start(raw[name, a, h][:], rows.rearrange("(p i) f -> p i f", i=PACK))
 
         planes = sb("planes", [P, PASSES * J // 4], I32)
         nc.vector.memset(planes[:], 0)
@@ -96,20 +97,36 @@ def tile_list_meltab_norm_kernel(
             nc.sync.dma_start(fb_plane[r:P:32, :], fb_rows[r])
 
         grouped, codes, scales = {}, {}, {}
-        for name, a in raw:
-            grouped[name, a] = sb("grouped_%s%d" % (name, a), [P, PACK, P, PACK], BF16)
-            for g in range(2):
-                codes[name, a, g] = sb("codes_%s%d%d" % (name, a, g), [P, 2 * P], U32)
-                scales[name, a, g] = sb("scales_%s%d%d" % (name, a, g), [P, 2 * P], U8)
+        for name in ("co", "si"):
+            for a in range(PASSES):
+                if name == "co":
+                    whole = sb("grouped_co%d" % a, [P, PACK, P, PACK], BF16)
+                    grouped[name, a] = whole
+                    for h in range(2):
+                        grouped[name, a, h] = whole[:, :, GROUPS * h : GROUPS * (h + 1), :]
+                else:
+                    for h in range(2):
+                        grouped[name, a, h] = sb("grouped_si%d%d" % (a, h), [P, PACK, GROUPS, PACK], BF16)[:]
+                for g in range(2):
+                    codes[name, a, g] = sb("codes_%s%d%d" % (name, a, g), [P, 2 * P], U32)
+                    scales[name, a, g] = sb("scales_%s%d%d" % (name, a, g), [P, 2 * P], U8)
 
-        def cast(copy, name, a, groups, classes):
-            src = raw[name, a][:].rearrange("p i (m t) -> p m i t", t=PACK)
-            dst = grouped[name, a][:].rearrange("p t m i -> p m i t")
-            copy(dst[:, groups, :, classes], src[:, groups, :, classes])
+        def cast(copy, name, a, h, classes):
+            src = raw[name, a, h][:].rearrange("p i (m t) -> p m i t", t=PACK)
+            dst = grouped[name, a, h].rearrange("p t m i -> p m i t")
+            copy(dst[:, :, :, classes], src[:, :, :, classes])
 
-        def cast_on_vector(name, a, groups):
+        def cast_on_vector(name, a, h):
             for g in range(2):
-                cast(nc.vector.tensor_copy, name, a, groups, slice(2 * g, 2 * g + 2))
+                cast(nc.vector.tensor_copy, name, a, h, slice(2 * g, 2 * g + 2))
+
+        def quantise_half(name, a, h, t):
+            cols = slice(P * (t % 2) + GROUPS * h, P * (t % 2) + GROUPS * (h + 1))
+            nc.vector.quantize_mx(
+                out=codes[name, a, t // 2][:, cols].bitcast(FP8X4),
+                scales=scales[name, a, t // 2][:, cols],
+                in_=grouped[name, a, h][:, t].rearrange("p m i -> p (m i)"),
+            )
 
         def quantise(name, a, t0, t1):
             cols = slice(P * (t0 % 2), P * (t0 % 2 + t1 - t0))
@@ -127,7 +144,7 @@ def tile_list_meltab_norm_kernel(
             nc.vector.tensor_copy(picked[h][:], tab[:].bitcast(U32).indirect(offsets[:, cols]))
 
         def part(h):
-            parted[h] = sb("parted%d" % h, [P, PASSES, HALF], U16, "grouped_co1" if h else None)
+            parted[h] = sb("parted%d" % h, [P, PASSES, HALF], U16, "grouped_co0" if h else None)
             nc.vector.tensor_copy(parted[h][:], picked[h][:].bitcast(U16).rearrange("p (j a) -> p a j", a=PASSES))
 
         def transform(dst, name, a, t, j0, j1, first):
@@ -232,14 +249,16 @@ def tile_list_meltab_norm_kernel(
         for h in range(2):
             gather(h)
         part(0)
-        cast(nc.scalar.copy, "co", 0, slice(0, CO0_ON_SCALAR), slice(0, PACK))
-        cast_on_vector("co", 0, slice(CO0_ON_SCALAR, P))
+        for h in range(2):
+            cast(nc.scalar.copy, "co", 0, h, slice(0, PACK))
         for g in range(2):
             quantise("co", 0, 2 * g, 2 * g + 2)
+        part(1)
         for t in range(2):
             half_pass(t, 0, True)
-        cast(nc.vector.tensor_copy, "co", 1, slice(0, P), slice(0, 2))
-        cast(nc.scalar.copy, "co", 1, slice(0, P), slice(2, PACK))
+        cast(nc.scalar.copy, "co", 1, 0, slice(0, PACK))
+        cast(nc.vector.tensor_copy, "co", 1, 1, slice(0, 2))
+        cast(nc.scalar.copy, "co", 1, 1, slice(2, PACK))
         for t in range(2):
             quantise("co", 1, t, t + 1)
             half_pass(t, 1, False)
@@ -247,23 +266,26 @@ def tile_list_meltab_norm_kernel(
         for t in range(2, PACK):
             half_pass(t, 1, True)
             half_pass(t, 0, False)
-        part(1)
         whole_sums("co", 2, range(PACK))
         turned_sums("co", 0)
 
-        cast_on_vector("si", 0, slice(0, P))
+        for h in range(2):
+            cast_on_vector("si", 0, h)
+            for t in range(PACK):
+                quantise_half("si", 0, h, t)
         for t in range(PACK):
             square(sq_re[0][:, t, :], acc["half", t][:], t)
         for t in range(PACK):
             square(sq_re[1][:, t, :], quarter_sums("co", 2, t), t)
         square_turned("co", 0)
-        for g in range(2):
-            quantise("si", 0, 2 * g, 2 * g + 2)
-            for t in (2 * g, 2 * g + 1):
-                quarter_pass("si", 0, 0, t, True)
-        cast_on_vector("si", 1, slice(0, P))
         for t in range(PACK):
-            quantise("si", 1, t, t + 1)
+            quarter_pass("si", 0, 0, t, True)
+        cast_on_vector("si", 1, 0)
+        for t in range(PACK):
+            quantise_half("si", 1, 0, t)
+        cast_on_vector("si", 1, 1)
+        for t in range(PACK):
+            quantise_half("si", 1, 1, t)
             quarter_pass("si", 1, 0, t, False)
         for q in (1, 2):
             whole_sums("si", q, (2, 1, 3, 0))

@@ -23,16 +23,20 @@ K_PASS = P * PACK
 PASSES = K // K_PASS
 HALF = 512
 QUARTER = 256
+PIECES = ((0, 512), (512, 768), (768, 1024))
 HEAD = 1024
 GROUPS = F // PACK // 2
-CHUNKS = ((0, 128), (128, 256), (256, 512), (512, 768), (768, 896), (896, 1024))
+CHUNKS = ((0, 128), (128, 256), (256, 512), (512, 640), (640, 768), (768, 896), (896, 1024))
+TURNED = 3
 DIRECT = 4
-STORES = ((0, 256),) + CHUNKS[2:]
-BY_GROUP = (1, 2)
+STORES = ((0, 256), (256, 640), (640, 768), (768, 896), (896, 1024))
+STORE_OF = (0, 0, 1, 1, 2, 3, 4)
+BY_GROUP = (1,)
 TWO_ENGINES = 3
-QUARTER_BANKS = {("co", 2): (4, 5), ("si", 0): (0, 1, 2, 3), ("si", 1): (4, 5), ("si", 2): (7, 6)}
-TURNED_BANKS = {"co": (6, 2), "si": (0, 1), "power": (3, 4)}
-Y_BANKS = ((5, 5), (6, 0), (7, 1), (2, 5), (3, 4))
+QUARTER_BANKS = {("si", 1): (5, 0)}
+ONE_BANK = {("co", 3): 4, ("si", 1): 4, ("si", 3): 1}
+TURNED_BANKS = {"co": (5, 6, 7), "si": (6, 2, 3), "power": (4, 5, 0)}
+Y_BANKS = ((7, 7), (1, 6), (2, 3), (7, 4), (1, 5))
 
 
 def tile_list_meltab_norm_kernel(
@@ -42,6 +46,7 @@ def tile_list_meltab_norm_kernel(
     with ExitStack() as ctx:
         keep = ctx.enter_context(tc.tile_pool(name="keep", bufs=1))
         psum = ctx.enter_context(tc.psum_pool(name="psum", bufs=1))
+        shared = ctx.enter_context(tc.tile_pool(name="shared", bufs=1))
 
         def sb(name, shape, dtype, tag=None):
             return keep.tile(shape, dtype, name=name, tag=tag or name, align_bytes=64)
@@ -99,17 +104,19 @@ def tile_list_meltab_norm_kernel(
         grouped, codes, scales = {}, {}, {}
         for name in ("co", "si"):
             for a in range(PASSES):
-                if name == "co":
-                    whole = sb("grouped_co%d" % a, [P, PACK, P, PACK], BF16)
+                if (name, a) != ("si", 1):
+                    at = 4096 * (a if name == "co" else 2)
+                    whole = shared.tile(
+                        [P, PACK, P, PACK], BF16, name="grouped_%s%d" % (name, a), align_bytes=64, offset=at
+                    )
                     grouped[name, a] = whole
                     for h in range(2):
                         grouped[name, a, h] = whole[:, :, GROUPS * h : GROUPS * (h + 1), :]
                 else:
                     for h in range(2):
                         grouped[name, a, h] = sb("grouped_si%d%d" % (a, h), [P, PACK, GROUPS, PACK], BF16)[:]
-                for g in range(2):
-                    codes[name, a, g] = sb("codes_%s%d%d" % (name, a, g), [P, 2 * P], U32)
-                    scales[name, a, g] = sb("scales_%s%d%d" % (name, a, g), [P, 2 * P], U8)
+                codes[name, a] = sb("codes_%s%d" % (name, a), [P, F], U32)
+                scales[name, a] = sb("scales_%s%d" % (name, a), [P, F], U8)
 
         def cast(copy, name, a, h, classes):
             src = raw[name, a, h][:].rearrange("p i (m t) -> p m i t", t=PACK)
@@ -121,43 +128,52 @@ def tile_list_meltab_norm_kernel(
                 cast(nc.vector.tensor_copy, name, a, h, slice(2 * g, 2 * g + 2))
 
         def quantise_half(name, a, h, t):
-            cols = slice(P * (t % 2) + GROUPS * h, P * (t % 2) + GROUPS * (h + 1))
+            cols = slice(P * t + GROUPS * h, P * t + GROUPS * (h + 1))
             nc.vector.quantize_mx(
-                out=codes[name, a, t // 2][:, cols].bitcast(FP8X4),
-                scales=scales[name, a, t // 2][:, cols],
+                out=codes[name, a][:, cols].bitcast(FP8X4),
+                scales=scales[name, a][:, cols],
                 in_=grouped[name, a, h][:, t].rearrange("p m i -> p (m i)"),
             )
 
         def quantise(name, a, t0, t1):
-            cols = slice(P * (t0 % 2), P * (t0 % 2 + t1 - t0))
+            cols = slice(P * t0, P * t1)
             nc.vector.quantize_mx(
-                out=codes[name, a, t0 // 2][:, cols].bitcast(FP8X4),
-                scales=scales[name, a, t0 // 2][:, cols],
+                out=codes[name, a][:, cols].bitcast(FP8X4),
+                scales=scales[name, a][:, cols],
                 in_=grouped[name, a][:, t0:t1].rearrange("p t m i -> p (t m i)"),
             )
 
         picked, parted = {}, {}
 
         def gather(h):
-            picked[h] = sb("picked%d" % h, [P, HALF], U32)
-            cols = slice(h * HALF // 16, (h + 1) * HALF // 16)
-            nc.vector.tensor_copy(picked[h][:], tab[:].bitcast(U32).indirect(offsets[:, cols]))
+            j0, j1 = PIECES[h]
+            if h < 2:
+                picked[h] = sb("picked%d" % h, [P, j1 - j0], U32)
+            else:
+                picked[h] = shared.tile([P, j1 - j0], U32, name="picked2", align_bytes=64, offset=0)
+            nc.vector.tensor_copy(picked[h][:], tab[:].bitcast(U32).indirect(offsets[:, j0 // 16 : j1 // 16]))
 
         def part(h):
-            parted[h] = sb("parted%d" % h, [P, PASSES, HALF], U16, "grouped_co0" if h else None)
+            j0, j1 = PIECES[h]
+            if h == 0:
+                parted[h] = sb("parted0", [P, PASSES, j1 - j0], U16)
+            else:
+                offset = 1024 if h == 1 else 4096
+                parted[h] = shared.tile([P, PASSES, j1 - j0], U16, name="parted%d" % h, align_bytes=64, offset=offset)
             nc.vector.tensor_copy(parted[h][:], picked[h][:].bitcast(U16).rearrange("p (j a) -> p a j", a=PASSES))
 
-        def transform(dst, name, a, t, j0, j1, first):
+        def transform(dst, name, a, t, j0, j1, first, last):
             h = j0 // HALF
-            cols = slice(P * (t % 2), P * (t % 2 + 1))
+            first_frame = PIECES[h][0]
+            cols = slice(P * t, P * (t + 1))
             nc.tensor.matmul_mx(
                 dst,
-                lhsT=codes[name, a, t // 2][:, cols].bitcast(FP8X4),
-                lhsT_scale=scales[name, a, t // 2][:, cols],
-                rhs=parted[h][:, a, j0 - h * HALF : j1 - h * HALF].bitcast(FP4X4),
+                lhsT=codes[name, a][:, cols].bitcast(FP8X4),
+                lhsT_scale=scales[name, a][:, cols],
+                rhs=parted[h][:, a, j0 - first_frame : j1 - first_frame].bitcast(FP4X4),
                 rhs_scale=planes[:].bitcast(U8)[:, a * J + j0 : a * J + j1],
                 start=first,
-                stop=not first,
+                stop=last,
             )
 
         acc = {}
@@ -165,48 +181,68 @@ def tile_list_meltab_norm_kernel(
         def half_pass(t, a, first):
             if first:
                 acc["half", t] = bank(t, "re_half%d" % t)
-            transform(acc["half", t][:], "co", a, t, 0, HALF, first)
+            transform(acc["half", t][:], "co", a, t, 0, HALF, first, not first)
 
         def quarter_sums(name, q, t):
-            if name == "co":
-                g, side = t // 2, t % 2
-            elif q == 0:
-                g, side = t, 0
-            else:
-                g, side = min(t, 3 - t), t // 2
+            g, side = min(t, 3 - t), t // 2
             if (name, q, g) not in acc:
                 acc[name, q, g] = bank(QUARTER_BANKS[name, q][g], "%s%d%d" % (name, q, g))
             return acc[name, q, g][:, QUARTER * side : QUARTER * (side + 1)]
 
         def quarter_pass(name, a, q, t, first):
-            transform(quarter_sums(name, q, t), name, a, t, QUARTER * q, QUARTER * (q + 1), first)
+            transform(quarter_sums(name, q, t), name, a, t, QUARTER * q, QUARTER * (q + 1), first, not first)
+
+        def short_sums(name, c, t):
+            b = ONE_BANK[name, c] if c else t
+            if (name, c, b) not in acc:
+                acc[name, c, b] = bank(b, "%s_short%d%d" % (name, c, b))
+            return acc[name, c, b][:, P * t : P * (t + 1)]
+
+        def short_pass(c, a, t, first, last, name="si"):
+            transform(short_sums(name, c, t), name, a, t, CHUNKS[c][0], CHUNKS[c][1], first, last)
+
+        def short_group(name, c):
+            for a in (1, 0):
+                for t in reversed(range(PACK)):
+                    short_pass(c, a, t, a == 1 and t == PACK - 1, a == 0 and t == 0, name)
 
         def whole_sums(name, q, classes):
             for t in classes:
                 quarter_pass(name, 1, q, t, True)
                 quarter_pass(name, 0, q, t, False)
 
-        def turned_sums(name, b):
-            acc[name, "turned", b] = bank(TURNED_BANKS[name][b], "%s_turned%d" % (name, b))
+        def turned_pass(name, b, a, first):
+            if first:
+                acc[name, "turned", b] = bank(TURNED_BANKS[name][b], "%s_turned%d" % (name, b))
             j0 = CHUNKS[DIRECT + b][0]
-            for a in (1, 0):
-                for g in (1, 0):
-                    nc.tensor.matmul_mx(
-                        acc[name, "turned", b][:, QUARTER * g : QUARTER * (g + 1)],
-                        lhsT=parted[1][:, a, j0 - HALF : j0 - HALF + P].bitcast(FP4X4),
-                        lhsT_scale=planes[:].bitcast(U8)[:, a * J + j0 : a * J + j0 + P],
-                        rhs=codes[name, a, g][:].bitcast(FP8X4),
-                        rhs_scale=scales[name, a, g][:],
-                        start=a == 1 and g == 1,
-                        stop=a == 0 and g == 0,
-                    )
+            nc.tensor.matmul_mx(
+                acc[name, "turned", b][:],
+                lhsT=parted[j0 // QUARTER - 1][:, a, j0 % QUARTER : j0 % QUARTER + P].bitcast(FP4X4),
+                lhsT_scale=planes[:].bitcast(U8)[:, a * J + j0 : a * J + j0 + P],
+                rhs=codes[name, a][:].bitcast(FP8X4),
+                rhs_scale=scales[name, a][:],
+                start=first,
+                stop=not first,
+            )
+
+        def turned_sums(name, b):
+            turned_pass(name, b, 1, True)
+            turned_pass(name, b, 0, False)
 
         identity = sb("identity", [P, P], F32)
         make_identity(nc, identity[:])
         sq_turned = {}
         for name in ("co", "si"):
-            for b in range(2):
+            for b in range(TURNED):
                 sq_turned[name, b] = sb("sq_turned_%s%d" % (name, b), [P, HALF], F32)
+
+        def square_on_vector(name, b):
+            twin = sb("twin", [P, HALF], F32, "grouped_si11")
+            halves = [slice(QUARTER * g, QUARTER * (g + 1)) for g in range(2)]
+            for cols in halves:
+                nc.vector.tensor_copy(twin[:, cols], acc[name, "turned", b][:, cols])
+            for cols in halves:
+                nc.vector.tensor_tensor(sq_turned[name, b][:, cols], acc[name, "turned", b][:, cols], twin[:, cols], ALU.mult)
 
         def square_turned(name, b):
             nc.scalar.activation(sq_turned[name, b][:], acc[name, "turned", b][:], ACT.Square)
@@ -233,7 +269,7 @@ def tile_list_meltab_norm_kernel(
         shift = sb("shift", [P, 2], F32)
         nc.vector.scalar_tensor_tensor(shift[:], mean[:], -1.0, rdev[:], ALU.mult, ALU.mult)
 
-        re_ranges = ((0, HALF), (HALF, HALF + QUARTER))
+        re_ranges = ((0, HALF), CHUNKS[3])
         sq_re = [sb("sq_re%d" % j0, [P, PACK, j1 - j0], F32) for j0, j1 in re_ranges]
         sq_im = [sb("sq_im%d" % j0, [P, PACK, j1 - j0], F32) for j0, j1 in CHUNKS[:DIRECT]]
 
@@ -241,20 +277,21 @@ def tile_list_meltab_norm_kernel(
             nc.scalar.activation(dst, src, ACT.Square, scale=root[:, t : t + 1])
 
         def square_im(c):
-            j0, j1 = CHUNKS[c]
-            q = j0 // QUARTER
             for t in range(PACK):
-                square(sq_im[c][:, t, :], quarter_sums("si", q, t)[:, j0 - q * QUARTER : j1 - q * QUARTER], t)
+                square(sq_im[c][:, t, :], quarter_sums("si", 1, t) if c == 2 else short_sums("si", c, t), t)
 
         for h in range(2):
             gather(h)
         part(0)
-        for h in range(2):
-            cast(nc.scalar.copy, "co", 0, h, slice(0, PACK))
-        for g in range(2):
-            quantise("co", 0, 2 * g, 2 * g + 2)
-        part(1)
+        cast(nc.scalar.copy, "co", 0, 0, slice(0, PACK))
+        cast(nc.vector.tensor_copy, "co", 0, 1, slice(0, 2))
+        cast(nc.scalar.copy, "co", 0, 1, slice(2, PACK))
         for t in range(2):
+            quantise("co", 0, t, t + 1)
+        quantise("co", 0, 2, PACK)
+        part(1)
+        gather(2)
+        for t in range(3):
             half_pass(t, 0, True)
         cast(nc.scalar.copy, "co", 1, 0, slice(0, PACK))
         cast(nc.vector.tensor_copy, "co", 1, 1, slice(0, 2))
@@ -263,32 +300,44 @@ def tile_list_meltab_norm_kernel(
             quantise("co", 1, t, t + 1)
             half_pass(t, 1, False)
         quantise("co", 1, 2, PACK)
-        for t in range(2, PACK):
-            half_pass(t, 1, True)
-            half_pass(t, 0, False)
-        whole_sums("co", 2, range(PACK))
-        turned_sums("co", 0)
+        half_pass(2, 1, False)
+        half_pass(3, 1, True)
+        half_pass(3, 0, False)
+        part(2)
+        short_group("co", 3)
+        for b in range(TURNED):
+            turned_sums("co", b)
 
         for h in range(2):
             cast_on_vector("si", 0, h)
-            for t in range(PACK):
-                quantise_half("si", 0, h, t)
+        for g in range(2):
+            quantise("si", 0, 2 * g, 2 * g + 2)
         for t in range(PACK):
             square(sq_re[0][:, t, :], acc["half", t][:], t)
         for t in range(PACK):
-            square(sq_re[1][:, t, :], quarter_sums("co", 2, t), t)
-        square_turned("co", 0)
+            square(sq_re[1][:, t, :], short_sums("co", 3, t), t)
+        for b in range(TURNED - 1):
+            square_turned("co", b)
         for t in range(PACK):
-            quarter_pass("si", 0, 0, t, True)
+            short_pass(0, 0, t, True, False)
+        for t in range(PACK):
+            short_pass(1, 0, t, t == 0, False)
+        for t in (0, 3):
+            transform(quarter_sums("si", 1, t), "si", 0, t, QUARTER, HALF, t == 0, False)
         cast_on_vector("si", 1, 0)
         for t in range(PACK):
             quantise_half("si", 1, 0, t)
         cast_on_vector("si", 1, 1)
         for t in range(PACK):
             quantise_half("si", 1, 1, t)
-            quarter_pass("si", 1, 0, t, False)
-        for q in (1, 2):
-            whole_sums("si", q, (2, 1, 3, 0))
+            short_pass(0, 1, t, False, True)
+        square_on_vector("co", TURNED - 1)
+        for t in reversed(range(PACK)):
+            short_pass(1, 1, t, False, t == 0)
+        for t in (3, 0):
+            transform(quarter_sums("si", 1, t), "si", 1, t, QUARTER, HALF, False, t == 0)
+        whole_sums("si", 1, (2, 1))
+        short_group("si", 3)
 
         widths = [j1 - j0 for j0, j1 in CHUNKS]
         power = [sb("power%d" % c, [P, w, PACK], BF16) for c, w in enumerate(widths[:DIRECT])]
@@ -325,7 +374,8 @@ def tile_list_meltab_norm_kernel(
             if ("y", s, b) not in acc:
                 acc["y", s, b] = bank(b, "y%d%d" % (s, u))
             width = STORES[s][1] - STORES[s][0]
-            return acc["y", s, b][:, width * u : width * (u + 1)]
+            side = u if Y_BANKS[s][0] == Y_BANKS[s][1] else 0
+            return acc["y", s, b][:, width * side : width * (side + 1)]
 
         def quantise_and_filter(c):
             nc.vector.quantize_mx(
@@ -333,7 +383,7 @@ def tile_list_meltab_norm_kernel(
                 scales=h_scales[c][:],
                 in_=signed[c][:].rearrange("p j t -> p (j t)"),
             )
-            s = max(0, c - 1)
+            s = STORE_OF[c]
             j0, j1 = CHUNKS[c]
             for u in range(2):
                 nc.tensor.matmul_mx(
@@ -365,23 +415,22 @@ def tile_list_meltab_norm_kernel(
 
         square_im(0)
         square_im(1)
-        turned_sums("si", 0)
-        turned_sums("co", 1)
-        turned_sums("si", 1)
-        turn("co", 0)
+        for b in range(TURNED):
+            turned_sums("si", b)
         square_im(2)
         square_im(3)
-        square_turned("si", 0)
-        turn("si", 0)
-        for name in ("co", "si"):
-            square_turned(name, 1)
-            turn(name, 1)
         pair_of_chunks(0)
+        for b in range(TURNED):
+            turn("co", b)
+        for b in range(TURNED):
+            square_turned("si", b)
+            turn("si", b)
         finish(0)
         pair_of_chunks(2)
-        for b in range(2):
+        weigh(0)
+        for b in range(1, TURNED):
             weigh(b)
-        for b in range(2):
-            quantise_and_filter(DIRECT + b)
+            quantise_and_filter(DIRECT + b - 1)
+        quantise_and_filter(DIRECT + TURNED - 1)
         for s in range(1, len(STORES)):
             finish(s)

@@ -24,7 +24,7 @@ PASSES = K // K_PASS
 HALF = 512
 QUARTER = 256
 PIECES = ((0, 512), (512, 768), (768, 1024))
-HEAD = 1024
+HEAD = 1536
 GROUPS = F // PACK // 2
 CHUNKS = ((0, 128), (128, 256), (256, 512), (512, 640), (640, 768), (768, 896), (896, 1024))
 TURNED = 3

@@ -88,11 +88,6 @@ def tile_list_meltab_norm_kernel(
         for a in range(PASSES):
             load_weight("si", a)
 
-        mean = sb("mean", [P, 2], F32)
-        rdev = sb("rdev", [P, 2], F32)
-        with nc.allow_non_contiguous_dma(reason="one value a partition"):
-            nc.sync.dma_start(mean[:], mu.rearrange("(u p) -> p u", p=P))
-            nc.sync.dma_start(rdev[:], isd.rearrange("(u p) -> p u", p=P))
         fb_codes = sb("fb_codes", [P, 2 * N // 4], I32)
         nc.sync.dma_start(fb_codes[:], fb_words[0].bitcast(I32))
         fb_plane = sb("fb_plane", [P, N // 4], I32)
@@ -100,6 +95,11 @@ def tile_list_meltab_norm_kernel(
         fb_rows = fb_scales[0].bitcast(I32).rearrange("(q r) w -> r q w", r=4)
         for r in range(4):
             nc.sync.dma_start(fb_plane[r:P:32, :], fb_rows[r])
+        mean = sb("mean", [P, 2], F32)
+        rdev = sb("rdev", [P, 2], F32)
+        with nc.allow_non_contiguous_dma(reason="one value a partition"):
+            nc.sync.dma_start(mean[:], mu.rearrange("(u p) -> p u", p=P))
+            nc.sync.dma_start(rdev[:], isd.rearrange("(u p) -> p u", p=P))
 
         grouped, codes, scales = {}, {}, {}
         for name in ("co", "si"):
@@ -266,8 +266,6 @@ def tile_list_meltab_norm_kernel(
         nc.scalar.activation(mag[:], gain[:], ACT.Abs)
         nc.scalar.activation(sgn[:], gain[:], ACT.Sign)
         nc.scalar.activation(root[:], mag[:], ACT.Sqrt)
-        shift = sb("shift", [P, 2], F32)
-        nc.vector.scalar_tensor_tensor(shift[:], mean[:], -1.0, rdev[:], ALU.mult, ALU.mult)
 
         re_ranges = ((0, HALF), CHUNKS[3])
         sq_re = [sb("sq_re%d" % j0, [P, PACK, j1 - j0], F32) for j0, j1 in re_ranges]
@@ -425,8 +423,17 @@ def tile_list_meltab_norm_kernel(
         for b in range(TURNED):
             square_turned("si", b)
             turn("si", b)
+        add(2)
+        minus_mean = sb("minus_mean", [P, 2], F32, "sq_im256")
+        shift = sb("shift", [P, 2], F32)
+        nc.scalar.activation(minus_mean[:], mean[:], ACT.Copy, scale=-1.0)
+        for u in range(2):
+            nc.scalar.activation(shift[:, u : u + 1], minus_mean[:, u : u + 1], ACT.Copy, scale=rdev[:, u : u + 1])
         finish(0)
-        pair_of_chunks(2)
+        add(3)
+        for stage in (sign, quantise_and_filter):
+            stage(2)
+            stage(3)
         weigh(0)
         for b in range(1, TURNED):
             weigh(b)

@@ -49,7 +49,7 @@ def tile_list_meltab_norm_kernel(
         shared = ctx.enter_context(tc.tile_pool(name="shared", bufs=1))
 
         def sb(name, shape, dtype, tag=None):
-            return keep.tile(shape, dtype, name=name, tag=tag or name, align_bytes=64)
+            return keep.tile(shape, dtype, name=name, tag=tag or name, align_bytes=256)
 
         def bank(b, name):
             return psum.tile([P, HALF], F32, name=name, tag="bank%d" % b)
@@ -107,7 +107,7 @@ def tile_list_meltab_norm_kernel(
                 if (name, a) != ("si", 1):
                     at = 4096 * (a if name == "co" else 2)
                     whole = shared.tile(
-                        [P, PACK, P, PACK], BF16, name="grouped_%s%d" % (name, a), align_bytes=64, offset=at
+                        [P, PACK, P, PACK], BF16, name="grouped_%s%d" % (name, a), align_bytes=256, offset=at
                     )
                     grouped[name, a] = whole
                     for h in range(2):
@@ -150,7 +150,7 @@ def tile_list_meltab_norm_kernel(
             if h < 2:
                 picked[h] = sb("picked%d" % h, [P, j1 - j0], U32)
             else:
-                picked[h] = shared.tile([P, j1 - j0], U32, name="picked2", align_bytes=64, offset=0)
+                picked[h] = shared.tile([P, j1 - j0], U32, name="picked2", align_bytes=256, offset=0)
             nc.vector.tensor_copy(picked[h][:], tab[:].bitcast(U32).indirect(offsets[:, j0 // 16 : j1 // 16]))
 
         def part(h):
@@ -159,7 +159,7 @@ def tile_list_meltab_norm_kernel(
                 parted[h] = sb("parted0", [P, PASSES, j1 - j0], U16)
             else:
                 offset = 1024 if h == 1 else 4096
-                parted[h] = shared.tile([P, PASSES, j1 - j0], U16, name="parted%d" % h, align_bytes=64, offset=offset)
+                parted[h] = shared.tile([P, PASSES, j1 - j0], U16, name="parted%d" % h, align_bytes=256, offset=offset)
             nc.vector.tensor_copy(parted[h][:], picked[h][:].bitcast(U16).rearrange("p (j a) -> p a j", a=PASSES))
 
         def transform(dst, name, a, t, j0, j1, first, last):

from contextlib import ExitStack

import concourse.mybir as mybir
from concourse.masks import make_identity

K, F, N, T, J = 1024, 512, 256, 4096, 1024
FLOPS = 2 * (2 * K * F * J + F * N * J)

F32 = mybir.dt.float32
BF16 = mybir.dt.bfloat16
I32 = mybir.dt.int32
U32 = mybir.dt.uint32
U16 = mybir.dt.uint16
U8 = mybir.dt.uint8
FP8X4 = mybir.dt.float8_e4m3fn_x4
FP4X4 = mybir.dt.float4_e2m1fn_x4
ALU = mybir.AluOpType
ACT = mybir.ActivationFunctionType

P = 128
PACK = 4
K_PASS = P * PACK
PASSES = K // K_PASS
HALF = 512
QUARTER = 256
PIECES = ((0, 512), (512, 768), (768, 1024))
HEAD = 1536
GROUPS = F // PACK // 2
CHUNKS = ((0, 128), (128, 256), (256, 512), (512, 640), (640, 768), (768, 896), (896, 1024))
TURNED = 3
DIRECT = 4
STORES = ((0, 256), (256, 640), (640, 768), (768, 896), (896, 1024))
STORE_OF = (0, 0, 1, 1, 2, 3, 4)
BY_GROUP = (1,)
TWO_ENGINES = 3
QUARTER_BANKS = {("si", 1): (5, 0)}
ONE_BANK = {("co", 3): 4, ("si", 1): 4, ("si", 3): 1}
TURNED_BANKS = {"co": (5, 6, 7), "si": (6, 2, 3), "power": (4, 5, 0)}
Y_BANKS = ((7, 7), (1, 6), (2, 3), (7, 4), (1, 5))


def tile_list_meltab_norm_kernel(
    tc, tab_words, tab_scales, co, si, gn, fb_words, fb_scales, mu, isd, offs, out
):
    nc = tc.nc
    with ExitStack() as ctx:
        keep = ctx.enter_context(tc.tile_pool(name="keep", bufs=1))
        psum = ctx.enter_context(tc.psum_pool(name="psum", bufs=1))
        shared = ctx.enter_context(tc.tile_pool(name="shared", bufs=1))

        def sb(name, shape, dtype, tag=None):
            return keep.tile(shape, dtype, name=name, tag=tag or name, align_bytes=256)

        def bank(b, name):
            return psum.tile([P, HALF], F32, name=name, tag="bank%d" % b)

        offsets = keep.tile([P, J // 16], U16, name="offsets")
        tab = sb("tab", [P, T], I32)
        tab_src = tab_words[0].rearrange("p t b -> p (t b)").bitcast(I32)
        nc.sync.dma_start(tab[:, :HEAD], tab_src[:, :HEAD])
        nc.sync.dma_start(offsets[:], offs)
        gain = sb("gain", [P, PACK], F32)
        nc.sync.dma_start(gain[:], gn.rearrange("(p t) -> p t", t=PACK))
        tab_rows = sb("tab_rows", [P, T // 4], I32)
        nc.vector.memset(tab_rows[:, : T // 8], 0)
        nc.gpsimd.memset(tab_rows[:, T // 8 :], 0)
        nc.sync.dma_start(tab_rows[0:P:4, :], tab_scales.bitcast(I32).rearrange("a q w -> q a w"))
        nc.sync.dma_start(tab[:, HEAD:], tab_src[:, HEAD:])

        raw = {}

        def load_weight(name, a):
            w = co if name == "co" else si
            for h in range(2):
                raw[name, a, h] = sb("raw_%s%d%d" % (name, a, h), [P, PACK, F // 2], F32)
                rows = w[K_PASS * a : K_PASS * (a + 1), F // 2 * h : F // 2 * (h + 1)]
                nc.sync.dma_start(raw[name, a, h][:], rows.rearrange("(p i) f -> p i f", i=PACK))

        planes = sb("planes", [P, PASSES * J // 4], I32)
        nc.vector.memset(planes[:], 0)
        picked_rows = sb("picked_rows", [P, J // 4], I32)
        nc.vector.tensor_copy(picked_rows[:].bitcast(U8), tab_rows[:].bitcast(U8).indirect(offsets[:]))
        load_weight("co", 0)
        for p0 in range(0, P, 32):
            queue = nc.sync if p0 < P // 2 else nc.scalar
            queue.dma_start(planes[p0 : p0 + 4, :], picked_rows[p0 : p0 + 32 : 4, :])
        load_weight("co", 1)
        for a in range(PASSES):
            load_weight("si", a)

        fb_codes = sb("fb_codes", [P, 2 * N // 4], I32)
        nc.sync.dma_start(fb_codes[:], fb_words[0].bitcast(I32))
        fb_plane = sb("fb_plane", [P, N // 4], I32)
        nc.vector.memset(fb_plane[:], 0)
        fb_rows = fb_scales[0].bitcast(I32).rearrange("(q r) w -> r q w", r=4)
        for r in range(4):
            nc.sync.dma_start(fb_plane[r:P:32, :], fb_rows[r])
        mean = sb("mean", [P, 2], F32)
        rdev = sb("rdev", [P, 2], F32)
        with nc.allow_non_contiguous_dma(reason="one value a partition"):
            nc.sync.dma_start(mean[:], mu.rearrange("(u p) -> p u", p=P))
            nc.sync.dma_start(rdev[:], isd.rearrange("(u p) -> p u", p=P))

        grouped, codes, scales = {}, {}, {}
        for name in ("co", "si"):
            for a in range(PASSES):
                if (name, a) != ("si", 1):
                    at = 4096 * (a if name == "co" else 2)
                    whole = shared.tile(
                        [P, PACK, P, PACK], BF16, name="grouped_%s%d" % (name, a), align_bytes=256, offset=at
                    )
                    grouped[name, a] = whole
                    for h in range(2):
                        grouped[name, a, h] = whole[:, :, GROUPS * h : GROUPS * (h + 1), :]
                else:
                    for h in range(2):
                        grouped[name, a, h] = sb("grouped_si%d%d" % (a, h), [P, PACK, GROUPS, PACK], BF16)[:]
                codes[name, a] = sb("codes_%s%d" % (name, a), [P, F], U32)
                scales[name, a] = sb("scales_%s%d" % (name, a), [P, F], U8)

        def cast(copy, name, a, h, classes):
            src = raw[name, a, h][:].rearrange("p i (m t) -> p m i t", t=PACK)
            dst = grouped[name, a, h].rearrange("p t m i -> p m i t")
            copy(dst[:, :, :, classes], src[:, :, :, classes])

        def cast_on_vector(name, a, h):
            for g in range(2):
                cast(nc.vector.tensor_copy, name, a, h, slice(2 * g, 2 * g + 2))

        def quantise_half(name, a, h, t):
            cols = slice(P * t + GROUPS * h, P * t + GROUPS * (h + 1))
            nc.vector.quantize_mx(
                out=codes[name, a][:, cols].bitcast(FP8X4),
                scales=scales[name, a][:, cols],
                in_=grouped[name, a, h][:, t].rearrange("p m i -> p (m i)"),
            )

        def quantise(name, a, t0, t1):
            cols = slice(P * t0, P * t1)
            nc.vector.quantize_mx(
                out=codes[name, a][:, cols].bitcast(FP8X4),
                scales=scales[name, a][:, cols],
                in_=grouped[name, a][:, t0:t1].rearrange("p t m i -> p (t m i)"),
            )

        picked, parted = {}, {}

        def gather(h):
            j0, j1 = PIECES[h]
            if h < 2:
                picked[h] = sb("picked%d" % h, [P, j1 - j0], U32)
            else:
                picked[h] = shared.tile([P, j1 - j0], U32, name="picked2", align_bytes=256, offset=0)
            nc.vector.tensor_copy(picked[h][:], tab[:].bitcast(U32).indirect(offsets[:, j0 // 16 : j1 // 16]))

        def part(h):
            j0, j1 = PIECES[h]
            if h == 0:
                parted[h] = sb("parted0", [P, PASSES, j1 - j0], U16)
            else:
                offset = 1024 if h == 1 else 4096
                parted[h] = shared.tile([P, PASSES, j1 - j0], U16, name="parted%d" % h, align_bytes=256, offset=offset)
            nc.vector.tensor_copy(parted[h][:], picked[h][:].bitcast(U16).rearrange("p (j a) -> p a j", a=PASSES))

        def transform(dst, name, a, t, j0, j1, first, last):
            h = j0 // HALF
            first_frame = PIECES[h][0]
            cols = slice(P * t, P * (t + 1))
            nc.tensor.matmul_mx(
                dst,
                lhsT=codes[name, a][:, cols].bitcast(FP8X4),
                lhsT_scale=scales[name, a][:, cols],
                rhs=parted[h][:, a, j0 - first_frame : j1 - first_frame].bitcast(FP4X4),
                rhs_scale=planes[:].bitcast(U8)[:, a * J + j0 : a * J + j1],
                start=first,
                stop=last,
            )

        acc = {}

        def half_pass(t, a, first):
            if first:
                acc["half", t] = bank(t, "re_half%d" % t)
            transform(acc["half", t][:], "co", a, t, 0, HALF, first, not first)

        def quarter_sums(name, q, t):
            g, side = min(t, 3 - t), t // 2
            if (name, q, g) not in acc:
                acc[name, q, g] = bank(QUARTER_BANKS[name, q][g], "%s%d%d" % (name, q, g))
            return acc[name, q, g][:, QUARTER * side : QUARTER * (side + 1)]

        def quarter_pass(name, a, q, t, first):
            transform(quarter_sums(name, q, t), name, a, t, QUARTER * q, QUARTER * (q + 1), first, not first)

        def short_sums(name, c, t):
            b = ONE_BANK[name, c] if c else t
            if (name, c, b) not in acc:
                acc[name, c, b] = bank(b, "%s_short%d%d" % (name, c, b))
            return acc[name, c, b][:, P * t : P * (t + 1)]

        def short_pass(c, a, t, first, last, name="si"):
            transform(short_sums(name, c, t), name, a, t, CHUNKS[c][0], CHUNKS[c][1], first, last)

        def short_group(name, c):
            for a in (1, 0):
                for t in reversed(range(PACK)):
                    short_pass(c, a, t, a == 1 and t == PACK - 1, a == 0 and t == 0, name)

        def whole_sums(name, q, classes):
            for t in classes:
                quarter_pass(name, 1, q, t, True)
                quarter_pass(name, 0, q, t, False)

        def turned_pass(name, b, a, first):
            if first:
                acc[name, "turned", b] = bank(TURNED_BANKS[name][b], "%s_turned%d" % (name, b))
            j0 = CHUNKS[DIRECT + b][0]
            nc.tensor.matmul_mx(
                acc[name, "turned", b][:],
                lhsT=parted[j0 // QUARTER - 1][:, a, j0 % QUARTER : j0 % QUARTER + P].bitcast(FP4X4),
                lhsT_scale=planes[:].bitcast(U8)[:, a * J + j0 : a * J + j0 + P],
                rhs=codes[name, a][:].bitcast(FP8X4),
                rhs_scale=scales[name, a][:],
                start=first,
                stop=not first,
            )

        def turned_sums(name, b):
            turned_pass(name, b, 1, True)
            turned_pass(name, b, 0, False)

        identity = sb("identity", [P, P], F32)
        make_identity(nc, identity[:])
        sq_turned = {}
        for name in ("co", "si"):
            for b in range(TURNED):
                sq_turned[name, b] = sb("sq_turned_%s%d" % (name, b), [P, HALF], F32)

        def square_on_vector(name, b):
            twin = sb("twin", [P, HALF], F32, "grouped_si11")
            halves = [slice(QUARTER * g, QUARTER * (g + 1)) for g in range(2)]
            for cols in halves:
                nc.vector.tensor_copy(twin[:, cols], acc[name, "turned", b][:, cols])
            for cols in halves:
                nc.vector.tensor_tensor(sq_turned[name, b][:, cols], acc[name, "turned", b][:, cols], twin[:, cols], ALU.mult)

        def square_turned(name, b):
            nc.scalar.activation(sq_turned[name, b][:], acc[name, "turned", b][:], ACT.Square)

        def turn(name, b):
            if name == "co":
                acc["power", b] = bank(TURNED_BANKS["power"][b], "power_turned%d" % b)
            for t in range(PACK):
                nc.tensor.matmul(
                    acc["power", b][:, P * t : P * (t + 1)],
                    lhsT=sq_turned[name, b][:, P * t : P * (t + 1)],
                    rhs=identity[:],
                    is_transpose=True,
                    start=name == "co" and t == 0,
                    stop=name == "si" and t == PACK - 1,
                )

        sgn = sb("sgn", [P, PACK], BF16)
        mag = sb("mag", [P, PACK], F32)
        root = sb("root", [P, PACK], F32)
        nc.scalar.activation(mag[:], gain[:], ACT.Abs)
        nc.scalar.activation(sgn[:], gain[:], ACT.Sign)
        nc.scalar.activation(root[:], mag[:], ACT.Sqrt)

        re_ranges = ((0, HALF), CHUNKS[3])
        sq_re = [sb("sq_re%d" % j0, [P, PACK, j1 - j0], F32) for j0, j1 in re_ranges]
        sq_im = [sb("sq_im%d" % j0, [P, PACK, j1 - j0], F32) for j0, j1 in CHUNKS[:DIRECT]]

        def square(dst, src, t):
            nc.scalar.activation(dst, src, ACT.Square, scale=root[:, t : t + 1])

        def square_im(c):
            for t in range(PACK):
                square(sq_im[c][:, t, :], quarter_sums("si", 1, t) if c == 2 else short_sums("si", c, t), t)

        for h in range(2):
            gather(h)
        part(0)
        cast(nc.scalar.copy, "co", 0, 0, slice(0, PACK))
        cast(nc.vector.tensor_copy, "co", 0, 1, slice(0, 2))
        cast(nc.scalar.copy, "co", 0, 1, slice(2, PACK))
        for t in range(2):
            quantise("co", 0, t, t + 1)
        quantise("co", 0, 2, PACK)
        part(1)
        gather(2)
        for t in range(3):
            half_pass(t, 0, True)
        cast(nc.scalar.copy, "co", 1, 0, slice(0, PACK))
        cast(nc.vector.tensor_copy, "co", 1, 1, slice(0, 2))
        cast(nc.scalar.copy, "co", 1, 1, slice(2, PACK))
        for t in range(2):
            quantise("co", 1, t, t + 1)
            half_pass(t, 1, False)
        quantise("co", 1, 2, PACK)
        half_pass(2, 1, False)
        half_pass(3, 1, True)
        half_pass(3, 0, False)
        part(2)
        short_group("co", 3)
        for b in range(TURNED):
            turned_sums("co", b)

        for h in range(2):
            cast_on_vector("si", 0, h)
        for g in range(2):
            quantise("si", 0, 2 * g, 2 * g + 2)
        for t in range(PACK):
            square(sq_re[0][:, t, :], acc["half", t][:], t)
        for t in range(PACK):
            square(sq_re[1][:, t, :], short_sums("co", 3, t), t)
        for b in range(TURNED - 1):
            square_turned("co", b)
        for t in range(PACK):
            short_pass(0, 0, t, True, False)
        for t in range(PACK):
            short_pass(1, 0, t, t == 0, False)
        for t in (0, 3):
            transform(quarter_sums("si", 1, t), "si", 0, t, QUARTER, HALF, t == 0, False)
        cast_on_vector("si", 1, 0)
        for t in range(PACK):
            quantise_half("si", 1, 0, t)
        cast_on_vector("si", 1, 1)
        for t in range(PACK):
            quantise_half("si", 1, 1, t)
            short_pass(0, 1, t, False, True)
        square_on_vector("co", TURNED - 1)
        for t in reversed(range(PACK)):
            short_pass(1, 1, t, False, t == 0)
        for t in (3, 0):
            transform(quarter_sums("si", 1, t), "si", 1, t, QUARTER, HALF, False, t == 0)
        whole_sums("si", 1, (2, 1))
        short_group("si", 3)

        widths = [j1 - j0 for j0, j1 in CHUNKS]
        power = [sb("power%d" % c, [P, w, PACK], BF16) for c, w in enumerate(widths[:DIRECT])]
        signed = [sb("signed%d" % c, [P, w, PACK], BF16) for c, w in enumerate(widths)]
        h_codes = [sb("h_codes%d" % c, [P, w], U32) for c, w in enumerate(widths)]
        h_scales = [sb("h_scales%d" % c, [P, w], U8) for c, w in enumerate(widths)]
        result = [sb("result%d" % j0, [P, 2, j1 - j0], F32) for j0, j1 in STORES]
        out_rows = out.rearrange("(u p) j -> p u j", p=P)

        def add(c):
            j0, j1 = CHUNKS[c]
            r = max(0, j0 // QUARTER - 1)
            nc.vector.tensor_tensor(
                power[c][:].rearrange("p (n e) t -> p n t e", e=2),
                sq_re[r][:, :, j0 - re_ranges[r][0] : j1 - re_ranges[r][0]].rearrange("p t (n e) -> p n t e", e=2),
                sq_im[c][:].rearrange("p t (n e) -> p n t e", e=2),
                ALU.add,
            )

        def sign(c):
            signs = sgn[:].unsqueeze(1).to_broadcast([P, widths[c], PACK])
            nc.vector.tensor_tensor(signed[c][:], power[c][:], signs, ALU.mult)

        def weigh(b):
            nc.vector.tensor_tensor(
                signed[DIRECT + b][:],
                acc["power", b][:].rearrange("p (t j) -> p j t", t=PACK),
                gain[:].unsqueeze(1).to_broadcast([P, P, PACK]),
                ALU.mult,
            )

        def y_sums(s, u):
            b = Y_BANKS[s][u]
            if ("y", s, b) not in acc:
                acc["y", s, b] = bank(b, "y%d%d" % (s, u))
            width = STORES[s][1] - STORES[s][0]
            side = u if Y_BANKS[s][0] == Y_BANKS[s][1] else 0
            return acc["y", s, b][:, width * side : width * (side + 1)]

        def quantise_and_filter(c):
            nc.vector.quantize_mx(
                out=h_codes[c][:].bitcast(FP8X4),
                scales=h_scales[c][:],
                in_=signed[c][:].rearrange("p j t -> p (j t)"),
            )
            s = STORE_OF[c]
            j0, j1 = CHUNKS[c]
            for u in range(2):
                nc.tensor.matmul_mx(
                    y_sums(s, u)[:, j0 - STORES[s][0] : j1 - STORES[s][0]],
                    lhsT=fb_codes[:].bitcast(U8)[:, 2 * P * u : 2 * P * (u + 1)].bitcast(FP4X4),
                    lhsT_scale=fb_plane[:].bitcast(U8)[:, P * u : P * (u + 1)],
                    rhs=h_codes[c][:].bitcast(FP8X4),
                    rhs_scale=h_scales[c][:],
                    start=True,
                    stop=True,
                )

        def pair_of_chunks(c):
            for stage in (add, sign, quantise_and_filter):
                stage(c)
                stage(c + 1)

        def finish(s):
            for u in range(2):
                scale, bias = rdev[:, u : u + 1], shift[:, u : u + 1]
                if s >= TWO_ENGINES and u == 1:
                    nc.vector.tensor_scalar(result[s][:, u, :], y_sums(s, u), scale, bias, ALU.mult, ALU.add)
                else:
                    nc.scalar.activation(result[s][:, u, :], y_sums(s, u), ACT.Identity, bias=bias, scale=scale)
                if s in BY_GROUP:
                    nc.sync.dma_start(out_rows[:, u, STORES[s][0] : STORES[s][1]], result[s][:, u, :])
            if s not in BY_GROUP:
                nc.sync.dma_start(out_rows[:, :, STORES[s][0] : STORES[s][1]], result[s][:])

        square_im(0)
        square_im(1)
        for b in range(TURNED):
            turned_sums("si", b)
        square_im(2)
        square_im(3)
        pair_of_chunks(0)
        for b in range(TURNED):
            turn("co", b)
        for b in range(TURNED):
            square_turned("si", b)
            turn("si", b)
        add(2)
        minus_mean = sb("minus_mean", [P, 2], F32, "sq_im256")
        shift = sb("shift", [P, 2], F32)
        nc.scalar.activation(minus_mean[:], mean[:], ACT.Copy, scale=-1.0)
        for u in range(2):
            nc.scalar.activation(shift[:, u : u + 1], minus_mean[:, u : u + 1], ACT.Copy, scale=rdev[:, u : u + 1])
        finish(0)
        add(3)
        for stage in (sign, quantise_and_filter):
            stage(2)
            stage(3)
        weigh(0)
        for b in range(1, TURNED):
            weigh(b)
            quantise_and_filter(DIRECT + b - 1)
        quantise_and_filter(DIRECT + TURNED - 1)
        for s in range(1, len(STORES)):
            finish(s)
